import numpy as np, ml_dtypes
CORES = [36,164,52,180,100,228,116,244]
N = 8
import mx_ref
BF = ml_dtypes.bfloat16
def gcols(t, e):
    v = np.concatenate([t.reshape(8, 16, -1, 4), np.zeros((8, 16, 1, 4), BF)], axis=2)
    return np.ascontiguousarray(np.stack([v[g][:, e[g]] for g in range(8)])).reshape(128, -1)
def tile(rs):
    return np.stack(rs, axis=2).reshape(128, -1).astype(BF)
def cut(t, i, w=512):
    return t[:, w * i:w * i + w]
def pick(q, e):
    c = np.concatenate([q[0].reshape(128, -1, 4), np.zeros((128, 1, 4), np.uint8)], axis=1); s = np.concatenate([q[1], np.ones((16, 1), np.uint8)], axis=1)
    return (np.ascontiguousarray(c[:, e].reshape(128, -1)), np.ascontiguousarray(s[:, e]))
def join(*qs):
    return (np.concatenate([q[0] for q in qs], axis=1), np.concatenate([q[1] for q in qs], axis=1))
def put(q, e, v):
    c, s = q[0].reshape(128, -1, 4).copy(), q[1].copy(); c[:, e] = v[0].reshape(128, -1, 4); s[:, e] = v[1]
    return (c.reshape(128, -1), s)
def pk(c, s):
    return (np.ascontiguousarray(c), mx_ref.live(s))
def emit(q):
    return q[0], q[1]
def packed(v, rng):
    q = [mx_ref.quantize(np.ascontiguousarray(v[r])) for r in range(N)]
    return np.stack([a for a, b in q]), np.stack([mx_ref.plane(b, rng) for a, b in q])
def values_of_codes():
    e, c = np.zeros((128, 128, 4), np.float32), np.zeros((128, 2, 4), np.uint8)
    e[np.arange(128), np.arange(128), 0] = 1
    c[:127, :, 0] = np.arange(256).reshape(2, 128).T[:127]
    return mx_ref.matmul(mx_ref.quantize(e.reshape(128, 512).astype(BF)), (c.reshape(128, 8), np.full((16, 2), 127, np.uint8))).T.reshape(-1).astype(np.float64)
CODE_VALUE, SCALE_VALUE = values_of_codes(), 2.0 ** (np.arange(256) - 127.0)
def decode(q):
    return (CODE_VALUE[q[0]].reshape(16, 8, -1, 4) * SCALE_VALUE[q[1]][:, None, :, None] + 0.0).reshape(128, -1).astype(np.float32)
def f(rng, *shape):
    return mx_ref.flush((rng.standard_normal(shape, dtype=np.float32) * np.exp2(rng.integers(-2, 3, shape[:-1] + (1,)))).astype(BF))
def wide(rng, *shape, cols=0):
    v = rng.standard_normal(shape, dtype=np.float32) * np.exp2(rng.integers(-12, 13, shape)).astype(np.float32)
    if cols: v *= np.repeat(np.exp2(rng.integers(-cols, cols + 1, shape[:-2] + (1, shape[-1] // 4))) * (rng.random(shape[:-2] + (1, shape[-1] // 4)) > 0.0625), 4, axis=-1).astype(np.float32)
    return mx_ref.flush(v.astype(BF))
C, H, R, STEP = 288, 128, 3, 9
def big(v):
    v = v.astype(np.float32)
    v[np.abs(v) < np.float32(2.0 ** -16)] = 0
    return v.astype(BF)
def numbers_of(rng):
    return {"x": big(f(rng, N, 128, 4 * C)), "u": np.array(f(rng, N, 128, 512)), "v": np.array(f(rng, N, 128, 512))}
def plays(rng):
    return rng.integers(1, 7, (N, 8, 1)).astype(np.int32)
def layers(rng):
    return big(f(rng, N, 128, 2048)).reshape(N, 8, 16, 4, 8, 16, 4)
def weights(rng, w):
    c, s = packed(np.ascontiguousarray(w).reshape(N, 128, 2048), rng)
    return {"wc": c, "ws": s}
def turning(rng):
    b = np.abs(128 - (STEP * np.arange(130)) % 256)
    k = np.flatnonzero((b[1:129] - b[:128]) * (b[2:] - b[1:129]) < 0) + 1
    e = min(STEP, C // 32) - 1
    k = np.concatenate([[0], k[:e], [128]])
    s = -np.ones(C)
    for i in range(e + 1):
        lo = 32 * i
        hi = lo + 32 if i < e else C
        m = [lo, hi - 1]
        w = rng.permutation(np.setdiff1d(np.arange(lo, hi), m))
        s[m] = 1
        s[w[:k[i + 1] - k[i] - len(m)]] = 1
    return s
def setup_inputs(rng):
    return {**numbers_of(rng), "p": plays(rng), **weights(rng, layers(rng))}
def setup_inputs_ties(rng):
    d = numbers_of(rng)
    e = rng.permutation(N)
    x = d["x"].reshape(N, 8, 16, C, 4)
    a = (1.0 + (2 * rng.integers(0, 64, (N, 8, 8, C, 4)) + 1) * 2.0 ** -7) * np.exp2(-rng.integers(8, 15, (N, 8, 8, C, 4)).astype(np.float64))
    a *= rng.integers(0, 2, a.shape) * 2.0 - 1.0
    a[:, :, 0, :, 0] = 1.96875
    x[:, :, 8:] = a.astype(np.float32).astype(BF)
    for r in range(N):
        k = rng.permutation(C) % 3
        if r == e[0]: k = np.ones(C, int)
        elif r in e[2::2]: k = rng.permutation(3)[np.arange(C) % 3]
        c = x[r, 0, :8, :3].copy()
        c[:, 0] = 0
        c[:, 2] = -c[:, 1]
        x[r, 0, :8] = c[:, k]
    x[e[1]] = 0
    u = d["u"].reshape(N, 8, 16, 128, 4)
    u[:, 1:, :, 0] = 0
    u[:, 0, 8:, 0] = 0
    w = layers(rng)
    w[:, :, :, :, 0, :8] = 0
    return {"x": x.reshape(N, 128, 4 * C), "u": u.reshape(N, 128, 512), "v": d["v"], "p": plays(rng), **weights(rng, w)}
def setup_inputs_near(rng):
    d = numbers_of(rng)
    x = d["x"].reshape(N, 8, 16, C, 4)
    u = d["u"].reshape(N, 128, 128, 4)
    o = rng.permutation(N) % 2
    x[:, 0, 0] = 0
    x[:, 0, 8:] = 0
    u[:, :, 0] = 0
    for r in range(N):
        k = 2.0 ** -30 if o[r] == 0 else 1.0
        c = rng.permutation(C) % 3
        x[r, 0, 8, :, 0] = (np.array([9, 8, 9])[c] * 0.125 * k).astype(np.float32).astype(BF)
        x[r, 0, 9, :, 0] = (np.array([10, 9, 11])[c] * 0.125 * k).astype(np.float32).astype(BF)
        x[r, 0, 0, rng.integers(C), 0] = 2.0 ** 29 * (rng.integers(0, 2) * 2.0 - 1.0)
        u[r, 0, 0, 0] = k
        u[r, 8, 0, 0] = 1.125 * k
        u[r, 9, 0, 0] = -k
    w = layers(rng)
    for i in [0] + [8 + j for j in range(8)]:
        w[:, 0, i] = 0
        w[:, :, :, :, 0, i] = 0
    return {"x": x.reshape(N, 128, 4 * C), "u": u.reshape(N, 128, 512), "v": d["v"], "p": plays(rng), **weights(rng, w)}
def setup_inputs_late(rng):
    d = numbers_of(rng)
    x = d["x"].reshape(N, 128, C, 4)
    k = rng.permutation(N) % 2
    c = (k * 2.0 - 1.0).astype(np.float32).astype(BF)
    x[:, 0] = c[:, None, None]
    x[:, 1:8] = np.clip(x[:, 1:8].astype(np.float32), -8, 8).astype(BF)
    u = d["u"].reshape(N, 128, 128, 4)
    u[:, :, 0] = 0
    u[:, 0, 0, 0] = 1
    p = plays(rng)
    p[k == 0, 0] = 1
    p[np.flatnonzero(k == 1)[0]] = 6
    return {"x": x.reshape(N, 128, 4 * C), "u": u.reshape(N, 128, 512), "v": d["v"], "p": p, **weights(rng, layers(rng))}
def setup_inputs_ends(rng):
    d = numbers_of(rng)
    x = np.zeros((N, 8, 16, C, 4), np.float32)
    u = d["u"].reshape(N, 128, 128, 4)
    v = d["v"]
    o = rng.permutation(N) % 4
    for t in range(N):
        for r in range(N):
            if o[r] == 3 and o[(r + 1) % N] == 2:
                o[r] = 2
                o[(r + 1) % N] = 3
    h = rng.permutation(N) % 2
    m = np.flatnonzero(o == 1)
    if (h[m] == 0).all():
        h[np.flatnonzero(h == 1)[0]] = 0
        h[m[0]] = 1
    p = np.zeros((N, 8, 1), np.int32)
    w = np.zeros((N, 128, 4, 128, 4), np.float32)
    i = np.arange(128)
    u[:, :, 0] = 0
    for r in range(N):
        p[r] = 6 if h[r] == 0 else 1
        for b in range(4): w[r, i, b, i, b] = 1 if o[r] == 3 else -1
        if o[r] < 3:
            a = rng.integers(8, 17, (8, 1, C, 1)) * 2.0 ** 26
            x[r] = a if o[r] == 0 else -a if o[r] == 1 else a * turning(rng)[None, None, :, None]
            u[r, :, 0] = 2.0 ** 30
        else:
            x[r] = rng.integers(8, 16, (8, 1, C, 1)) * 2.0 ** -33
            x[r, 0, 0, :, 0] = (2 + rng.permutation(C) % 3) * 2.0 ** -31
            x[r, 0, 1, :, 0] = 2.0 ** -30
            u[r, 0, 0, 0] = 2.0 ** -30
            u[r, 1, 0, 0] = -1.5 * 2.0 ** -30
        if o[r] in (0, 2): v[r] = (2.0 ** 30 * (rng.integers(0, 2, (128, 512)) * 2.0 - 1.0)).astype(np.float32).astype(BF)
        if o[r] == 3: v[r] = 2.0 ** -30
    return {"x": x.reshape(N, 128, 4 * C).astype(BF), "u": u.reshape(N, 128, 512), "v": v, "p": p, **weights(rng, w.astype(BF))}
def setup_inputs_spread(rng):
    d = setup_inputs(rng)
    d["x"] = big(wide(rng, N, 128, 4 * C, cols=6))
    return d
def check_inputs(d):
    b = []
    for k in ("x", "u", "v"):
        a = np.abs(d[k].astype(np.float32))
        if not (np.isfinite(a).all() and ((a == 0) | (a >= 2.0 ** -30) & (a <= 2.0 ** 30)).all()): b.append("a value of " + k)
    if not ((d["p"] >= 1) & (d["p"] <= 6)).all(): b.append("an entry of p")
    none, least, most = [emit(mx_ref.quantize(np.full((128, 16), k, np.float32).astype(BF)))[1][0, 0] for k in (0.0, 2.0 ** -30, 2.0 ** 30)]
    for r in range(N):
        if ((d["wc"][r] == 0x7F) | (d["wc"][r] == 0xFF)).any(): b.append("wc: a code that is no number")
        s = mx_ref.live(d["ws"][r])
        if ((s != none) & ((s < least) | (s > most))).any(): b.append("ws: a scale out of range")
    return b
def reference(x, u, v, p, wc, ws):
    qu = [mx_ref.quantize(u[r]) for r in range(N)]
    lay = [pk(wc[r], ws[r]) for r in range(N)]
    now = [x[r] for r in range(N)]
    n, kept = np.zeros(N, np.int64), np.zeros((N, 8), np.int64)
    a = np.zeros((N, 8, C), np.int64)
    for t in range(R):
        q = [mx_ref.quantize(now[r]) for r in range(N)]
        held = [decode(q[r]).astype(BF) for r in range(N)]
        s = np.stack([mx_ref.matmul(qu[r], q[r])[0] > 0 for r in range(N)])
        for j in range(C):
            n = n + s[:, j]
            c = np.abs(128 - (STEP * n) % 256)
            for g in range(8):
                c = np.minimum(np.maximum(kept[:, g], c - p[:, g, 0]), c + p[:, g, 0])
                kept[:, g] = c
            a[:, :, j] = kept
        made = []
        for r in range(N):
            window = np.concatenate([held[r], cut(held[(r + 1) % N], 0, 4 * H)], axis=1)
            far = gcols(window, np.arange(C) + a[r])
            z = mx_ref.quantize(((held[r].astype(np.float32) + far.astype(np.float32)) * np.float32(0.5)).astype(BF))
            made.append(tile([mx_ref.matmul(pick(lay[r], np.arange(128 * b, 128 * b + 128)), z) * np.float32(0.03125) + now[r][:, b::4].astype(np.float32) for b in range(4)]))
        now = made
    y, ao = np.zeros((N, 128, C), np.float32), np.zeros((N, 8, C), np.float32)
    oc, osc = np.zeros((N, 128, 4 * C), np.uint8), np.zeros((N, 16, C), np.uint8)
    for r in range(N):
        q = mx_ref.quantize(now[r])
        y[r] = mx_ref.matmul(mx_ref.quantize(v[r]), q)
        ao[r] = a[r]
        oc[r], osc[r] = emit(q)
    return {"y": y, "ao": ao, "oc": oc, "osc": osc}

@@ -1,0 +1,427 @@
+from concourse.bass import DstId, RemoteDMATransfer
+from concourse.mybir import dt, AluOpType as O, AxisListType, ActivationFunctionType as F
+
+C, H, R, W = 288, 128, 3, 416
+C0 = (0, 128)
+NB = (128, 160)
+TAB = 880
+VC = ((), (1, 3))
+
+F8 = "float8_e4m3fn_x4"
+SCRATCH = {
+    "X0": ("sbuf", [128, 4 * C], "bfloat16"), "X1": ("sbuf", [128, 4 * C], "bfloat16"),
+    "X2": ("sbuf", [128, 4 * C], "bfloat16"), "X3": ("sbuf", [128, 4 * C], "bfloat16"),
+    "ut": ("sbuf", [128, 512], "bfloat16"), "vt": ("sbuf", [128, 512], "bfloat16"),
+    "uq": ("sbuf", [128, 128], F8), "us": ("sbuf", [128, 128], "uint8"),
+    "u2q": ("sbuf", [128, 128], F8), "u2s": ("sbuf", [128, 128], "uint8"),
+    "vq": ("sbuf", [128, 128], F8), "vs": ("sbuf", [128, 128], "uint8"),
+    "wq": ("sbuf", [128, 512], F8), "wsc": ("sbuf", [128, 512], "uint8"),
+    "cst": ("sbuf", [128, 128], "bfloat16"),
+    "e0": ("sbuf", [128, 516], "bfloat16"), "e1": ("sbuf", [128, 516], "bfloat16"), "e2": ("sbuf", [128, 516], "bfloat16"),
+    "eq": ("sbuf", [128, 1536], F8), "es": ("sbuf", [128, 1536], "uint8"),
+    "off0": ("sbuf", [128, 8], "uint16"),
+    "pci": ("sbuf", [128, 4], "int32"), "pcf": ("sbuf", [128, 16], "float32"),
+    "di": ("sbuf", [128, 64], "int32"), "df": ("sbuf", [128, 32], "float32"), "hold": ("sbuf", [128, 320], "bfloat16"),
+    "tf": ("sbuf", [128, 1280], "float32"), "tab": ("sbuf", [128, TAB], "bfloat16"),
+    "m16": ("sbuf", [128, 10], "float32"), "base": ("sbuf", [128, 36], "float32"),
+    "one8": ("sbuf", [128, 8], "float32"), "mk": ("sbuf", [128, 16], "float32"),
+    "pin": ("sbuf", [1, 8], "int32"), "pfl": ("sbuf", [1, 8], "float32"), "pbc": ("sbuf", [128, 8], "float32"),
+    "pm": ("sbuf", [128, 16], "float32"),
+    "carry": ("sbuf", [128, 16], "float32"),
+    "pos": ("sbuf", [128, R * C], "bfloat16"), "cnt": ("sbuf", [128, R * C], "bfloat16"),
+    "hn": ("sbuf", [128, R * C], "bfloat16"), "bt": ("sbuf", [128, R * C], "bfloat16"),
+    "nw": ("sbuf", [128, R * 18], "uint16"),
+    "d1": ("sbuf", [128, R * 2 * C], "bfloat16"), "pl": ("sbuf", [128, R * 2 * C], "bfloat16"),
+    "hh": ("sbuf", [128, R * 2 * C], "bfloat16"),
+    "of": ("sbuf", [128, R * 36], "float32"), "off": ("sbuf", [128, R * 36], "uint16"),
+    "zt": ("sbuf", [128, R * 4 * C], "bfloat16"),
+    "zq": ("sbuf", [128, R * C], F8), "zs": ("sbuf", [128, R * C], "uint8"),
+    "ysb": ("sbuf", [128, C], "float32"), "ao0": ("sbuf", [128, C], "float32"), "ao1": ("sbuf", [128, C], "float32"),
+    "ps": ("psum", [128, 4096], "float32"),
+}
+for _t in range(R + 1):
+    SCRATCH["q%d" % _t] = ("sbuf", [128, W], F8)
+    SCRATCH["s%d" % _t] = ("sbuf", [128, W], "uint8")
+for _t in range(R):
+    for _k in range(2):
+        SCRATCH["f%d%d" % (_t, _k)] = ("sbuf", [128, 2 * NB[_k]], F8)
+        SCRATCH["g%d%d" % (_t, _k)] = ("sbuf", [128, 2 * NB[_k]], "uint8")
+SEMAPHORES = ["V", "S", "T", "G", "dXA", "dXB", "dU", "dP", "dW", "dV", "arr0", "arr1", "arr2", "sent", "outA", "outB"]
+
+
+def rank_program(g, core, T, topo):
+    rank = T.rank_of(core)
+    if rank is None:
+        return
+    n_ranks = len(T.cores)
+    prev = T.cores[(rank - 1) % n_ranks]
+    nxt = T.cores[(rank + 1) % n_ranks]
+    eng = {"V": g.vector, "S": g.scalar, "T": g.tensor, "G": g, "Y": g.sync}
+    count = {"V": 0, "S": 0, "T": 0, "G": 0}
+    known = {}
+
+    def need(q, toks):
+        best = {}
+        for tk in toks:
+            if tk is None:
+                continue
+            best[tk[0]] = max(best.get(tk[0], 0), tk[1])
+        for s in best:
+            if best[s] > known.get((q, s), 0):
+                eng[q].wait_ge(T.sem[s], best[s])
+                known[(q, s)] = best[s]
+
+    def run(q, deps, call):
+        need(q, deps)
+        call().then_inc(T.sem[q], 1)
+        count[q] += 1
+        return (q, count[q])
+
+    def ts(out, in0, s1, op0, s2=None, op1=None):
+        if op1 is None:
+            return lambda: g.vector.tensor_scalar(out, in0, s1, None, op0)
+        return lambda: g.vector.tensor_scalar(out, in0, s1, s2, op0, op1)
+
+    def tt(out, a, b, op):
+        return lambda: g.vector.tensor_tensor(out, a, b, op)
+
+    def cp(out, in_):
+        return lambda: g.vector.tensor_copy(out, in_)
+
+    def scan(out, d0, d1, init, op0, op1):
+        return lambda: g.vector.tensor_tensor_scan(out, d0, d1, init, op0, op1)
+
+    def act(out, in_, f=F.Copy, **kw):
+        return lambda: g.scalar.activation(out, in_, f, **kw)
+
+    def quant(q, s, t):
+        return lambda: g.vector.quantize_mx(q, s, t)
+
+    def mm(bank, n, lq, ls, rq, rs, start=True, stop=True):
+        return lambda: g.tensor.matmul_mx(T.ps[:, 512 * bank:512 * bank + n], lq, ls, rq, rs, start, stop)
+
+    g.sync.dma_start(T.X0[:, 0:512], T.x[:, 0:512]).then_inc(T.sem.dXA, 16)
+    g.scalar.dma_start(T.pin[0:1, :], T.p[:, :]).then_inc(T.sem.dP, 16)
+    g.sync.dma_start(T.ut[:, :], T.u[:, :]).then_inc(T.sem.dU, 16)
+    g.sync.dma_start(T.X0[:, 512:1152], T.x[:, 512:1152]).then_inc(T.sem.dXB, 16)
+    need("Y", [("dXA", 16)])
+    g.sync.dma_start(T.wq[:, :].bitcast(dt.uint8), T.wc[:, :]).then_inc(T.sem.dW, 16)
+    g.sync.dma_start(T.wsc[:, :], T.ws[:, :]).then_inc(T.sem.dW, 16)
+    g.sync.dma_start(T.vt[:, :], T.v[:, :]).then_inc(T.sem.dV, 16)
+
+    c_cst = run("V", [], lambda: g.vector.memset(T.cst[:, :], 2.0 ** -6))
+    c_e0 = run("V", [], lambda: g.vector.memset(T.e0[:, :], 0.0))
+    c_off0 = run("V", [], lambda: g.vector.memset(T.off0[:, :], 0))
+    c_one = run("V", [], lambda: g.vector.memset(T.one8[:, :], 1.0))
+    i_p = run("G", [], lambda: g.iota(T.pci[:, 0:1], [[0, 1]], 0, 1))
+    i_t = run("G", [], lambda: g.iota(T.tf[:, 0:256], [[9, 256]], 0, 0, allow_small_or_imprecise_dtypes=True))
+    i_d = run("G", [], lambda: g.iota(T.di[:, 0:32], [[1, 32]], 128, -1))
+    a_e0 = run("G", [c_cst, c_e0], lambda: g.affine_select(T.e0[:, 3:515:4], T.cst[:, :], [[-1, 128]], O.is_equal, 0.0, 0, 1))
+    i_m = run("G", [], lambda: g.iota(T.m16[:, :], [[16, 10]], 0, 0, allow_small_or_imprecise_dtypes=True))
+    a_m0 = run("G", [c_one], lambda: g.affine_select(T.mk[:, 0:8], T.one8[:, :], [[-32, 4], [-32, 2]], O.is_ge, 0.0, 0, 1))
+    a_m1 = run("G", [c_one], lambda: g.affine_select(T.mk[:, 8:16], T.one8[:, :], [[-32, 4], [0, 2]], O.is_ge, 0.0, 0, 1))
+
+    col = lambda k: T.pcf[:, k:k + 1]
+    h = run("V", [i_p], ts(T.pci[:, 1:2], T.pci[:, 0:1], 16, O.bitwise_and))
+    q15 = run("V", [i_p], ts(T.pci[:, 2:3], T.pci[:, 0:1], 15, O.bitwise_and))
+    d_and = run("V", [i_d], ts(T.di[:, 32:64], T.di[:, 0:32], 15, O.bitwise_and))
+    k_e = run("V", [h], ts(col(0), T.pci[:, 1:2], 0.0, O.is_equal))
+    k_o = run("V", [h], ts(col(1), T.pci[:, 1:2], 0.0, O.is_gt))
+    k_q = run("V", [q15], ts(col(2), T.pci[:, 2:3], -9.0, O.mult, 150.0, O.add))
+    carry = [run("V", [q15], ts(T.carry[:, 0:1], T.pci[:, 2:3], -10.0, O.mult, 150.0, O.add)), 0]
+    d_f = run("V", [d_and], ts(T.df[:, :], T.di[:, 32:64], 0.0, O.is_gt, -522.0, O.mult))
+    m_e = [a_e0,
+           run("V", [a_e0, k_e], ts(T.e1[:, :], T.e0[:, :], col(0), O.mult)),
+           run("V", [a_e0, k_o], ts(T.e2[:, :], T.e0[:, :], col(1), O.mult))]
+    E = {}
+
+    def equant(y, b):
+        k = 128 * (4 * y + b)
+        src = (T.e0, T.e1, T.e2)[y]
+        E[y, b] = run("V", [m_e[y]], quant(T.eq[:, k:k + 128], T.es[:, k:k + 128], src[:, 3 - b:515 - b]))
+
+    for b in range(4):
+        equant(0, b)
+    for i, c in enumerate((1280.0, 768.0, 512.0, 256.0)):
+        i_t = run("S", [i_t], act(T.tf[:, 256 * i + 256:256 * i + 512], T.tf[:, 256 * i:256 * i + 256], F.Abs, bias=-c))
+        if i == 0:
+            d_h = run("S", [d_f], act(T.hold[:, 0:32], T.df[:, :], F.Identity, bias=512.0))
+        else:
+            lo = 16 << i
+            d_h = run("S", [d_h], act(T.hold[:, lo:2 * lo], T.hold[:, 0:lo]))
+    m_t = [run("S", [i_t], act(T.tab[:, 0:256], T.tf[:, 1024:1280], F.Abs, bias=-128.0))]
+    d_h = run("S", [d_h], act(T.hold[:, 256:320], T.hold[:, 0:64]))
+
+    def eside(y, b):
+        k = 128 * (4 * y + b)
+        return T.eq[:, k:k + 128], T.es[:, k:k + 128]
+
+    u2 = []
+
+    QT = [T.q0, T.q1, T.q2, T.q3]
+    ST = [T.s0, T.s1, T.s2, T.s3]
+    XT = [T.X0, T.X1, T.X2, T.X3]
+    bank = {}
+    qx, S, st = {}, {}, {}
+
+    def sl(k):
+        return slice(C0[k], C0[k] + NB[k])
+
+    def quantx(t, k, deps):
+        a, n = C0[k], NB[k]
+        qx[t, k] = run("V", deps, quant(QT[t][:, a:a + n], ST[t][:, a:a + n], XT[t][:, 4 * a:4 * a + 4 * n]))
+
+    def send(t):
+        need("G", [qx[t, 0]])
+        rid, pid = topo.addr(prev, core)
+        m = sum(1 << e for e in topo.engines(core, prev)[::2])
+        g.remote_dma(QT[t][:, C:W].bitcast(dt.uint8), QT[t][:, 0:H].bitcast(dt.uint8), T.sem["arr%d" % t], T.sem.sent, pid, rid, m)
+        g.remote_dma(ST[t][:, C:W], ST[t][:, 0:H], T.sem["arr%d" % t], T.sem.sent, pid, rid, m)
+
+    def sprod(t, k):
+        bk = 4 * k + 3
+        S[t, k] = run("T", [qx[t, k], bank.get(bk)] + u2,
+                      mm(bk, NB[k], T.u2q[:, :], T.u2s[:, :], QT[t][:, sl(k)], ST[t][:, sl(k)]))
+
+    def fill(todo):
+        if todo:
+            todo.pop(0)()
+
+    def chain1(t, k, todo=None):
+        n, a = NB[k], C * t + C0[k]
+        bk = 4 * k + 3
+        x = run("V", [S[t, k]], ts(T.pos[:, a:a + n], T.ps[:, 512 * bk:512 * bk + n], 0.0, O.is_gt))
+        bank[bk] = x
+        fill(todo)
+        x = run("V", [x], scan(T.cnt[:, a:a + n], T.pos[:, a:a + n], T.pos[:, a:a + n], 0.0, O.add, O.max))
+        fill(todo)
+        y = run("V", [x, d_h], scan(T.hn[:, a:a + n], T.hold[:, 0:n], T.cnt[:, a:a + n], 0.0, O.add, O.min))
+        fill(todo)
+        w = 18 * t + 8 * k
+        cc = carry[1]
+        st[t, k, "nw"] = run("V", [y, carry[0]], ts(T.nw[:, w:w + n // 16], T.hn[:, a + 15:a + n:16], T.carry[:, cc:cc + 1], O.add))
+        st[t, k, "last"] = (x, T.cnt[:, a + n - 1:a + n])
+
+    def gath(t, k):
+        n, a, w = NB[k], C * t + C0[k], 18 * t + 8 * k
+        width = (256, 512)[k] if t == 0 else TAB
+        st[t, k, "b"] = run("S", [st[t, k, "nw"]] + m_t[:1 if width == 256 else 2 if width == 512 else 4],
+                            act(T.bt[:, a:a + n], T.tab[:, 0:width].indirect(T.nw[:, w:w + n // 16])))
+
+    def count_on(t, k):
+        x, e = st[t, k, "last"]
+        cc = carry[1]
+        carry[0] = run("S", [x, carry[0]], act(T.carry[:, cc + 1:cc + 2], e, F.Identity, bias=T.carry[:, cc:cc + 1]))
+        carry[1] = cc + 1
+
+    last = {}
+
+    def chain2a(t, k, todo=None):
+        n, a, d = NB[k], C * t + C0[k], 2 * (C * t + C0[k])
+        x = [run("V", [st[t, k, "b"], sc[l]], ts(T.d1[:, d + l * n:d + l * n + n], T.bt[:, a:a + n], col(3 + l), O.add, col(3 + l), O.add)) for l in range(2)]
+        pp = []
+        fill(todo)
+        for l in range(2):
+            init, tok = last.get(l, (col(3 + l), None))
+            e = d + l * n
+            pt = run("V", [x[l], st[t, k, "b"], tok], scan(T.pl[:, e:e + n], T.bt[:, a:a + n], T.d1[:, e:e + n], init, O.max, O.min))
+            last[l] = (T.pl[:, e + n - 1:e + n], pt)
+            pp.append(pt)
+        st[t, k, "pl"] = pp
+
+    def chain2b(t, k, todo=None):
+        n, d, o = NB[k], 2 * (C * t + C0[k]), 36 * t + 16 * k
+        m = 2 * n // 16
+        fill(todo)
+        x = run("V", st[t, k, "pl"] + [d_h], scan(T.hh[:, d:d + 2 * n], T.hold[:, 0:2 * n], T.pl[:, d:d + 2 * n], 0.0, O.add, O.min))
+        fill(todo)
+        x = run("V", [x] + bs[k], tt(T.of[:, o:o + m], T.hh[:, d + 15:d + 2 * n:16], T.base[:, 16 * k:16 * k + m], O.add))
+        fill(todo)
+        st[t, k, "off"] = run("V", [x], cp(T.off[:, o:o + m], T.of[:, o:o + m]))
+
+    def picks(t, k):
+        n, o = NB[k], 36 * t + 16 * k
+        lo, hi = (0, C) if k == 0 else (H, W)
+        fq, fs = T["f%d%d" % (t, k)], T["g%d%d" % (t, k)]
+        deps = [st[t, k, "off"], qx[t, 0], qx[t, 1]] + ([("arr%d" % t, 2 * len(topo.engines(nxt, core)[::2]))] if k else [])
+        for l in range(2):
+            off = T.off[:, o + l * n // 16:o + (l + 1) * n // 16]
+            c, d = l * n, (l + 1) * n
+            st[t, k, "pk", l] = [
+                run("V", deps, cp(fq[:, c:d].bitcast(dt.uint32), QT[t][:, lo:hi].bitcast(dt.uint32).indirect(off))),
+                run("S", deps, act(fs[:, c:d], ST[t][:, lo:hi].indirect(off)))]
+
+    def own(t, k, bs_=range(4)):
+        for b in bs_:
+            bk = 4 * k + b
+            lq, ls = eside(0, b)
+            run("T", [E[0, b], qx[t, k], bank.get(bk)], mm(bk, NB[k], lq, ls, QT[t][:, sl(k)], ST[t][:, sl(k)], True, False))
+
+    def far(t, k, l):
+        n = NB[k]
+        fq, fs = T["f%d%d" % (t, k)], T["g%d%d" % (t, k)]
+        for b in range(4):
+            lq, ls = eside(1 + l, b)
+            st[t, k, "z", b] = run("T", [E[1 + l, b]] + st[t, k, "pk", l],
+                                   mm(4 * k + b, n, lq, ls, fq[:, l * n:l * n + n], fs[:, l * n:l * n + n], False, l == 1))
+
+    def on_v(k):
+        return VC[k]
+
+    def on_s(k):
+        return [b for b in range(4) if b not in VC[k]]
+
+    def cast(t, k, b):
+        n, z = NB[k], 4 * (C * t + C0[k])
+        out, in_ = T.zt[:, z + b:z + 4 * n:4], T.ps[:, 512 * (4 * k + b):512 * (4 * k + b) + n]
+        v = b in on_v(k)
+        st[t, k, "c", b] = bank[4 * k + b] = run("V" if v else "S", [st[t, k, "z", b]], cp(out, in_) if v else act(out, in_))
+
+    def qz(t, k):
+        n, a = NB[k], C * t + C0[k]
+        st[t, k, "qz"] = run("V", [st[t, k, "c", b] for b in range(4)], quant(T.zq[:, a:a + n], T.zs[:, a:a + n], T.zt[:, 4 * a:4 * a + 4 * n]))
+
+    def wprod(t, k):
+        n, a = NB[k], C * t + C0[k]
+        for b in range(4):
+            st[t, k, "r", b] = run("T", [("dW", 32), st[t, k, "qz"], bank.get(4 * k + b)],
+                                   mm(4 * k + b, n, T.wq[:, 128 * b:128 * b + 128], T.wsc[:, 128 * b:128 * b + 128], T.zq[:, a:a + n], T.zs[:, a:a + n]))
+
+    def xupd(t, k, bs_):
+        n, a, e = NB[k], 4 * C0[k], 4 * (C0[k] + NB[k])
+        for b in bs_:
+            st[t, k, "x", b] = bank[4 * k + b] = run(
+                "V", [st[t, k, "r", b], ("dXA", 16) if t == 0 and k == 0 else ("dXB", 16) if t == 0 else st[t - 1, k, "x", b]],
+                tt(XT[t + 1][:, a + b:e:4], T.ps[:, 512 * (4 * k + b):512 * (4 * k + b) + n], XT[t][:, a + b:e:4], O.add))
+
+    def newx(t, k):
+        quantx(t + 1, k, [st[t, k, "x", b] for b in range(4)])
+
+    def yprod(k):
+        n = NB[k]
+        bk = 4 * k
+        return run("T", [vq, qx[R, k], bank.get(bk)], mm(bk, n, T.vq[:, :], T.vs[:, :], T.q3[:, sl(k)], T.s3[:, sl(k)]))
+
+    pf = run("V", [("dP", 16)], cp(T.pfl[0:1, :], T.pin[0:1, :]))
+    pb = run("G", [pf], lambda: g.partition_broadcast(T.pbc[:, :], T.pfl[0:1, :], 128))
+    quantx(0, 0, [("dXA", 16)])
+    send(0)
+    uq = run("V", [("dU", 16)], quant(T.uq[:, :], T.us[:, :], T.ut[:, :]))
+    u2 += [run("V", [uq, c_off0], cp(T.u2q[:, 0:128].bitcast(dt.uint32), T.uq[:, 0:128].bitcast(dt.uint32).indirect(T.off0[:, 0:8]))),
+           run("S", [uq, c_off0], act(T.u2s[:, 0:128], T.us[:, 0:128].indirect(T.off0[:, 0:8])))]
+    sprod(0, 0)
+    equant(1, 0)
+    equant(1, 1)
+    chain1(0, 0, [lambda: equant(1, 2), lambda: equant(1, 3)])
+    gath(0, 0)
+    count_on(0, 0)
+    for lo, hi in ((256, 512), (512, 768), (768, TAB)):
+        m_t.append(run("S", m_t[:1], act(T.tab[:, lo:hi], T.tab[:, 0:hi - lo])))
+    pm = [run("V", [pb, (a_m0, a_m1)[l]], tt(T.pm[:, 8 * l:8 * l + 8], T.pbc[:, :], T.mk[:, 8 * l:8 * l + 8], O.mult)) for l in range(2)]
+    sc = [run("V", [pm[l]], lambda l=l: g.vector.tensor_reduce(col(3 + l), T.pm[:, 8 * l:8 * l + 8], AxisListType.X, O.add)) for l in range(2)]
+    quantx(0, 1, [("dXB", 16)])
+    cc2, bs = [], [[], []]
+
+    def c_cc():
+        for l in range(2):
+            cc2.append(run("V", [sc[l], k_q], tt(col(7 + l), col(2), col(3 + l), O.subtract)))
+
+    def c_base(k):
+        m = NB[k] // 16
+        for l in range(2):
+            o = 16 * k + m * l
+            bs[k].append(run("V", [cc2[l], i_m], ts(T.base[:, o:o + m], T.m16[:, 0:m], col(7 + l), O.add)))
+
+    chain2a(0, 0, [c_cc])
+    chain2b(0, 0, [lambda: c_base(0), lambda: equant(2, 0), lambda: equant(2, 1)])
+    own(0, 0)
+    vq = None
+
+    for t in range(R):
+        sprod(t, 1)
+        picks(t, 0)
+        far(t, 0, 0)
+        if t == 0:
+            equant(2, 2)
+            equant(2, 3)
+        far(t, 0, 1)
+        for b in on_s(0):
+            cast(t, 0, b)
+        chain1(t, 1, [lambda: None] + [lambda b=b: cast(t, 0, b) for b in on_v(0)])
+        gath(t, 1)
+        count_on(t, 1)
+        own(t, 1, (0, 1))
+        qz(t, 0)
+        wprod(t, 0)
+        own(t, 1, (2, 3))
+        if t == 0:
+            c_base(1)
+        xs = [lambda b=b: xupd(t, 0, (b,)) for b in range(4)]
+        chain2a(t, 1, xs)
+        chain2b(t, 1, xs)
+        for f in xs:
+            f()
+        newx(t, 0)
+        if t < R - 1:
+            send(t + 1)
+            picks(t, 1)
+            sprod(t + 1, 0)
+            far(t, 1, 0)
+            far(t, 1, 1)
+            chain1(t + 1, 0)
+            gath(t + 1, 0)
+            for b in on_s(1) + list(on_v(1)[:-1]):
+                cast(t, 1, b)
+            count_on(t + 1, 0)
+
+            def zb():
+                for b in on_v(1)[-1:]:
+                    cast(t, 1, b)
+                qz(t, 1)
+            chain2a(t + 1, 0, [zb])
+            wprod(t, 1)
+            xs = [lambda b=b: xupd(t, 1, (b,)) for b in range(4)]
+            chain2b(t + 1, 0, [lambda: None] + xs)
+            for b in range(2, 4):
+                xs[b]()
+            newx(t, 1)
+            own(t + 1, 0)
+        else:
+            picks(t, 1)
+            far(t, 1, 0)
+            far(t, 1, 1)
+            vq = run("V", [("dV", 16)], quant(T.vq[:, :], T.vs[:, :], T.vt[:, :]))
+            ns = [run("V", [sc[l]], ts(col(5 + l), col(3 + l), -1.0, O.mult)) for l in range(2)]
+            y0 = yprod(0)
+            for b in range(4):
+                cast(t, 1, b)
+            ax = []
+            for kk in range(2):
+                n, d = NB[kk], 2 * (C * t + C0[kk])
+                for l in range(2):
+                    ax.append(run("S", st[t, kk, "pl"] + [ns[l]], act((T.ao0, T.ao1)[l][:, sl(kk)], T.pl[:, d + l * n:d + l * n + n], F.Identity, bias=col(5 + l))))
+            ys = run("S", [y0], act(T.ysb[:, 0:128], T.ps[:, 0:128]))
+            need("Y", [qx[R, 0]])
+            g.sync.dma_start(T.oc[:, 0:512], T.q3[:, 0:128].bitcast(dt.uint8)).then_inc(T.sem.outA, 16)
+            need("Y", ax)
+            for l in range(2):
+                g.sync.dma_start(T.ao[l:8:2, :], (T.ao0, T.ao1)[l][0:128:32, :]).then_inc(T.sem.outA, 16)
+            need("Y", [ys])
+            g.sync.dma_start(T.y[:, 0:128], T.ysb[:, 0:128]).then_inc(T.sem.outA, 16)
+            qz(t, 1)
+            wprod(t, 1)
+            xupd(t, 1, range(4))
+            newx(t, 1)
+    y1 = run("S", [yprod(1)], act(T.ysb[:, 128:288], T.ps[:, 2048:2208]))
+    need("Y", [qx[R, 1]])
+    for k in range(3):
+        g.sync.dma_start(T.osc[4 * k:4 * k + 4, :], T.s3[32 * k:32 * k + 4, 0:C]).then_inc(T.sem.outA, 16)
+    g.scalar.dma_start(T.oc[:, 512:1152], T.q3[:, 128:288].bitcast(dt.uint8)).then_inc(T.sem.outB, 16)
+    g.scalar.dma_start(T.osc[12:16, :], T.s3[96:100, 0:C]).then_inc(T.sem.outB, 16)
+    need("Y", [y1])
+    g.sync.dma_start(T.y[:, 128:288], T.ysb[:, 128:288]).then_inc(T.sem.outA, 16)
+    for q in ("V", "S", "T", "G"):
+        need("Y", [(q, count[q])])
+    g.sync.wait_ge(T.sem.outA, 16 * 8)
+    g.scalar.wait_ge(T.sem.outB, 16 * 2)
+    g.wait_ge(T.sem.sent, 2 * R * len(topo.engines(core, prev)[::2]))

@@ -1,51 +1,47 @@
-from concourse.bass import DstId, RemoteDMATransfer
 from concourse.mybir import dt, AluOpType as O, AxisListType, ActivationFunctionType as F
 
 C, H, R, W = 288, 128, 3, 416
-C0 = (0, 128)
-NB = (128, 160)
-TAB = 880
-VC = ((), (1, 3))
+N = 144
+TAB, TAB0 = 880, 308
+BIG = 2.0 ** 90
 
 F8 = "float8_e4m3fn_x4"
 SCRATCH = {
-    "X0": ("sbuf", [128, 4 * C], "bfloat16"), "X1": ("sbuf", [128, 4 * C], "bfloat16"),
-    "X2": ("sbuf", [128, 4 * C], "bfloat16"), "X3": ("sbuf", [128, 4 * C], "bfloat16"),
     "ut": ("sbuf", [128, 512], "bfloat16"), "vt": ("sbuf", [128, 512], "bfloat16"),
     "uq": ("sbuf", [128, 128], F8), "us": ("sbuf", [128, 128], "uint8"),
     "u2q": ("sbuf", [128, 128], F8), "u2s": ("sbuf", [128, 128], "uint8"),
     "vq": ("sbuf", [128, 128], F8), "vs": ("sbuf", [128, 128], "uint8"),
     "wq": ("sbuf", [128, 512], F8), "wsc": ("sbuf", [128, 512], "uint8"),
-    "cst": ("sbuf", [128, 128], "bfloat16"),
-    "e0": ("sbuf", [128, 516], "bfloat16"), "e1": ("sbuf", [128, 516], "bfloat16"), "e2": ("sbuf", [128, 516], "bfloat16"),
-    "eq": ("sbuf", [128, 1536], F8), "es": ("sbuf", [128, 1536], "uint8"),
+    "one": ("sbuf", [128, 128], "bfloat16"), "e0": ("sbuf", [128, 516], "bfloat16"),
+    "eq": ("sbuf", [128, 512], F8), "es": ("sbuf", [128, 512], "uint8"),
     "off0": ("sbuf", [128, 8], "uint16"),
-    "pci": ("sbuf", [128, 4], "int32"), "pcf": ("sbuf", [128, 16], "float32"),
-    "di": ("sbuf", [128, 64], "int32"), "df": ("sbuf", [128, 32], "float32"), "hold": ("sbuf", [128, 320], "bfloat16"),
-    "tf": ("sbuf", [128, 1280], "float32"), "tab": ("sbuf", [128, TAB], "bfloat16"),
-    "m16": ("sbuf", [128, 10], "float32"), "base": ("sbuf", [128, 36], "float32"),
-    "one8": ("sbuf", [128, 8], "float32"), "mk": ("sbuf", [128, 16], "float32"),
-    "pin": ("sbuf", [1, 8], "int32"), "pfl": ("sbuf", [1, 8], "float32"), "pbc": ("sbuf", [128, 8], "float32"),
-    "pm": ("sbuf", [128, 16], "float32"),
-    "carry": ("sbuf", [128, 16], "float32"),
-    "pos": ("sbuf", [128, R * C], "bfloat16"), "cnt": ("sbuf", [128, R * C], "bfloat16"),
-    "hn": ("sbuf", [128, R * C], "bfloat16"), "bt": ("sbuf", [128, R * C], "bfloat16"),
-    "nw": ("sbuf", [128, R * 18], "uint16"),
-    "d1": ("sbuf", [128, R * 2 * C], "bfloat16"), "pl": ("sbuf", [128, R * 2 * C], "bfloat16"),
-    "hh": ("sbuf", [128, R * 2 * C], "bfloat16"),
-    "of": ("sbuf", [128, R * 36], "float32"), "off": ("sbuf", [128, R * 36], "uint16"),
+    "pci": ("sbuf", [128, 4], "int32"), "pcf": ("sbuf", [128, 8], "float32"),
+    "y9": ("sbuf", [128, TAB0], "bfloat16"), "d9": ("sbuf", [128, TAB0], "bfloat16"), "b9": ("sbuf", [128, TAB0], "bfloat16"),
+    "lo": ("sbuf", [128, TAB0], "bfloat16"), "hi": ("sbuf", [128, TAB0], "bfloat16"),
+    "tab": ("sbuf", [128, TAB], "bfloat16"),
+    "c16": ("sbuf", [128, N], "bfloat16"), "c4": ("sbuf", [128, N], "bfloat16"),
+    "tha": ("sbuf", [128, N], "bfloat16"), "thb": ("sbuf", [128, N], "bfloat16"),
+    "hold": ("sbuf", [128, 2 * N], "bfloat16"),
+    "mk": ("sbuf", [128, 8], "bfloat16"), "pm": ("sbuf", [128, 8], "float32"),
+    "pin": ("sbuf", [1, 8], "int32"), "pbc": ("sbuf", [128, 8], "int32"),
+    "carry": ("sbuf", [128, 8], "float32"),
+    "pa": ("sbuf", [128, R * C], "bfloat16"), "pb": ("sbuf", [128, 16 + R * C], "bfloat16"),
+    "cnt": ("sbuf", [128, R * C], "bfloat16"),
+    "nw": ("sbuf", [128, R * 20], "uint16"),
+    "av": ("sbuf", [128, 2 * C], "bfloat16"), "hh": ("sbuf", [128, R * 2 * C], "bfloat16"),
+    "off": ("sbuf", [128, R * 72], "uint16"),
     "zt": ("sbuf", [128, R * 4 * C], "bfloat16"),
+    "own": ("sbuf", [128, R * 4 * C], "bfloat16"),
     "zq": ("sbuf", [128, R * C], F8), "zs": ("sbuf", [128, R * C], "uint8"),
-    "ysb": ("sbuf", [128, C], "float32"), "ao0": ("sbuf", [128, C], "float32"), "ao1": ("sbuf", [128, C], "float32"),
+    "ysb": ("sbuf", [128, C], "float32"), "aof": ("sbuf", [128, C], "float32"),
     "ps": ("psum", [128, 4096], "float32"),
 }
 for _t in range(R + 1):
+    SCRATCH["X%d" % _t] = ("sbuf", [128, 4 * C], "bfloat16")
     SCRATCH["q%d" % _t] = ("sbuf", [128, W], F8)
     SCRATCH["s%d" % _t] = ("sbuf", [128, W], "uint8")
 for _t in range(R):
-    for _k in range(2):
-        SCRATCH["f%d%d" % (_t, _k)] = ("sbuf", [128, 2 * NB[_k]], F8)
-        SCRATCH["g%d%d" % (_t, _k)] = ("sbuf", [128, 2 * NB[_k]], "uint8")
+    SCRATCH["w%d" % _t] = ("sbuf", [128, 4 * W], "bfloat16")
 SEMAPHORES = ["V", "S", "T", "G", "dXA", "dXB", "dU", "dP", "dW", "dV", "arr0", "arr1", "arr2", "sent", "outA", "outB"]
 
 
@@ -97,331 +93,265 @@ def rank_program(g, core, T, topo):
     def quant(q, s, t):
         return lambda: g.vector.quantize_mx(q, s, t)
 
-    def mm(bank, n, lq, ls, rq, rs, start=True, stop=True):
-        return lambda: g.tensor.matmul_mx(T.ps[:, 512 * bank:512 * bank + n], lq, ls, rq, rs, start, stop)
+    def fill(ap, c):
+        return lambda: g.vector.memset(ap, c)
 
-    g.sync.dma_start(T.X0[:, 0:512], T.x[:, 0:512]).then_inc(T.sem.dXA, 16)
-    g.scalar.dma_start(T.pin[0:1, :], T.p[:, :]).then_inc(T.sem.dP, 16)
+    def iota(out, pattern, base):
+        return lambda: g.iota(out, pattern, base, 0, allow_small_or_imprecise_dtypes=True)
+
+    def ps(bank, n):
+        return T.ps[:, 512 * bank:512 * bank + n]
+
+    bank = {}
+
+    def mm(bk, n, deps, lq, ls, rq, rs):
+        return run("T", deps + [bank.get(bk)], lambda: g.tensor.matmul_mx(ps(bk, n), lq, ls, rq, rs, True, True))
+
+    QT = [T["q%d" % t] for t in range(R + 1)]
+    ST = [T["s%d" % t] for t in range(R + 1)]
+    XT = [T["X%d" % t] for t in range(R + 1)]
+    WT = [T["w%d" % t] for t in range(R)]
+
     g.sync.dma_start(T.ut[:, :], T.u[:, :]).then_inc(T.sem.dU, 16)
-    g.sync.dma_start(T.X0[:, 512:1152], T.x[:, 512:1152]).then_inc(T.sem.dXB, 16)
+    g.scalar.dma_start(T.pin[0:1, :], T.p[:, :]).then_inc(T.sem.dP, 16)
+    g.scalar.dma_start(T.X0[:, 0:4 * N], T.x[:, 0:4 * N]).then_inc(T.sem.dXA, 16)
+    g.sync.dma_start(T.X0[:, 4 * N:4 * C], T.x[:, 4 * N:4 * C]).then_inc(T.sem.dXB, 16)
     need("Y", [("dXA", 16)])
     g.sync.dma_start(T.wq[:, :].bitcast(dt.uint8), T.wc[:, :]).then_inc(T.sem.dW, 16)
     g.sync.dma_start(T.wsc[:, :], T.ws[:, :]).then_inc(T.sem.dW, 16)
     g.sync.dma_start(T.vt[:, :], T.v[:, :]).then_inc(T.sem.dV, 16)
 
-    c_cst = run("V", [], lambda: g.vector.memset(T.cst[:, :], 2.0 ** -6))
-    c_e0 = run("V", [], lambda: g.vector.memset(T.e0[:, :], 0.0))
-    c_off0 = run("V", [], lambda: g.vector.memset(T.off0[:, :], 0))
-    c_one = run("V", [], lambda: g.vector.memset(T.one8[:, :], 1.0))
-    i_p = run("G", [], lambda: g.iota(T.pci[:, 0:1], [[0, 1]], 0, 1))
-    i_t = run("G", [], lambda: g.iota(T.tf[:, 0:256], [[9, 256]], 0, 0, allow_small_or_imprecise_dtypes=True))
-    i_d = run("G", [], lambda: g.iota(T.di[:, 0:32], [[1, 32]], 128, -1))
-    a_e0 = run("G", [c_cst, c_e0], lambda: g.affine_select(T.e0[:, 3:515:4], T.cst[:, :], [[-1, 128]], O.is_equal, 0.0, 0, 1))
-    i_m = run("G", [], lambda: g.iota(T.m16[:, :], [[16, 10]], 0, 0, allow_small_or_imprecise_dtypes=True))
-    a_m0 = run("G", [c_one], lambda: g.affine_select(T.mk[:, 0:8], T.one8[:, :], [[-32, 4], [-32, 2]], O.is_ge, 0.0, 0, 1))
-    a_m1 = run("G", [c_one], lambda: g.affine_select(T.mk[:, 8:16], T.one8[:, :], [[-32, 4], [0, 2]], O.is_ge, 0.0, 0, 1))
-
     col = lambda k: T.pcf[:, k:k + 1]
-    h = run("V", [i_p], ts(T.pci[:, 1:2], T.pci[:, 0:1], 16, O.bitwise_and))
-    q15 = run("V", [i_p], ts(T.pci[:, 2:3], T.pci[:, 0:1], 15, O.bitwise_and))
-    d_and = run("V", [i_d], ts(T.di[:, 32:64], T.di[:, 0:32], 15, O.bitwise_and))
-    k_e = run("V", [h], ts(col(0), T.pci[:, 1:2], 0.0, O.is_equal))
-    k_o = run("V", [h], ts(col(1), T.pci[:, 1:2], 0.0, O.is_gt))
-    k_q = run("V", [q15], ts(col(2), T.pci[:, 2:3], -9.0, O.mult, 150.0, O.add))
-    carry = [run("V", [q15], ts(T.carry[:, 0:1], T.pci[:, 2:3], -10.0, O.mult, 150.0, O.add)), 0]
-    d_f = run("V", [d_and], ts(T.df[:, :], T.di[:, 32:64], 0.0, O.is_gt, -522.0, O.mult))
-    m_e = [a_e0,
-           run("V", [a_e0, k_e], ts(T.e1[:, :], T.e0[:, :], col(0), O.mult)),
-           run("V", [a_e0, k_o], ts(T.e2[:, :], T.e0[:, :], col(1), O.mult))]
-    E = {}
+    c_one = run("V", [], fill(T.one[:, :], 1.0))
+    c_e0 = run("V", [], fill(T.e0[:, :], 0.0))
+    i_p = run("G", [], lambda: g.iota(T.pci[:, 0:1], [[0, 1]], 0, 1))
+    i_9 = run("G", [], iota(T.y9[:, :], [[-4, TAB0 // 28], [9, 28]], 0))
+    a_e0 = run("G", [c_one, c_e0], lambda: g.affine_select(T.e0[:, 3:515:4], T.one[:, :], [[-1, 128]], O.is_equal, 0.0, 0, 1))
+    i_16 = run("G", [], iota(T.c16[:, :], [[0, N // 16], [1, 16]], 148))
+    a_mk = run("G", [c_one], lambda: g.affine_select(T.mk[:, :], T.one[:, 0:8], [[-16, 8]], O.is_ge, 0.0, 0, 1))
+    pbc = run("G", [("dP", 16)], lambda: g.partition_broadcast(T.pbc[:, :], T.pin[0:1, :], 128))
+    d_9 = run("S", [i_9], act(T.d9[:, :], T.y9[:, :], F.Abs))
+    b_9 = run("S", [d_9], act(T.b9[:, :], T.d9[:, :], F.Abs, bias=-128.0))
+    k15 = run("V", [i_p], ts(T.pci[:, 1:2], T.pci[:, 0:1], 15, O.bitwise_and))
+    k3 = run("V", [i_p], ts(T.pci[:, 2:3], T.pci[:, 0:1], 2, O.logical_shift_right, 3, O.bitwise_and))
+    c_off0 = run("V", [], fill(T.off0[:, :], 0))
+    c_pb = run("V", [], fill(T.pb[:, 0:16], 0.0))
+    c_ca = run("V", [], fill(T.carry[:, 0:1], 0.0))
+    c_ho = run("V", [], fill(T.hold[:, 1:2 * N:2], 9.0))
+    k_q = run("V", [k15], ts(col(0), T.pci[:, 1:2], 148.0, O.add))
+    k_4 = run("V", [k3], cp(col(1), T.pci[:, 2:3]))
+    c_av = run("V", [], fill(T.av[:, 1:2 * C:2], -256.0))
+    k_o = run("V", [k3, k_q], ts(col(3), T.pci[:, 2:3], 36.0, O.mult, col(0), O.add))
+    i_4 = run("G", [], iota(T.c4[:, :], [[0, N // 4], [1, 4]], 0))
+    i_r = run("G", [c_ho], iota(T.hold[:, 7:2 * N:8], [[4, N // 4]], -64))
+    E = [run("V", [a_e0], quant(T.eq[:, 128 * b:128 * b + 128], T.es[:, 128 * b:128 * b + 128], T.e0[:, 3 - b:515 - b])) for b in range(4)]
 
-    def equant(y, b):
-        k = 128 * (4 * y + b)
-        src = (T.e0, T.e1, T.e2)[y]
-        E[y, b] = run("V", [m_e[y]], quant(T.eq[:, k:k + 128], T.es[:, k:k + 128], src[:, 3 - b:515 - b]))
-
-    for b in range(4):
-        equant(0, b)
-    for i, c in enumerate((1280.0, 768.0, 512.0, 256.0)):
-        i_t = run("S", [i_t], act(T.tf[:, 256 * i + 256:256 * i + 512], T.tf[:, 256 * i:256 * i + 256], F.Abs, bias=-c))
-        if i == 0:
-            d_h = run("S", [d_f], act(T.hold[:, 0:32], T.df[:, :], F.Identity, bias=512.0))
-        else:
-            lo = 16 << i
-            d_h = run("S", [d_h], act(T.hold[:, lo:2 * lo], T.hold[:, 0:lo]))
-    m_t = [run("S", [i_t], act(T.tab[:, 0:256], T.tf[:, 1024:1280], F.Abs, bias=-128.0))]
-    d_h = run("S", [d_h], act(T.hold[:, 256:320], T.hold[:, 0:64]))
-
-    def eside(y, b):
-        k = 128 * (4 * y + b)
-        return T.eq[:, k:k + 128], T.es[:, k:k + 128]
-
+    st = {}
+    carry = [c_ca, 0]
+    tabs = []
     u2 = []
-
-    QT = [T.q0, T.q1, T.q2, T.q3]
-    ST = [T.s0, T.s1, T.s2, T.s3]
-    XT = [T.X0, T.X1, T.X2, T.X3]
-    bank = {}
-    qx, S, st = {}, {}, {}
+    hd = []
+    th = []
 
     def sl(k):
-        return slice(C0[k], C0[k] + NB[k])
+        return slice(N * k, N * k + N)
 
-    def quantx(t, k, deps):
-        a, n = C0[k], NB[k]
-        qx[t, k] = run("V", deps, quant(QT[t][:, a:a + n], ST[t][:, a:a + n], XT[t][:, 4 * a:4 * a + 4 * n]))
+    def qx(t, k):
+        a = N * k
+        deps = [("dXB" if k else "dXA", 16)] if t == 0 else [st[t - 1, k, "x", b] for b in range(4)]
+        st[t, k, "q"] = run("V", deps, quant(QT[t][:, sl(k)], ST[t][:, sl(k)], XT[t][:, 4 * a:4 * a + 4 * N]))
 
     def send(t):
-        need("G", [qx[t, 0]])
+        need("G", [st[t, 0, "q"]])
         rid, pid = topo.addr(prev, core)
         m = sum(1 << e for e in topo.engines(core, prev)[::2])
         g.remote_dma(QT[t][:, C:W].bitcast(dt.uint8), QT[t][:, 0:H].bitcast(dt.uint8), T.sem["arr%d" % t], T.sem.sent, pid, rid, m)
         g.remote_dma(ST[t][:, C:W], ST[t][:, 0:H], T.sem["arr%d" % t], T.sem.sent, pid, rid, m)
 
-    def sprod(t, k):
-        bk = 4 * k + 3
-        S[t, k] = run("T", [qx[t, k], bank.get(bk)] + u2,
-                      mm(bk, NB[k], T.u2q[:, :], T.u2s[:, :], QT[t][:, sl(k)], ST[t][:, sl(k)]))
+    def score(t, k):
+        st[t, k, "S"] = mm(7, N, [st[t, k, "q"]] + u2, T.u2q[:, :], T.u2s[:, :], QT[t][:, sl(k)], ST[t][:, sl(k)])
 
-    def fill(todo):
-        if todo:
-            todo.pop(0)()
+    BANKS = ((4, 5, 6, 4), (0, 1, 2, 3), (5, 6, 7, 4))
 
-    def chain1(t, k, todo=None):
-        n, a = NB[k], C * t + C0[k]
-        bk = 4 * k + 3
-        x = run("V", [S[t, k]], ts(T.pos[:, a:a + n], T.ps[:, 512 * bk:512 * bk + n], 0.0, O.is_gt))
-        bank[bk] = x
-        fill(todo)
-        x = run("V", [x], scan(T.cnt[:, a:a + n], T.pos[:, a:a + n], T.pos[:, a:a + n], 0.0, O.add, O.max))
-        fill(todo)
-        y = run("V", [x, d_h], scan(T.hn[:, a:a + n], T.hold[:, 0:n], T.cnt[:, a:a + n], 0.0, O.add, O.min))
-        fill(todo)
-        w = 18 * t + 8 * k
-        cc = carry[1]
-        st[t, k, "nw"] = run("V", [y, carry[0]], ts(T.nw[:, w:w + n // 16], T.hn[:, a + 15:a + n:16], T.carry[:, cc:cc + 1], O.add))
-        st[t, k, "last"] = (x, T.cnt[:, a + n - 1:a + n])
+    def unpack(t, k, bs=range(4)):
+        a, n = N * k, min(N, W - N * k)
+        dep = st[t, k, "q"] if k < 2 else ("arr%d" % t, 2 * len(topo.engines(nxt, core)[::2]))
+        for b in bs:
+            st[t, k, "D", b] = mm(BANKS[k][b], n, [E[b], dep], T.eq[:, 128 * b:128 * b + 128], T.es[:, 128 * b:128 * b + 128], QT[t][:, a:a + n], ST[t][:, a:a + n])
 
-    def gath(t, k):
-        n, a, w = NB[k], C * t + C0[k], 18 * t + 8 * k
-        width = (256, 512)[k] if t == 0 else TAB
-        st[t, k, "b"] = run("S", [st[t, k, "nw"]] + m_t[:1 if width == 256 else 2 if width == 512 else 4],
-                            act(T.bt[:, a:a + n], T.tab[:, 0:width].indirect(T.nw[:, w:w + n // 16])))
+    def lay(t, k, bs=range(4)):
+        a, n = N * k, min(N, W - N * k)
+        for b in bs:
+            st[t, k, "T"] = bank[BANKS[k][b]] = run("S", [st[t, k, "D", b]], act(WT[t][:, 4 * a + b:4 * a + 4 * n:4], ps(BANKS[k][b], n), scale=2.0 ** -6))
+
+    def signs(t, k):
+        a = C * t + N * k
+        x = st[t, k, "S"]
+        st[t, k, "pa"] = run("V", [x] + th, tt(T.pa[:, a:a + N], ps(7, N), T.tha[:, :], O.is_gt))
+        st[t, k, "pb"] = bank[7] = run("V", [x] + th, tt(T.pb[:, a + 16:a + 16 + N], ps(7, N), T.thb[:, :], O.is_gt))
+
+    def counts(t, k):
+        a = C * t + N * k
+        st[t, k, "cnt"] = run("V", [st[t, k, "pb"], c_pb], scan(T.cnt[:, a:a + N], T.pa[:, a:a + N], T.pb[:, a:a + N], 0.0, O.add, O.add))
+
+    def places(t, k):
+        a, w, cc = C * t + N * k, 20 * t + 10 * k, carry[1]
+        st[t, k, "nw"] = run("V", [st[t, k, "cnt"], carry[0]], ts(T.nw[:, w:w + N // 16], T.cnt[:, a + 15:a + N:16], T.carry[:, cc:cc + 1], O.add))
 
     def count_on(t, k):
-        x, e = st[t, k, "last"]
-        cc = carry[1]
-        carry[0] = run("S", [x, carry[0]], act(T.carry[:, cc + 1:cc + 2], e, F.Identity, bias=T.carry[:, cc:cc + 1]))
+        a, cc = C * t + N * k, 2 * t + k
+        carry[0] = run("S", [st[t, k, "cnt"], carry[0]], act(T.carry[:, cc + 1:cc + 2], T.cnt[:, a + N - 1:a + N], F.Identity, bias=T.carry[:, cc:cc + 1]))
         carry[1] = cc + 1
 
-    last = {}
+    def look(t, k):
+        w = 20 * t + 10 * k
+        width = TAB0 // 16 * 16 if t == 0 else TAB
+        st[t, k, "a"] = run("S", [st[t, k, "nw"], c_av, st.get((t - 1, k, "hh"))] + (tabs[:2] if t == 0 else tabs),
+                            act(T.av[:, 2 * N * k:2 * N * k + 2 * N:2], T.tab[:, 0:width].indirect(T.nw[:, w:w + N // 16])))
 
-    def chain2a(t, k, todo=None):
-        n, a, d = NB[k], C * t + C0[k], 2 * (C * t + C0[k])
-        x = [run("V", [st[t, k, "b"], sc[l]], ts(T.d1[:, d + l * n:d + l * n + n], T.bt[:, a:a + n], col(3 + l), O.add, col(3 + l), O.add)) for l in range(2)]
-        pp = []
-        fill(todo)
-        for l in range(2):
-            init, tok = last.get(l, (col(3 + l), None))
-            e = d + l * n
-            pt = run("V", [x[l], st[t, k, "b"], tok], scan(T.pl[:, e:e + n], T.bt[:, a:a + n], T.d1[:, e:e + n], init, O.max, O.min))
-            last[l] = (T.pl[:, e + n - 1:e + n], pt)
-            pp.append(pt)
-        st[t, k, "pl"] = pp
+    def held(t, k):
+        d = 2 * (C * t + N * k)
+        st[t, k, "hh"] = run("V", [st[t, k, "a"]] + hd, scan(T.hh[:, d:d + 2 * N], T.hold[:, :], T.av[:, 2 * N * k:2 * N * k + 2 * N], 0.0, O.add, O.max))
 
-    def chain2b(t, k, todo=None):
-        n, d, o = NB[k], 2 * (C * t + C0[k]), 36 * t + 16 * k
-        m = 2 * n // 16
-        fill(todo)
-        x = run("V", st[t, k, "pl"] + [d_h], scan(T.hh[:, d:d + 2 * n], T.hold[:, 0:2 * n], T.pl[:, d:d + 2 * n], 0.0, O.add, O.min))
-        fill(todo)
-        x = run("V", [x] + bs[k], tt(T.of[:, o:o + m], T.hh[:, d + 15:d + 2 * n:16], T.base[:, 16 * k:16 * k + m], O.add))
-        fill(todo)
-        st[t, k, "off"] = run("V", [x], cp(T.off[:, o:o + m], T.of[:, o:o + m]))
+    def offs(t, k):
+        d, o = 2 * (C * t + N * k), 72 * t + 36 * k
+        st[t, k, "off"] = run("V", [st[t, k, "hh"], k_o], ts(T.off[:, o:o + 36], T.hh[:, d + 7:d + 2 * N:8], 4.0, O.mult, col(3), O.add))
 
-    def picks(t, k):
-        n, o = NB[k], 36 * t + 16 * k
-        lo, hi = (0, C) if k == 0 else (H, W)
-        fq, fs = T["f%d%d" % (t, k)], T["g%d%d" % (t, k)]
-        deps = [st[t, k, "off"], qx[t, 0], qx[t, 1]] + ([("arr%d" % t, 2 * len(topo.engines(nxt, core)[::2]))] if k else [])
-        for l in range(2):
-            off = T.off[:, o + l * n // 16:o + (l + 1) * n // 16]
-            c, d = l * n, (l + 1) * n
-            st[t, k, "pk", l] = [
-                run("V", deps, cp(fq[:, c:d].bitcast(dt.uint32), QT[t][:, lo:hi].bitcast(dt.uint32).indirect(off))),
-                run("S", deps, act(fs[:, c:d], ST[t][:, lo:hi].indirect(off)))]
+    def twin(t, k, q):
+        a, z = 4 * N * k, 4 * (C * t + N * k)
+        st[t, k, "own"] = run(q, [st[t, k, "T"]], (cp if q == "V" else act)(T.own[:, z:z + 4 * N], WT[t][:, a:a + 4 * N]))
 
-    def own(t, k, bs_=range(4)):
-        for b in bs_:
-            bk = 4 * k + b
-            lq, ls = eside(0, b)
-            run("T", [E[0, b], qx[t, k], bank.get(bk)], mm(bk, NB[k], lq, ls, QT[t][:, sl(k)], ST[t][:, sl(k)], True, False))
-
-    def far(t, k, l):
-        n = NB[k]
-        fq, fs = T["f%d%d" % (t, k)], T["g%d%d" % (t, k)]
-        for b in range(4):
-            lq, ls = eside(1 + l, b)
-            st[t, k, "z", b] = run("T", [E[1 + l, b]] + st[t, k, "pk", l],
-                                   mm(4 * k + b, n, lq, ls, fq[:, l * n:l * n + n], fs[:, l * n:l * n + n], False, l == 1))
-
-    def on_v(k):
-        return VC[k]
-
-    def on_s(k):
-        return [b for b in range(4) if b not in VC[k]]
-
-    def cast(t, k, b):
-        n, z = NB[k], 4 * (C * t + C0[k])
-        out, in_ = T.zt[:, z + b:z + 4 * n:4], T.ps[:, 512 * (4 * k + b):512 * (4 * k + b) + n]
-        v = b in on_v(k)
-        st[t, k, "c", b] = bank[4 * k + b] = run("V" if v else "S", [st[t, k, "z", b]], cp(out, in_) if v else act(out, in_))
+    def blend(t, k):
+        a, o, z = 4 * N * k, 72 * t + 36 * k, 4 * (C * t + N * k)
+        st[t, k, "z"] = run("V", [st[t, k, "off"], st[t, k, "own"], st[t, k + 1, "T"]],
+                            tt(T.zt[:, z:z + 4 * N], WT[t][:, a:min(a + 8 * N, 4 * W)].indirect(T.off[:, o:o + 36]), T.own[:, z:z + 4 * N], O.add))
 
     def qz(t, k):
-        n, a = NB[k], C * t + C0[k]
-        st[t, k, "qz"] = run("V", [st[t, k, "c", b] for b in range(4)], quant(T.zq[:, a:a + n], T.zs[:, a:a + n], T.zt[:, 4 * a:4 * a + 4 * n]))
+        a = C * t + N * k
+        st[t, k, "qz"] = run("V", [st[t, k, "z"]], quant(T.zq[:, a:a + N], T.zs[:, a:a + N], T.zt[:, 4 * a:4 * a + 4 * N]))
 
-    def wprod(t, k):
-        n, a = NB[k], C * t + C0[k]
+    def layer(t, k):
+        a = C * t + N * k
         for b in range(4):
-            st[t, k, "r", b] = run("T", [("dW", 32), st[t, k, "qz"], bank.get(4 * k + b)],
-                                   mm(4 * k + b, n, T.wq[:, 128 * b:128 * b + 128], T.wsc[:, 128 * b:128 * b + 128], T.zq[:, a:a + n], T.zs[:, a:a + n]))
+            st[t, k, "r", b] = mm(b, N, [("dW", 32), st[t, k, "qz"]], T.wq[:, 128 * b:128 * b + 128], T.wsc[:, 128 * b:128 * b + 128], T.zq[:, a:a + N], T.zs[:, a:a + N])
 
-    def xupd(t, k, bs_):
-        n, a, e = NB[k], 4 * C0[k], 4 * (C0[k] + NB[k])
-        for b in bs_:
-            st[t, k, "x", b] = bank[4 * k + b] = run(
-                "V", [st[t, k, "r", b], ("dXA", 16) if t == 0 and k == 0 else ("dXB", 16) if t == 0 else st[t - 1, k, "x", b]],
-                tt(XT[t + 1][:, a + b:e:4], T.ps[:, 512 * (4 * k + b):512 * (4 * k + b) + n], XT[t][:, a + b:e:4], O.add))
+    def xupd(t, k, bs=range(4)):
+        a, e = 4 * N * k, 4 * N * k + 4 * N
+        for b in bs:
+            st[t, k, "x", b] = bank[b] = run("V", [st[t, k, "r", b], st[t, k, "q"]], tt(XT[t + 1][:, a + b:e:4], ps(b, N), XT[t][:, a + b:e:4], O.add))
 
-    def newx(t, k):
-        quantx(t + 1, k, [st[t, k, "x", b] for b in range(4)])
+    def results(k):
+        y = mm(4 + k, N, [vq, st[R, k, "q"]], T.vq[:, :], T.vs[:, :], QT[R][:, sl(k)], ST[R][:, sl(k)])
+        st["y", k] = run("S", [y], act(T.ysb[:, sl(k)], ps(4 + k, N)))
 
-    def yprod(k):
-        n = NB[k]
-        bk = 4 * k
-        return run("T", [vq, qx[R, k], bank.get(bk)], mm(bk, n, T.vq[:, :], T.vs[:, :], T.q3[:, sl(k)], T.s3[:, sl(k)]))
-
-    pf = run("V", [("dP", 16)], cp(T.pfl[0:1, :], T.pin[0:1, :]))
-    pb = run("G", [pf], lambda: g.partition_broadcast(T.pbc[:, :], T.pfl[0:1, :], 128))
-    quantx(0, 0, [("dXA", 16)])
-    send(0)
     uq = run("V", [("dU", 16)], quant(T.uq[:, :], T.us[:, :], T.ut[:, :]))
+    th += [run("V", [i_16, k_q], ts(T.tha[:, :], T.c16[:, :], col(0), O.is_gt, BIG, O.mult)),
+           run("V", [i_16, k_q], ts(T.thb[:, :], T.c16[:, :], col(0), O.is_le, BIG, O.mult))]
     u2 += [run("V", [uq, c_off0], cp(T.u2q[:, 0:128].bitcast(dt.uint32), T.uq[:, 0:128].bitcast(dt.uint32).indirect(T.off0[:, 0:8]))),
            run("S", [uq, c_off0], act(T.u2s[:, 0:128], T.us[:, 0:128].indirect(T.off0[:, 0:8])))]
-    sprod(0, 0)
-    equant(1, 0)
-    equant(1, 1)
-    chain1(0, 0, [lambda: equant(1, 2), lambda: equant(1, 3)])
-    gath(0, 0)
+    qx(0, 0)
+    send(0)
+    score(0, 0)
+    unpack(0, 0, (0, 1, 2))
+    pm = run("V", [pbc, a_mk], tt(T.pm[:, :], T.pbc[:, :], T.mk[:, :], O.mult))
+    hd += [i_r, run("V", [i_4, k_4], ts(T.hold[:, 0:2 * N:2], T.c4[:, :], col(1), O.is_equal, -1024.0, O.mult))]
+    k_s = run("V", [pm], lambda: g.vector.tensor_reduce(col(4), T.pm[:, :], AxisListType.X, O.add))
+    hi = run("S", [k_s, b_9], act(T.hi[:, :], T.b9[:, :], F.Identity, bias=col(4)))
+    lo = run("V", [k_s, b_9], ts(T.lo[:, :], T.b9[:, :], col(4), O.subtract))
+    tabs.append(run("S", [lo], act(T.tab[:, 0:1], T.lo[:, 0:1])))
+    signs(0, 0)
+    qx(0, 1)
+    lay(0, 0, (0, 1, 2))
+    score(0, 1)
+    unpack(0, 0, (3,))
+    unpack(0, 1)
+    k_i = run("V", [lo, st[0, 0, "pa"]], ts(col(5), T.pa[:, 0:1], 0.0, O.is_equal, T.lo[:, 0:1], O.mult))
+    counts(0, 0)
     count_on(0, 0)
-    for lo, hi in ((256, 512), (512, 768), (768, TAB)):
-        m_t.append(run("S", m_t[:1], act(T.tab[:, lo:hi], T.tab[:, 0:hi - lo])))
-    pm = [run("V", [pb, (a_m0, a_m1)[l]], tt(T.pm[:, 8 * l:8 * l + 8], T.pbc[:, :], T.mk[:, 8 * l:8 * l + 8], O.mult)) for l in range(2)]
-    sc = [run("V", [pm[l]], lambda l=l: g.vector.tensor_reduce(col(3 + l), T.pm[:, 8 * l:8 * l + 8], AxisListType.X, O.add)) for l in range(2)]
-    quantx(0, 1, [("dXB", 16)])
-    cc2, bs = [], [[], []]
-
-    def c_cc():
-        for l in range(2):
-            cc2.append(run("V", [sc[l], k_q], tt(col(7 + l), col(2), col(3 + l), O.subtract)))
-
-    def c_base(k):
-        m = NB[k] // 16
-        for l in range(2):
-            o = 16 * k + m * l
-            bs[k].append(run("V", [cc2[l], i_m], ts(T.base[:, o:o + m], T.m16[:, 0:m], col(7 + l), O.add)))
-
-    chain2a(0, 0, [c_cc])
-    chain2b(0, 0, [lambda: c_base(0), lambda: equant(2, 0), lambda: equant(2, 1)])
-    own(0, 0)
-    vq = None
+    tabs.append(run("V", [k_i, hi], scan(T.tab[:, 1:TAB0], T.lo[:, 1:TAB0], T.hi[:, 1:TAB0], col(5), O.max, O.min)))
+    carry[:] = [c_ca, 0]
+    places(0, 0)
+    carry[:] = [("S", count["S"]), 1]
+    look(0, 0)
+    lay(0, 0, (3,))
+    lay(0, 1)
+    signs(0, 1)
+    counts(0, 1)
+    held(0, 0)
+    places(0, 1)
+    look(0, 1)
+    count_on(0, 1)
+    twin(0, 0, "V")
+    offs(0, 0)
 
     for t in range(R):
-        sprod(t, 1)
-        picks(t, 0)
-        far(t, 0, 0)
-        if t == 0:
-            equant(2, 2)
-            equant(2, 3)
-        far(t, 0, 1)
-        for b in on_s(0):
-            cast(t, 0, b)
-        chain1(t, 1, [lambda: None] + [lambda b=b: cast(t, 0, b) for b in on_v(0)])
-        gath(t, 1)
-        count_on(t, 1)
-        own(t, 1, (0, 1))
+        last = t == R - 1
+        twin(t, 1, "S")
+        unpack(t, 2)
+        lay(t, 2)
+        blend(t, 0)
+        held(t, 1)
         qz(t, 0)
-        wprod(t, 0)
-        own(t, 1, (2, 3))
+        layer(t, 0)
+        offs(t, 1)
         if t == 0:
-            c_base(1)
-        xs = [lambda b=b: xupd(t, 0, (b,)) for b in range(4)]
-        chain2a(t, 1, xs)
-        chain2b(t, 1, xs)
-        for f in xs:
-            f()
-        newx(t, 0)
-        if t < R - 1:
-            send(t + 1)
-            picks(t, 1)
-            sprod(t + 1, 0)
-            far(t, 1, 0)
-            far(t, 1, 1)
-            chain1(t + 1, 0)
-            gath(t + 1, 0)
-            for b in on_s(1) + list(on_v(1)[:-1]):
-                cast(t, 1, b)
-            count_on(t + 1, 0)
-
-            def zb():
-                for b in on_v(1)[-1:]:
-                    cast(t, 1, b)
-                qz(t, 1)
-            chain2a(t + 1, 0, [zb])
-            wprod(t, 1)
-            xs = [lambda b=b: xupd(t, 1, (b,)) for b in range(4)]
-            chain2b(t + 1, 0, [lambda: None] + xs)
-            for b in range(2, 4):
-                xs[b]()
-            newx(t, 1)
-            own(t + 1, 0)
-        else:
-            picks(t, 1)
-            far(t, 1, 0)
-            far(t, 1, 1)
+            for a, e in ((TAB0, TAB0 + 256), (TAB0 + 256, TAB0 + 512), (TAB0 + 512, TAB)):
+                tabs.append(run("S", tabs[-1:], act(T.tab[:, a:e], T.tab[:, a - 256:e - 256])))
+        if last:
+            ax = run("S", [st[t, 0, "a"], st[t, 1, "a"]], act(T.aof[:, :], T.av[:, 0:2 * C:2]))
+            need("Y", [ax])
+            g.sync.dma_start(T.ao[:, :], T.aof[0:128:16, :]).then_inc(T.sem.outA, 16)
             vq = run("V", [("dV", 16)], quant(T.vq[:, :], T.vs[:, :], T.vt[:, :]))
-            ns = [run("V", [sc[l]], ts(col(5 + l), col(3 + l), -1.0, O.mult)) for l in range(2)]
-            y0 = yprod(0)
-            for b in range(4):
-                cast(t, 1, b)
-            ax = []
-            for kk in range(2):
-                n, d = NB[kk], 2 * (C * t + C0[kk])
-                for l in range(2):
-                    ax.append(run("S", st[t, kk, "pl"] + [ns[l]], act((T.ao0, T.ao1)[l][:, sl(kk)], T.pl[:, d + l * n:d + l * n + n], F.Identity, bias=col(5 + l))))
-            ys = run("S", [y0], act(T.ysb[:, 0:128], T.ps[:, 0:128]))
-            need("Y", [qx[R, 0]])
-            g.sync.dma_start(T.oc[:, 0:512], T.q3[:, 0:128].bitcast(dt.uint8)).then_inc(T.sem.outA, 16)
-            need("Y", ax)
-            for l in range(2):
-                g.sync.dma_start(T.ao[l:8:2, :], (T.ao0, T.ao1)[l][0:128:32, :]).then_inc(T.sem.outA, 16)
-            need("Y", [ys])
-            g.sync.dma_start(T.y[:, 0:128], T.ysb[:, 0:128]).then_inc(T.sem.outA, 16)
-            qz(t, 1)
-            wprod(t, 1)
-            xupd(t, 1, range(4))
-            newx(t, 1)
-    y1 = run("S", [yprod(1)], act(T.ysb[:, 128:288], T.ps[:, 2048:2208]))
-    need("Y", [qx[R, 1]])
-    for k in range(3):
-        g.sync.dma_start(T.osc[4 * k:4 * k + 4, :], T.s3[32 * k:32 * k + 4, 0:C]).then_inc(T.sem.outA, 16)
-    g.scalar.dma_start(T.oc[:, 512:1152], T.q3[:, 128:288].bitcast(dt.uint8)).then_inc(T.sem.outB, 16)
-    g.scalar.dma_start(T.osc[12:16, :], T.s3[96:100, 0:C]).then_inc(T.sem.outB, 16)
-    need("Y", [y1])
-    g.sync.dma_start(T.y[:, 128:288], T.ysb[:, 128:288]).then_inc(T.sem.outA, 16)
+        blend(t, 1)
+        xupd(t, 0, (0, 1))
+        qz(t, 1)
+        xupd(t, 0, (2, 3))
+        layer(t, 1)
+        qx(t + 1, 0)
+        if last:
+            xupd(t, 1)
+            qx(t + 1, 1)
+            break
+        send(t + 1)
+        score(t + 1, 0)
+        unpack(t + 1, 0, (0, 1, 2))
+        lay(t + 1, 0, (0, 1, 2))
+        unpack(t + 1, 0, (3,))
+        lay(t + 1, 0, (3,))
+        xupd(t, 1)
+        signs(t + 1, 0)
+        qx(t + 1, 1)
+        score(t + 1, 1)
+        unpack(t + 1, 1)
+        counts(t + 1, 0)
+        places(t + 1, 0)
+        count_on(t + 1, 0)
+        look(t + 1, 0)
+        lay(t + 1, 1)
+        signs(t + 1, 1)
+        twin(t + 1, 0, "V")
+        counts(t + 1, 1)
+        held(t + 1, 0)
+        places(t + 1, 1)
+        look(t + 1, 1)
+        if t + 1 < R - 1:
+            count_on(t + 1, 1)
+        offs(t + 1, 0)
+    results(0)
+    need("Y", [st[R, 0, "q"]])
+    g.sync.dma_start(T.oc[:, 0:4 * N], QT[R][:, 0:N].bitcast(dt.uint8)).then_inc(T.sem.outA, 16)
+    need("Y", [st["y", 0]])
+    g.sync.dma_start(T.y[:, 0:N], T.ysb[:, 0:N]).then_inc(T.sem.outA, 16)
+    need("S", [st[R, 1, "q"]])
+    g.scalar.dma_start(T.oc[:, 4 * N:4 * C], QT[R][:, N:C].bitcast(dt.uint8)).then_inc(T.sem.outB, 16)
+    results(1)
+    need("Y", [st[R, 1, "q"]])
+    for k in range(4):
+        g.sync.dma_start(T.osc[4 * k:4 * k + 4, :], ST[R][32 * k:32 * k + 4, 0:C]).then_inc(T.sem.outA, 16)
+    need("S", [st["y", 1]])
+    g.scalar.dma_start(T.y[:, N:C], T.ysb[:, N:C]).then_inc(T.sem.outB, 16)
     for q in ("V", "S", "T", "G"):
         need("Y", [(q, count[q])])
-    g.sync.wait_ge(T.sem.outA, 16 * 8)
+    g.sync.wait_ge(T.sem.outA, 16 * 7)
     g.scalar.wait_ge(T.sem.outB, 16 * 2)
     g.wait_ge(T.sem.sent, 2 * R * len(topo.engines(core, prev)[::2]))

@@ -2,8 +2,10 @@ from concourse.mybir import dt, AluOpType as O, AxisListType, ActivationFunction
 
 C, H, R, W = 288, 128, 3, 416
 N = 144
-TAB, TAB0 = 880, 308
+C0, NB = (0, N, C), (N, N, H)
+TAB, TAB0, TAB1 = 880, 308, 168
 BIG = 2.0 ** 90
+OPT = {}
 
 F8 = "float8_e4m3fn_x4"
 SCRATCH = {
@@ -12,14 +14,13 @@ SCRATCH = {
     "u2q": ("sbuf", [128, 128], F8), "u2s": ("sbuf", [128, 128], "uint8"),
     "vq": ("sbuf", [128, 128], F8), "vs": ("sbuf", [128, 128], "uint8"),
     "wq": ("sbuf", [128, 512], F8), "wsc": ("sbuf", [128, 512], "uint8"),
-    "one": ("sbuf", [128, 128], "bfloat16"), "e0": ("sbuf", [128, 516], "bfloat16"),
+    "two": ("sbuf", [128, 128], "bfloat16"), "four": ("sbuf", [128, 32], "bfloat16"), "e0": ("sbuf", [128, 516], "bfloat16"),
     "eq": ("sbuf", [128, 512], F8), "es": ("sbuf", [128, 512], "uint8"),
     "off0": ("sbuf", [128, 8], "uint16"),
     "pci": ("sbuf", [128, 4], "int32"), "pcf": ("sbuf", [128, 8], "float32"),
-    "y9": ("sbuf", [128, TAB0], "bfloat16"), "d9": ("sbuf", [128, TAB0], "bfloat16"), "b9": ("sbuf", [128, TAB0], "bfloat16"),
-    "lo": ("sbuf", [128, TAB0], "bfloat16"), "hi": ("sbuf", [128, TAB0], "bfloat16"),
-    "tab": ("sbuf", [128, TAB], "bfloat16"),
-    "c16": ("sbuf", [128, N], "bfloat16"), "c4": ("sbuf", [128, N], "bfloat16"),
+    "y9": ("sbuf", [128, TAB1], "bfloat16"), "d9": ("sbuf", [128, TAB0], "bfloat16"), "b9": ("sbuf", [128, TAB0], "bfloat16"),
+    "hi": ("sbuf", [128, TAB0], "bfloat16"), "tab": ("sbuf", [128, TAB], "bfloat16"),
+    "c16": ("sbuf", [128, N], "bfloat16"), "c8": ("sbuf", [128, N], "bfloat16"),
     "tha": ("sbuf", [128, N], "bfloat16"), "thb": ("sbuf", [128, N], "bfloat16"),
     "hold": ("sbuf", [128, 2 * N], "bfloat16"),
     "mk": ("sbuf", [128, 8], "bfloat16"), "pm": ("sbuf", [128, 8], "float32"),
@@ -29,7 +30,7 @@ SCRATCH = {
     "cnt": ("sbuf", [128, R * C], "bfloat16"),
     "nw": ("sbuf", [128, R * 20], "uint16"),
     "av": ("sbuf", [128, 2 * C], "bfloat16"), "hh": ("sbuf", [128, R * 2 * C], "bfloat16"),
-    "off": ("sbuf", [128, R * 72], "uint16"),
+    "off": ("sbuf", [128, R * 36], "uint16"),
     "zt": ("sbuf", [128, R * 4 * C], "bfloat16"),
     "own": ("sbuf", [128, R * 4 * C], "bfloat16"),
     "zq": ("sbuf", [128, R * C], F8), "zs": ("sbuf", [128, R * C], "uint8"),
@@ -43,6 +44,9 @@ for _t in range(R + 1):
 for _t in range(R):
     SCRATCH["w%d" % _t] = ("sbuf", [128, 4 * W], "bfloat16")
 SEMAPHORES = ["V", "S", "T", "G", "dXA", "dXB", "dU", "dP", "dW", "dV", "arr0", "arr1", "arr2", "sent", "outA", "outB"]
+B_S = (4, 0)
+B_D = ((5, 7, 6, 4), (1, 3, 2, 5), (1, 3, 2, 0))
+B_W = ((4, 5, 6, 7), (0, 1, 2, 3))
 
 
 def rank_program(g, core, T, topo):
@@ -112,9 +116,9 @@ def rank_program(g, core, T, topo):
     XT = [T["X%d" % t] for t in range(R + 1)]
     WT = [T["w%d" % t] for t in range(R)]
 
-    g.sync.dma_start(T.ut[:, :], T.u[:, :]).then_inc(T.sem.dU, 16)
     g.scalar.dma_start(T.pin[0:1, :], T.p[:, :]).then_inc(T.sem.dP, 16)
-    g.scalar.dma_start(T.X0[:, 0:4 * N], T.x[:, 0:4 * N]).then_inc(T.sem.dXA, 16)
+    g.sync.dma_start(T.ut[:, 0:8], T.u[:, 0:8]).then_inc(T.sem.dU, 16)
+    g.sync.dma_start(T.X0[:, 0:4 * N], T.x[:, 0:4 * N]).then_inc(T.sem.dXA, 16)
     g.sync.dma_start(T.X0[:, 4 * N:4 * C], T.x[:, 4 * N:4 * C]).then_inc(T.sem.dXB, 16)
     need("Y", [("dXA", 16)])
     g.sync.dma_start(T.wq[:, :].bitcast(dt.uint8), T.wc[:, :]).then_inc(T.sem.dW, 16)
@@ -122,178 +126,191 @@ def rank_program(g, core, T, topo):
     g.sync.dma_start(T.vt[:, :], T.v[:, :]).then_inc(T.sem.dV, 16)
 
     col = lambda k: T.pcf[:, k:k + 1]
-    c_one = run("V", [], fill(T.one[:, :], 1.0))
+    c_two = run("V", [], fill(T.two[:, :], 2.0))
+    c_ut = run("V", [], fill(T.ut[:, 8:512], 0.0))
+    c_off0 = run("V", [], fill(T.off0[:, :], 0))
     c_e0 = run("V", [], fill(T.e0[:, :], 0.0))
     i_p = run("G", [], lambda: g.iota(T.pci[:, 0:1], [[0, 1]], 0, 1))
-    i_9 = run("G", [], iota(T.y9[:, :], [[-4, TAB0 // 28], [9, 28]], 0))
-    a_e0 = run("G", [c_one, c_e0], lambda: g.affine_select(T.e0[:, 3:515:4], T.one[:, :], [[-1, 128]], O.is_equal, 0.0, 0, 1))
-    i_16 = run("G", [], iota(T.c16[:, :], [[0, N // 16], [1, 16]], 148))
-    a_mk = run("G", [c_one], lambda: g.affine_select(T.mk[:, :], T.one[:, 0:8], [[-16, 8]], O.is_ge, 0.0, 0, 1))
+    i_9 = run("G", [], iota(T.y9[:, :], [[-4, TAB1 // 28], [9, 28]], 0))
+    a_mk = run("G", [c_two], lambda: g.affine_select(T.mk[:, :], T.two[:, 0:8], [[-16, 8]], O.is_ge, 0.0, 0, 1))
     pbc = run("G", [("dP", 16)], lambda: g.partition_broadcast(T.pbc[:, :], T.pin[0:1, :], 128))
-    d_9 = run("S", [i_9], act(T.d9[:, :], T.y9[:, :], F.Abs))
-    b_9 = run("S", [d_9], act(T.b9[:, :], T.d9[:, :], F.Abs, bias=-128.0))
+    i_16 = run("G", [], iota(T.c16[:, :], [[0, N // 16], [1, 16]], 74))
+    a_e0 = run("G", [c_two, c_e0], lambda: g.affine_select(T.e0[:, 3:515:4], T.two[:, :], [[-1, 128]], O.is_equal, 0.0, 0, 1))
+    d_9 = [run("S", [i_9], act(T.d9[:, 0:TAB1], T.y9[:, :], F.Abs)),
+           run("S", [i_9], act(T.d9[:, TAB1:TAB0], T.y9[:, 0:TAB0 - TAB1], F.Abs, bias=-4.0 * (TAB1 // 28)))]
+    b_9 = [run("S", [d_9[0]], act(T.b9[:, 0:TAB1], T.d9[:, 0:TAB1], F.Abs, bias=-128.0)),
+           run("S", [d_9[1]], act(T.b9[:, TAB1:TAB0], T.d9[:, TAB1:TAB0], F.Abs, bias=-128.0))]
     k15 = run("V", [i_p], ts(T.pci[:, 1:2], T.pci[:, 0:1], 15, O.bitwise_and))
-    k3 = run("V", [i_p], ts(T.pci[:, 2:3], T.pci[:, 0:1], 2, O.logical_shift_right, 3, O.bitwise_and))
-    c_off0 = run("V", [], fill(T.off0[:, :], 0))
+    k7 = run("V", [i_p], ts(T.pci[:, 2:3], T.pci[:, 0:1], 1, O.logical_shift_right, 7, O.bitwise_and))
     c_pb = run("V", [], fill(T.pb[:, 0:16], 0.0))
     c_ca = run("V", [], fill(T.carry[:, 0:1], 0.0))
+    c_tab = run("V", [], fill(T.tab[:, 0:1], 128.0))
+    k_q = run("V", [k15], ts(col(0), T.pci[:, 1:2], 74.0, O.add))
+    k_8 = run("V", [k7], ts(col(1), T.pci[:, 2:3], -1.0, O.mult, -78.0, O.add))
+    uq = run("V", [("dU", 16), c_ut], quant(T.uq[:, :], T.us[:, :], T.ut[:, :]))
     c_ho = run("V", [], fill(T.hold[:, 1:2 * N:2], 9.0))
-    k_q = run("V", [k15], ts(col(0), T.pci[:, 1:2], 148.0, O.add))
-    k_4 = run("V", [k3], cp(col(1), T.pci[:, 2:3]))
+    c_four = run("V", [], fill(T.four[:, :], 4.0))
     c_av = run("V", [], fill(T.av[:, 1:2 * C:2], -256.0))
-    k_o = run("V", [k3, k_q], ts(col(3), T.pci[:, 2:3], 36.0, O.mult, col(0), O.add))
-    i_4 = run("G", [], iota(T.c4[:, :], [[0, N // 4], [1, 4]], 0))
-    i_r = run("G", [c_ho], iota(T.hold[:, 7:2 * N:8], [[4, N // 4]], -64))
-    E = [run("V", [a_e0], quant(T.eq[:, 128 * b:128 * b + 128], T.es[:, 128 * b:128 * b + 128], T.e0[:, 3 - b:515 - b])) for b in range(4)]
+    u2 = [run("V", [uq, c_off0], cp(T.u2q[:, 0:128].bitcast(dt.uint32), T.uq[:, 0:2].bitcast(dt.uint32).indirect(T.off0[:, 0:8]))),
+          run("S", [uq, c_off0], act(T.u2s[:, 0:128], T.us[:, 0:2].indirect(T.off0[:, 0:8])))]
+    E = {}
+
+    def equant(b):
+        E[b] = run("V", [a_e0], quant(T.eq[:, 128 * b:128 * b + 128], T.es[:, 128 * b:128 * b + 128], T.e0[:, 3 - b:515 - b]))
 
     st = {}
     carry = [c_ca, 0]
-    tabs = []
-    u2 = []
-    hd = []
-    th = []
 
     def sl(k):
-        return slice(N * k, N * k + N)
+        return slice(C0[k], C0[k] + NB[k])
 
     def qx(t, k):
-        a = N * k
+        a = C0[k]
         deps = [("dXB" if k else "dXA", 16)] if t == 0 else [st[t - 1, k, "x", b] for b in range(4)]
         st[t, k, "q"] = run("V", deps, quant(QT[t][:, sl(k)], ST[t][:, sl(k)], XT[t][:, 4 * a:4 * a + 4 * N]))
 
     def send(t):
         need("G", [st[t, 0, "q"]])
         rid, pid = topo.addr(prev, core)
-        m = sum(1 << e for e in topo.engines(core, prev)[::2])
+        m = topo.mask(core, prev)
         g.remote_dma(QT[t][:, C:W].bitcast(dt.uint8), QT[t][:, 0:H].bitcast(dt.uint8), T.sem["arr%d" % t], T.sem.sent, pid, rid, m)
         g.remote_dma(ST[t][:, C:W], ST[t][:, 0:H], T.sem["arr%d" % t], T.sem.sent, pid, rid, m)
 
     def score(t, k):
-        st[t, k, "S"] = mm(7, N, [st[t, k, "q"]] + u2, T.u2q[:, :], T.u2s[:, :], QT[t][:, sl(k)], ST[t][:, sl(k)])
+        st[t, k, "S"] = mm(B_S[k], N, [st[t, k, "q"]] + u2, T.u2q[:, :], T.u2s[:, :], QT[t][:, sl(k)], ST[t][:, sl(k)])
 
-    BANKS = ((4, 5, 6, 4), (0, 1, 2, 3), (5, 6, 7, 4))
-
-    def unpack(t, k, bs=range(4)):
-        a, n = N * k, min(N, W - N * k)
-        dep = st[t, k, "q"] if k < 2 else ("arr%d" % t, 2 * len(topo.engines(nxt, core)[::2]))
+    def unpack(t, k, bs):
+        dep = st[t, k, "q"] if k < 2 else ("arr%d" % t, 2 * len(topo.engines(nxt, core)))
         for b in bs:
-            st[t, k, "D", b] = mm(BANKS[k][b], n, [E[b], dep], T.eq[:, 128 * b:128 * b + 128], T.es[:, 128 * b:128 * b + 128], QT[t][:, a:a + n], ST[t][:, a:a + n])
+            st[t, k, "D", b] = mm(B_D[k][b], NB[k], [E[b], dep], T.eq[:, 128 * b:128 * b + 128], T.es[:, 128 * b:128 * b + 128], QT[t][:, sl(k)], ST[t][:, sl(k)])
 
-    def lay(t, k, bs=range(4)):
-        a, n = N * k, min(N, W - N * k)
+    def half(t, c, lo, hi, i=0, step=1):
+        return WT[t][:, 2 * (W * c + lo) + i:2 * (W * c + hi):step]
+
+    def lay(t, k, bs):
         for b in bs:
-            st[t, k, "T"] = bank[BANKS[k][b]] = run("S", [st[t, k, "D", b]], act(WT[t][:, 4 * a + b:4 * a + 4 * n:4], ps(BANKS[k][b], n), scale=2.0 ** -6))
+            st[t, k, "T", b] = bank[B_D[k][b]] = run("S", [st[t, k, "D", b]], act(half(t, b % 2, C0[k], C0[k] + NB[k], b // 2, 2), ps(B_D[k][b], NB[k]), scale=2.0 ** -7))
 
     def signs(t, k):
-        a = C * t + N * k
+        a = C * t + C0[k]
         x = st[t, k, "S"]
-        st[t, k, "pa"] = run("V", [x] + th, tt(T.pa[:, a:a + N], ps(7, N), T.tha[:, :], O.is_gt))
-        st[t, k, "pb"] = bank[7] = run("V", [x] + th, tt(T.pb[:, a + 16:a + 16 + N], ps(7, N), T.thb[:, :], O.is_gt))
+        st[t, k, "pa"] = run("V", [x] + th, tt(T.pa[:, a:a + N], ps(B_S[k], N), T.tha[:, :], O.is_gt))
+        st[t, k, "pb"] = bank[B_S[k]] = run("V", [x] + th, tt(T.pb[:, a + 16:a + 16 + N], ps(B_S[k], N), T.thb[:, :], O.is_gt))
 
     def counts(t, k):
-        a = C * t + N * k
+        a = C * t + C0[k]
         st[t, k, "cnt"] = run("V", [st[t, k, "pb"], c_pb], scan(T.cnt[:, a:a + N], T.pa[:, a:a + N], T.pb[:, a:a + N], 0.0, O.add, O.add))
 
     def places(t, k):
-        a, w, cc = C * t + N * k, 20 * t + 10 * k, carry[1]
+        a, w, cc = C * t + C0[k], 20 * t + 10 * k, carry[1]
         st[t, k, "nw"] = run("V", [st[t, k, "cnt"], carry[0]], ts(T.nw[:, w:w + N // 16], T.cnt[:, a + 15:a + N:16], T.carry[:, cc:cc + 1], O.add))
 
     def count_on(t, k):
-        a, cc = C * t + N * k, 2 * t + k
-        carry[0] = run("S", [st[t, k, "cnt"], carry[0]], act(T.carry[:, cc + 1:cc + 2], T.cnt[:, a + N - 1:a + N], F.Identity, bias=T.carry[:, cc:cc + 1]))
-        carry[1] = cc + 1
+        a, cc = C * t + C0[k], 2 * t + k
+        if (t, k) != (R - 1, 1):
+            carry[0] = run("S", [st[t, k, "cnt"], carry[0]], act(T.carry[:, cc + 1:cc + 2], T.cnt[:, a + N - 1:a + N], F.Identity, bias=T.carry[:, cc:cc + 1]))
+            carry[1] = cc + 1
 
     def look(t, k):
         w = 20 * t + 10 * k
-        width = TAB0 // 16 * 16 if t == 0 else TAB
-        st[t, k, "a"] = run("S", [st[t, k, "nw"], c_av, st.get((t - 1, k, "hh"))] + (tabs[:2] if t == 0 else tabs),
-                            act(T.av[:, 2 * N * k:2 * N * k + 2 * N:2], T.tab[:, 0:width].indirect(T.nw[:, w:w + N // 16])))
+        width = (TAB1, TAB0)[k] // 16 * 16 if t == 0 else TAB
+        st[t, k, "a"] = run("S", [st[t, k, "nw"], c_av, st.get((t - 1, k, "hh"))] + tabs,
+                            act(T.av[:, 2 * C0[k]:2 * C0[k] + 2 * N:2], T.tab[:, 0:width].indirect(T.nw[:, w:w + N // 16]), F.Identity, bias=col(2)))
 
     def held(t, k):
-        d = 2 * (C * t + N * k)
-        st[t, k, "hh"] = run("V", [st[t, k, "a"]] + hd, scan(T.hh[:, d:d + 2 * N], T.hold[:, :], T.av[:, 2 * N * k:2 * N * k + 2 * N], 0.0, O.add, O.max))
+        d = 2 * (C * t + C0[k])
+        st[t, k, "hh"] = run("V", [st[t, k, "a"]] + hd, scan(T.hh[:, d:d + 2 * N], T.hold[:, :], T.av[:, 2 * C0[k]:2 * C0[k] + 2 * N], 0.0, O.add, O.max))
 
     def offs(t, k):
-        d, o = 2 * (C * t + N * k), 72 * t + 36 * k
-        st[t, k, "off"] = run("V", [st[t, k, "hh"], k_o], ts(T.off[:, o:o + 36], T.hh[:, d + 7:d + 2 * N:8], 4.0, O.mult, col(3), O.add))
+        d, o = 2 * (C * t + C0[k]), 36 * t + 18 * k
+        st[t, k, "off"] = run("V", [st[t, k, "hh"], k_o], ts(T.off[:, o:o + 18], T.hh[:, d + 15:d + 2 * N:16], 2.0, O.mult, col(3), O.add))
 
-    def twin(t, k, q):
-        a, z = 4 * N * k, 4 * (C * t + N * k)
-        st[t, k, "own"] = run(q, [st[t, k, "T"]], (cp if q == "V" else act)(T.own[:, z:z + 4 * N], WT[t][:, a:a + 4 * N]))
+    def twin(t, k, c, q):
+        z = 4 * (C * t + C0[k]) + 2 * N * c
+        st[t, k, "own", c] = run(q, [st[t, k, "T", c], st[t, k, "T", c + 2]], (cp if q == "V" else act)(T.own[:, z:z + 2 * N], half(t, c, C0[k], C0[k] + N)))
 
-    def blend(t, k):
-        a, o, z = 4 * N * k, 72 * t + 36 * k, 4 * (C * t + N * k)
-        st[t, k, "z"] = run("V", [st[t, k, "off"], st[t, k, "own"], st[t, k + 1, "T"]],
-                            tt(T.zt[:, z:z + 4 * N], WT[t][:, a:min(a + 8 * N, 4 * W)].indirect(T.off[:, o:o + 36]), T.own[:, z:z + 4 * N], O.add))
+    def blend(t, k, c):
+        o, z = 36 * t + 18 * k, 4 * (C * t + C0[k])
+        st[t, k, "z", c] = run("V", [st[t, k, "off"], st[t, k, "own", c], st[t, k + 1, "T", c], st[t, k + 1, "T", c + 2]],
+                               tt(T.zt[:, z + c:z + 4 * N:2], half(t, c, C0[k], (C, W)[k]).indirect(T.off[:, o:o + 18]), T.own[:, z + 2 * N * c:z + 2 * N * c + 2 * N], O.add))
 
     def qz(t, k):
-        a = C * t + N * k
-        st[t, k, "qz"] = run("V", [st[t, k, "z"]], quant(T.zq[:, a:a + N], T.zs[:, a:a + N], T.zt[:, 4 * a:4 * a + 4 * N]))
+        a = C * t + C0[k]
+        st[t, k, "qz"] = run("V", [st[t, k, "z", 0], st[t, k, "z", 1]], quant(T.zq[:, a:a + N], T.zs[:, a:a + N], T.zt[:, 4 * a:4 * a + 4 * N]))
 
     def layer(t, k):
-        a = C * t + N * k
+        a = C * t + C0[k]
         for b in range(4):
-            st[t, k, "r", b] = mm(b, N, [("dW", 32), st[t, k, "qz"]], T.wq[:, 128 * b:128 * b + 128], T.wsc[:, 128 * b:128 * b + 128], T.zq[:, a:a + N], T.zs[:, a:a + N])
+            st[t, k, "r", b] = mm(B_W[k][b], N, [("dW", 32), st[t, k, "qz"]], T.wq[:, 128 * b:128 * b + 128], T.wsc[:, 128 * b:128 * b + 128], T.zq[:, a:a + N], T.zs[:, a:a + N])
 
     def xupd(t, k, bs=range(4)):
-        a, e = 4 * N * k, 4 * N * k + 4 * N
+        a, e = 4 * C0[k], 4 * C0[k] + 4 * N
         for b in bs:
-            st[t, k, "x", b] = bank[b] = run("V", [st[t, k, "r", b], st[t, k, "q"]], tt(XT[t + 1][:, a + b:e:4], ps(b, N), XT[t][:, a + b:e:4], O.add))
+            st[t, k, "x", b] = bank[B_W[k][b]] = run("V", [st[t, k, "r", b], st[t, k, "q"]], tt(XT[t + 1][:, a + b:e:4], ps(B_W[k][b], N), XT[t][:, a + b:e:4], O.add))
 
     def results(k):
-        y = mm(4 + k, N, [vq, st[R, k, "q"]], T.vq[:, :], T.vs[:, :], QT[R][:, sl(k)], ST[R][:, sl(k)])
-        st["y", k] = run("S", [y], act(T.ysb[:, sl(k)], ps(4 + k, N)))
+        y = mm(B_S[k], N, [vq, st[R, k, "q"]], T.vq[:, :], T.vs[:, :], QT[R][:, sl(k)], ST[R][:, sl(k)])
+        st["y", k] = run("S", [y], act(T.ysb[:, sl(k)], ps(B_S[k], N)))
 
-    uq = run("V", [("dU", 16)], quant(T.uq[:, :], T.us[:, :], T.ut[:, :]))
-    th += [run("V", [i_16, k_q], ts(T.tha[:, :], T.c16[:, :], col(0), O.is_gt, BIG, O.mult)),
-           run("V", [i_16, k_q], ts(T.thb[:, :], T.c16[:, :], col(0), O.is_le, BIG, O.mult))]
-    u2 += [run("V", [uq, c_off0], cp(T.u2q[:, 0:128].bitcast(dt.uint32), T.uq[:, 0:128].bitcast(dt.uint32).indirect(T.off0[:, 0:8]))),
-           run("S", [uq, c_off0], act(T.u2s[:, 0:128], T.us[:, 0:128].indirect(T.off0[:, 0:8])))]
     qx(0, 0)
     send(0)
     score(0, 0)
-    unpack(0, 0, (0, 1, 2))
     pm = run("V", [pbc, a_mk], tt(T.pm[:, :], T.pbc[:, :], T.mk[:, :], O.mult))
-    hd += [i_r, run("V", [i_4, k_4], ts(T.hold[:, 0:2 * N:2], T.c4[:, :], col(1), O.is_equal, -1024.0, O.mult))]
+    th = [run("V", [i_16, k_q], ts(T.tha[:, :], T.c16[:, :], col(0), O.is_gt, BIG, O.mult)),
+          run("V", [i_16, k_q], ts(T.thb[:, :], T.c16[:, :], col(0), O.is_le, BIG, O.mult))]
     k_s = run("V", [pm], lambda: g.vector.tensor_reduce(col(4), T.pm[:, :], AxisListType.X, O.add))
-    hi = run("S", [k_s, b_9], act(T.hi[:, :], T.b9[:, :], F.Identity, bias=col(4)))
-    lo = run("V", [k_s, b_9], ts(T.lo[:, :], T.b9[:, :], col(4), O.subtract))
-    tabs.append(run("S", [lo], act(T.tab[:, 0:1], T.lo[:, 0:1])))
+    hi = [run("S", [k_s, b_9[0]], act(T.hi[:, 0:TAB1], T.b9[:, 0:TAB1], F.Identity, bias=col(4))),
+          run("S", [k_s, b_9[1]], act(T.hi[:, TAB1:TAB0], T.b9[:, TAB1:TAB0], F.Identity, bias=col(4)))]
+    i_8 = run("S", [i_16, k_8], act(T.c8[:, :], T.c16[:, :], F.Abs, bias=col(1)))
+    equant(0)
+    k_n = run("V", [k_s], ts(col(2), col(4), -0.5, O.mult))
+    equant(2)
+    unpack(0, 0, (0, 2))
     signs(0, 0)
     qx(0, 1)
-    lay(0, 0, (0, 1, 2))
+    k_i = run("V", [st[0, 0, "pa"]], ts(col(5), T.pa[:, 0:1], -128.0, O.mult, 128.0, O.add))
     score(0, 1)
-    unpack(0, 0, (3,))
-    unpack(0, 1)
-    k_i = run("V", [lo, st[0, 0, "pa"]], ts(col(5), T.pa[:, 0:1], 0.0, O.is_equal, T.lo[:, 0:1], O.mult))
     counts(0, 0)
-    count_on(0, 0)
-    tabs.append(run("V", [k_i, hi], scan(T.tab[:, 1:TAB0], T.lo[:, 1:TAB0], T.hi[:, 1:TAB0], col(5), O.max, O.min)))
-    carry[:] = [c_ca, 0]
+    equant(1)
+    tabs = [c_tab, k_n, run("V", [k_i, hi[0]], scan(T.tab[:, 1:TAB1], T.b9[:, 1:TAB1], T.hi[:, 1:TAB1], col(5), O.max, O.min))]
     places(0, 0)
-    carry[:] = [("S", count["S"]), 1]
+    equant(3)
+    lay(0, 0, (0, 2))
     look(0, 0)
-    lay(0, 0, (3,))
-    lay(0, 1)
+    count_on(0, 0)
+    unpack(0, 1, (0, 2))
+    unpack(0, 0, (1, 3))
     signs(0, 1)
+    hd = [run("V", [c_ho, c_four], scan(T.hold[:, 15:2 * N:16], T.four[:, 0:N // 8], T.four[:, 0:N // 8], -108.0, O.add, O.add)),
+          run("V", [i_8], ts(T.hold[:, 0:2 * N:2], T.c8[:, :], 4.0, O.is_equal, -1024.0, O.mult))]
+    k_o = run("V", [k7, k_q], ts(col(3), T.pci[:, 2:3], 18.0, O.mult, col(0), O.add))
     counts(0, 1)
+    tabs.append(run("V", [tabs[-1], hi[1]], scan(T.tab[:, TAB1:TAB0], T.b9[:, TAB1:TAB0], T.hi[:, TAB1:TAB0], T.tab[:, TAB1 - 1:TAB1], O.max, O.min)))
     held(0, 0)
     places(0, 1)
-    look(0, 1)
-    count_on(0, 1)
-    twin(0, 0, "V")
+    lay(0, 1, (0, 2))
+    lay(0, 0, (1, 3))
+    unpack(0, 1, (1, 3))
+    twin(0, 0, 0, "V")
     offs(0, 0)
+    lay(0, 1, (1,))
+    look(0, 1)
+    lay(0, 1, (3,))
+    twin(0, 0, 1, "V")
 
     for t in range(R):
         last = t == R - 1
-        twin(t, 1, "S")
-        unpack(t, 2)
-        lay(t, 2)
-        blend(t, 0)
+        blend(t, 0, 0)
         held(t, 1)
+        blend(t, 0, 1)
+        offs(t, 1)
+        twin(t, 1, 0, "S")
+        twin(t, 1, 1, "S")
+        unpack(t, 2, (0, 2, 1, 3))
+        lay(t, 2, (0, 2, 1, 3))
+        count_on(t, 1)
         qz(t, 0)
         layer(t, 0)
-        offs(t, 1)
         if t == 0:
             for a, e in ((TAB0, TAB0 + 256), (TAB0 + 256, TAB0 + 512), (TAB0 + 512, TAB)):
                 tabs.append(run("S", tabs[-1:], act(T.tab[:, a:e], T.tab[:, a - 256:e - 256])))
@@ -301,57 +318,60 @@ def rank_program(g, core, T, topo):
             ax = run("S", [st[t, 0, "a"], st[t, 1, "a"]], act(T.aof[:, :], T.av[:, 0:2 * C:2]))
             need("Y", [ax])
             g.sync.dma_start(T.ao[:, :], T.aof[0:128:16, :]).then_inc(T.sem.outA, 16)
-            vq = run("V", [("dV", 16)], quant(T.vq[:, :], T.vs[:, :], T.vt[:, :]))
-        blend(t, 1)
-        xupd(t, 0, (0, 1))
+        blend(t, 1, 0)
+        blend(t, 1, 1)
+        xupd(t, 0, (0,))
         qz(t, 1)
-        xupd(t, 0, (2, 3))
+        xupd(t, 0, (1, 2, 3))
         layer(t, 1)
+        if last:
+            vq = run("V", [("dV", 16)], quant(T.vq[:, :], T.vs[:, :], T.vt[:, :]))
         qx(t + 1, 0)
         if last:
             xupd(t, 1)
             qx(t + 1, 1)
             break
-        send(t + 1)
-        score(t + 1, 0)
-        unpack(t + 1, 0, (0, 1, 2))
-        lay(t + 1, 0, (0, 1, 2))
-        unpack(t + 1, 0, (3,))
-        lay(t + 1, 0, (3,))
+        u = t + 1
+        send(u)
+        score(u, 0)
+        unpack(u, 0, (0, 2, 1))
         xupd(t, 1)
-        signs(t + 1, 0)
-        qx(t + 1, 1)
-        score(t + 1, 1)
-        unpack(t + 1, 1)
-        counts(t + 1, 0)
-        places(t + 1, 0)
-        count_on(t + 1, 0)
-        look(t + 1, 0)
-        lay(t + 1, 1)
-        signs(t + 1, 1)
-        twin(t + 1, 0, "V")
-        counts(t + 1, 1)
-        held(t + 1, 0)
-        places(t + 1, 1)
-        look(t + 1, 1)
-        if t + 1 < R - 1:
-            count_on(t + 1, 1)
-        offs(t + 1, 0)
+        signs(u, 0)
+        unpack(u, 0, (3,))
+        lay(u, 0, (0, 2))
+        qx(u, 1)
+        score(u, 1)
+        unpack(u, 1, (0, 2, 1, 3))
+        counts(u, 0)
+        places(u, 0)
+        lay(u, 0, (1,))
+        look(u, 0)
+        count_on(u, 0)
+        lay(u, 0, (3,))
+        twin(u, 0, 0, "V")
+        signs(u, 1)
+        counts(u, 1)
+        held(u, 0)
+        places(u, 1)
+        offs(u, 0)
+        twin(u, 0, 1, "V")
+        lay(u, 1, (0, 2, 1))
+        look(u, 1)
+        lay(u, 1, (3,))
     results(0)
     need("Y", [st[R, 0, "q"]])
     g.sync.dma_start(T.oc[:, 0:4 * N], QT[R][:, 0:N].bitcast(dt.uint8)).then_inc(T.sem.outA, 16)
     need("Y", [st["y", 0]])
     g.sync.dma_start(T.y[:, 0:N], T.ysb[:, 0:N]).then_inc(T.sem.outA, 16)
-    need("S", [st[R, 1, "q"]])
-    g.scalar.dma_start(T.oc[:, 4 * N:4 * C], QT[R][:, N:C].bitcast(dt.uint8)).then_inc(T.sem.outB, 16)
     results(1)
     need("Y", [st[R, 1, "q"]])
+    g.sync.dma_start(T.oc[:, 4 * N:4 * C], QT[R][:, N:C].bitcast(dt.uint8)).then_inc(T.sem.outA, 16)
     for k in range(4):
         g.sync.dma_start(T.osc[4 * k:4 * k + 4, :], ST[R][32 * k:32 * k + 4, 0:C]).then_inc(T.sem.outA, 16)
     need("S", [st["y", 1]])
     g.scalar.dma_start(T.y[:, N:C], T.ysb[:, N:C]).then_inc(T.sem.outB, 16)
     for q in ("V", "S", "T", "G"):
         need("Y", [(q, count[q])])
-    g.sync.wait_ge(T.sem.outA, 16 * 7)
-    g.scalar.wait_ge(T.sem.outB, 16 * 2)
-    g.wait_ge(T.sem.sent, 2 * R * len(topo.engines(core, prev)[::2]))
+    g.sync.wait_ge(T.sem.outA, 16 * 8)
+    g.scalar.wait_ge(T.sem.outB, 16)
+    g.wait_ge(T.sem.sent, 2 * R * len(topo.engines(core, prev)))

@@ -2,51 +2,110 @@ from concourse.mybir import dt, AluOpType as O, AxisListType, ActivationFunction
 
 C, H, R, W = 288, 128, 3, 416
 N = 144
-C0, NB = (0, N, C), (N, N, H)
+NB = (N, N, H)
 TAB, TAB0, TAB1 = 880, 308, 168
+TINY = 2.0 ** -126
 BIG = 2.0 ** 90
+LIFT, SINK = 8, 264
 OPT = {}
 
 F8 = "float8_e4m3fn_x4"
 SCRATCH = {
-    "ut": ("sbuf", [128, 512], "bfloat16"), "vt": ("sbuf", [128, 512], "bfloat16"),
+    "e0": ("sbuf", [128, 8 + 520], "bfloat16"), "vt": ("sbuf", [128, 512], "bfloat16"),
     "uq": ("sbuf", [128, 128], F8), "us": ("sbuf", [128, 128], "uint8"),
     "u2q": ("sbuf", [128, 128], F8), "u2s": ("sbuf", [128, 128], "uint8"),
     "vq": ("sbuf", [128, 128], F8), "vs": ("sbuf", [128, 128], "uint8"),
     "wq": ("sbuf", [128, 512], F8), "wsc": ("sbuf", [128, 512], "uint8"),
-    "two": ("sbuf", [128, 128], "bfloat16"), "four": ("sbuf", [128, 32], "bfloat16"), "e0": ("sbuf", [128, 516], "bfloat16"),
     "eq": ("sbuf", [128, 512], F8), "es": ("sbuf", [128, 512], "uint8"),
     "off0": ("sbuf", [128, 8], "uint16"),
-    "pci": ("sbuf", [128, 4], "int32"), "pcf": ("sbuf", [128, 8], "float32"),
+    "pci": ("sbuf", [128, 4], "int32"), "pcf": ("sbuf", [128, 16], "float32"),
+    "cols": ("sbuf", [128, 128], "bfloat16"), "c16": ("sbuf", [128, N], "bfloat16"), "c8": ("sbuf", [128, N], "bfloat16"),
     "y9": ("sbuf", [128, TAB1], "bfloat16"), "d9": ("sbuf", [128, TAB0], "bfloat16"), "b9": ("sbuf", [128, TAB0], "bfloat16"),
     "hi": ("sbuf", [128, TAB0], "bfloat16"), "tab": ("sbuf", [128, TAB], "bfloat16"),
-    "c16": ("sbuf", [128, N], "bfloat16"), "c8": ("sbuf", [128, N], "bfloat16"),
-    "tha": ("sbuf", [128, N], "bfloat16"), "thb": ("sbuf", [128, N], "bfloat16"),
-    "hold": ("sbuf", [128, 2 * N], "bfloat16"),
     "mk": ("sbuf", [128, 8], "bfloat16"), "pm": ("sbuf", [128, 8], "float32"),
     "pin": ("sbuf", [1, 8], "int32"), "pbc": ("sbuf", [128, 8], "int32"),
     "carry": ("sbuf", [128, 8], "float32"),
-    "pa": ("sbuf", [128, R * C], "bfloat16"), "pb": ("sbuf", [128, 16 + R * C], "bfloat16"),
-    "cnt": ("sbuf", [128, R * C], "bfloat16"),
-    "nw": ("sbuf", [128, R * 20], "uint16"),
-    "av": ("sbuf", [128, 2 * C], "bfloat16"), "hh": ("sbuf", [128, R * 2 * C], "bfloat16"),
-    "off": ("sbuf", [128, R * 36], "uint16"),
-    "zt": ("sbuf", [128, R * 4 * C], "bfloat16"),
-    "own": ("sbuf", [128, R * 4 * C], "bfloat16"),
-    "zq": ("sbuf", [128, R * C], F8), "zs": ("sbuf", [128, R * C], "uint8"),
+    "sg": ("sbuf", [128, C], "bfloat16"), "one": ("sbuf", [128, N], "bfloat16"), "th": ("sbuf", [128, 2 * N], "bfloat16"),
+    "pb": ("sbuf", [128, 16 + R * C], "bfloat16"),
+    "h16": ("sbuf", [128, N], "bfloat16"), "h8": ("sbuf", [128, N], "bfloat16"),
+    "cnt": ("sbuf", [128, C], "bfloat16"), "kept": ("sbuf", [128, C], "bfloat16"), "nw": ("sbuf", [128, 20], "uint16"),
+    "av": ("sbuf", [128, C], "bfloat16"), "hh": ("sbuf", [128, C], "bfloat16"), "off": ("sbuf", [128, 36], "uint16"),
+    "win": ("sbuf", [128, 4 * W], "bfloat16"), "own": ("sbuf", [128, 4 * C], "bfloat16"), "zt": ("sbuf", [128, 4 * C], "bfloat16"),
+    "zq": ("sbuf", [128, C], F8), "zs": ("sbuf", [128, C], "uint8"),
+    "X": ("sbuf", [128, 4 * (R + 1) * C], "bfloat16"),
     "ysb": ("sbuf", [128, C], "float32"), "aof": ("sbuf", [128, C], "float32"),
     "ps": ("psum", [128, 4096], "float32"),
 }
 for _t in range(R + 1):
-    SCRATCH["X%d" % _t] = ("sbuf", [128, 4 * C], "bfloat16")
     SCRATCH["q%d" % _t] = ("sbuf", [128, W], F8)
     SCRATCH["s%d" % _t] = ("sbuf", [128, W], "uint8")
-for _t in range(R):
-    SCRATCH["w%d" % _t] = ("sbuf", [128, 4 * W], "bfloat16")
-SEMAPHORES = ["V", "S", "T", "G", "dXA", "dXB", "dU", "dP", "dW", "dV", "arr0", "arr1", "arr2", "sent", "outA", "outB"]
-B_S = (4, 0)
-B_D = ((5, 7, 6, 4), (1, 3, 2, 5), (1, 3, 2, 0))
-B_W = ((4, 5, 6, 7), (0, 1, 2, 3))
+SEMAPHORES = ["V", "S", "T", "G", "dX0", "dX1", "dU", "dP", "dW", "dV", "sent0", "sent", "outA", "outB", "arr0", "arr1", "arr2"]
+RING = [[("U", 0, 0), ("L", 0, 0)], [("U", 0, 1), ("S", 1, 0), ("U", 2, 1), ("L", 0, 1)], [("U", 0, 2), ("L", 0, 2)], [("S", 0, 0), ("U", 0, 3), ("U", 2, 3), ("L", 0, 3)],
+        [("U", 1, 0), ("L", 1, 0)], [("U", 1, 1), ("U", 2, 0), ("L", 1, 1)], [("U", 1, 2), ("L", 1, 2)], [("U", 1, 3), ("U", 2, 2), ("L", 1, 3)]]
+RING = [[("U", 0, 0), ("S", 1, 0), ("L", 0, 0)], [("U", 0, 1), ("U", 2, 2), ("L", 0, 1)], [("U", 0, 2), ("U", 2, 0), ("L", 0, 2)], [("S", 0, 0), ("U", 0, 3), ("L", 0, 3)],
+        [("U", 1, 0), ("L", 1, 0)], [("U", 1, 1), ("U", 2, 1), ("L", 1, 1)], [("U", 1, 2), ("L", 1, 2)], [("U", 1, 3), ("U", 2, 3), ("L", 1, 3)]]
+START = """ic, e0, off0, pb, ip, i9, diag, mk, k0, k1, uq, pbc, i16, E1, kf, E3, d0, qx A, send A, u2s, u2q, d1, b0, pm, kc, th0, th1, score A, unpack A1,
+    qx B, b1, ks, k15, c8, E0, score B, unpack A0, E2, hi0, signs A0, signs A1, unpack B1, unpack B3, unpack B0, unpack A2, kb, lay A1, h8, signs B0, tab,
+    tally A, unpack A3, ki, h9, lay A0, signs B1, unpack B2, carry A, hi1, places A, cap, lay A3, gtwin A1, tally B, h8end, look A, vlay A2, tab1, places B,
+    lay B1, vlay B3, ko, look B, vtwin A0, held A, vlay B0, lay B2, offs A, twin B1, twin B0, held B, blend A1, blend A0, offs B,
+    unpack C1, unpack C3, unpack C0, unpack C2, lay C1, lay C3, lay C0, lay C2, carry B, more0, qz A, layer A0, layer A3, layer A1, layer A2,
+    blend B1, blend B0, more1, more2, xupd A0, xupd A3, qz B, layer B0, layer B1, layer B2, layer B3, xupd A1, xupd A2"""
+ROUND = """qx A, send A, score A, unpack A0, unpack A2, unpack A1, xupd b0, xupd b1, xupd b2, xupd b3, signs A0, signs A1, unpack A3, lay A0, lay A2, lay A1,
+    qx B, score B, unpack B0, unpack B2, unpack B1, unpack B3, tally A, twin A0, lay A3, gtwin A1, places A, look A, carry A, signs B0, signs B1,
+    lay B0, lay B2, lay B1, lay B3, tally B, held A, places B, offs A, look B, gtwin B1, unpack C0, unpack C2, unpack C1, unpack C3,
+    blend A0, held B, blend A1, offs B, lay C0, lay C2, lay C1, lay C3, gather B0, carry B, qz A, layer A0, layer A3, layer A1, layer A2, blend B1,
+    xupd A0, add B0, add B2, xupd A3, xupd A1, qz B, layer B0, layer B1, layer B2, layer B3, xupd A2"""
+END = "last A, codes A, result A, store A, xupd b0, xupd b1, xupd b2, xupd b3, last B, codes B, result B, store B"
+START = """ic, off0, e0, pb, ip, i9, diag, mk, k0, k1, E0, pbc, uq, d1, i16, E2, d0, kf, u2s, kc, qx A, send A, b1, pm, u2q, b0, unpack A0, c8, E1, k15, ks, th1,
+    score A, th0, qx B, unpack A1, hi0, unpack A2, E3, lay A0, signs A0, score B, signs A1, kb, unpack B1, hi1, unpack B0, h8, tab, lay A1, ki, unpack A3,
+    tally A, ko, signs B0, lay A2, signs B1, h9, places A, cap, carry A, lay A3, unpack B2, tally B, tab1, unpack B3, lay B0, h8end, look A, gtwin A1,
+    places B, vtwin A0, vlay B2, look B, held A, vlay B3, more0, offs A, held B, lay B1, carry B, blend A0, twin B0, twin B1, blend A1, offs B,
+    unpack C3, unpack C1, unpack C0, unpack C2, vlay C1, qz A, lay C3, lay C0, layer A0, lay C2, blend B1, more1, layer A3, layer A2, layer A1, blend B0,
+    xupd A0, xupd A3, qz B, layer B0, layer B1, layer B2, layer B3, xupd A2, xupd A1, more2"""
+ROUND = """qx A, send A, score A, unpack A0, unpack A2, unpack A1, xupd b0, xupd b1, xupd b2, xupd b3, signs A0, lay A0, signs A1, qx B, lay A2, lay A1, unpack A3,
+    tally A, score B, gtwin A0, unpack B0, lay A3, places A, unpack B1, unpack B2, signs B0, unpack B3, signs B1, look A, vlay B1, carry A, gtwin A1, lay B2,
+    tally B, held A, lay B0, lay B3, places B, offs A, look B, unpack C0, gtwin B1, blend A0, unpack C2, unpack C1, unpack C3, lay C0, lay C2, held B,
+    blend A1, lay C3, offs B, vlay C1, qz A, gather B0, blend B1, layer A0, layer A1, carry B, layer A3, layer A2,
+    xupd A0, add B2, add B0, xupd A1, xupd A3, qz B, layer B0, layer B1, layer B2, layer B3, xupd A2, vq"""
+LAST = """qx A, send A, score A, unpack A0, unpack A2, unpack A1, xupd b0, xupd b1, xupd b2, xupd b3, signs A0, lay A0, signs A1, qx B, lay A2, lay A1, unpack A3,
+    tally A, score B, gtwin A0, unpack B0, lay A3, places A, unpack B1, unpack B2, signs B0, unpack B3, signs B1, look A, vlay B1, carry A, gtwin A1, lay B2,
+    tally B, held A, lay B0, lay B3, places B, offs A, look B, blend A0, gtwin B1, unpack C1, twin B0, unpack C3, unpack C2, unpack C0, held B,
+    lay C1, blend A1, lay C3, lay C0, lay C2, offs B, ao A, qz A, blend B1, layer A3, layer A0, layer A1, blend B0, layer A2,
+    xupd A3, xupd A0, qz B, layer B0, layer B1, layer B2, layer B3, xupd A1, xupd A2"""
+ORDER = [(t, step.strip()) for t, s in enumerate((START, ROUND, LAST, END)) for step in s.split(",")]
+TALLY, SPLIT, LD, APART = True, "B", ("u", 0, 1), (0,)
+PACK = "0u1z340t0w0x0i0s111w331r0y0h20240r2o0f2p2303101406012k0g282j2r250p2b0z0b2c07290k2y2f2a2t122h2w2d0m21162e18000q2i0c0d0l132mG021p2u2q222g2x1aV192s0n1q1cV15V1b2nG0o1x171y090e2l311s2z08321f301g1e1dV260a0j1h1k1j351i0405382737361l1o1n4e1m393c4k4i3b4x3a4w4u4l4m3o4f1t4p3nV4y3p4j4c523qV1u3i4z4rV48514n504sG3s4o3t3l4q3r3uV4d4a573f495455534t563m3g3x3w3y3z4b4g3k3h41423j433e403d5a4h5958455b4644476h5e5d6n6l5f705c6y6z6o5s6p5r6i5q6s7175736f6m5t726b746q6wG6u6r5o6t5m5xV5u6d5w6g5j795y766c78776xG5k62615z605p5i6j6e5n665l6563647c5h5g7a6k7b7d67686a7k697e7h7i7m7f7g7l7j7n"
+
+
+def steps(tally, split):
+    c = "ip ic i16 i9 pbc e0 off0 k0 k1 kf diag mk E1 uq E3 u2q u2s k15 d0 d1 b0 b1 pm E0 ks kb E2 hi0 hi1 tab tab1 kc c8 h8 h9 h8end ko".split()
+    o = [(0, x) for x in c + (["th0", "th1", "pb"] if tally else ["one", "h16"])]
+    for t in range(R):
+        s = []
+        for b in "AB":
+            s += ["qx " + b] + ["send A"] * (b == "A") + ["score " + b]
+            s += ["signs %s0" % b, "signs %s1" % b, "tally " + b] if tally else ["sign " + b, "counts " + b, "keep " + b]
+            s += ["ki", "cap"] * ((t, b) == (0, "A")) + ["places " + b] + ["carry " + b] * ((t, b) != (R - 1, "B")) + ["look " + b, "held " + b, "offs " + b]
+            s += ["unpack %s%d" % (b, j) for j in range(4)] + ["lay %s%d" % (b, j) for j in range(4)] + ["twin %s%d" % (b, j) for j in range(b in split, 2)]
+        s += (["more0", "more1", "more2"], ["vq"], ["ao A"])[t]
+        s += [x + " C%d" % j for j in range(4) for x in ("unpack", "lay")]
+        for b in "AB":
+            s += (["gather %s0" % b, "add %s0" % b, "add %s2" % b] if b in split else ["blend %s0" % b]) + ["blend %s1" % b, "qz " + b]
+            s += ["layer %s%d" % (b, j) for j in range(4)] + ["xupd %s%d" % (b, j) for j in range(4)]
+        o += [(t, x) for x in s]
+    return o + [(R, x) for x in ("last A", "codes A", "result A", "last B", "codes B", "result B")]
+
+
+def order(code, tally, split):
+    al, can, out, i = "0123456789abcdefghijklmnopqrstuwxyz", sorted(steps(tally, split)), [], 0
+    while i < len(code):
+        t, s = can[al.index(code[i]) * 35 + al.index(code[i + 1])]
+        i += 2
+        if code[i:i + 1] in ("V", "G"):
+            s = code[i].lower() + s
+            i += 1
+        out.append((t, s))
+    return out
 
 
 def rank_program(g, core, T, topo):
@@ -59,8 +118,12 @@ def rank_program(g, core, T, topo):
     eng = {"V": g.vector, "S": g.scalar, "T": g.tensor, "G": g, "Y": g.sync}
     count = {"V": 0, "S": 0, "T": 0, "G": 0}
     known = {}
+    cur = [None]
+    tallied = OPT.get("tally", TALLY)
 
     def need(q, toks):
+        if "trace" in OPT:
+            OPT["trace"].append((cur[0], q, toks, count.get(q, 0) + 1))
         best = {}
         for tk in toks:
             if tk is None:
@@ -100,278 +163,249 @@ def rank_program(g, core, T, topo):
     def fill(ap, c):
         return lambda: g.vector.memset(ap, c)
 
-    def iota(out, pattern, base):
-        return lambda: g.iota(out, pattern, base, 0, allow_small_or_imprecise_dtypes=True)
+    def iota(out, pattern, step=0, base=0):
+        return lambda: g.iota(out, pattern, base, step, allow_small_or_imprecise_dtypes=True)
 
-    def ps(bank, n):
+    def ps(bank, n=N):
         return T.ps[:, 512 * bank:512 * bank + n]
 
-    bank = {}
+    def mm(bank, n, deps, lq, ls, rq, rs):
+        return run("T", deps, lambda: g.tensor.matmul_mx(ps(bank, n), lq, ls, rq, rs, True, True))
 
-    def mm(bk, n, deps, lq, ls, rq, rs):
-        return run("T", deps + [bank.get(bk)], lambda: g.tensor.matmul_mx(ps(bk, n), lq, ls, rq, rs, True, True))
+    def sl(k, n=N):
+        return slice(n * k, n * k + n)
+
+    def xs(t, k, b=0, step=1):
+        return T.X[:, 4 * (C * t + N * k) + b:4 * (C * t + N * k + N):step]
 
     QT = [T["q%d" % t] for t in range(R + 1)]
     ST = [T["s%d" % t] for t in range(R + 1)]
-    XT = [T["X%d" % t] for t in range(R + 1)]
-    WT = [T["w%d" % t] for t in range(R)]
+    st = {"dU": ("dU", 16), "dP": ("dP", 16), "dV": ("dV", 16)}
+    col = lambda k: T.pcf[:, k:k + 1]
+    pint = lambda a, b: T.pci[:, a:b]
+    lanes = len(topo.engines(core, prev))
 
+    if "u" not in OPT.get("LD", LD):
+        g.scalar.dma_start(T.e0[:, 0:8], T.u[:, 0:8]).then_inc(T.sem.dU, 16)
     g.scalar.dma_start(T.pin[0:1, :], T.p[:, :]).then_inc(T.sem.dP, 16)
-    g.sync.dma_start(T.ut[:, 0:8], T.u[:, 0:8]).then_inc(T.sem.dU, 16)
-    g.sync.dma_start(T.X0[:, 0:4 * N], T.x[:, 0:4 * N]).then_inc(T.sem.dXA, 16)
-    g.sync.dma_start(T.X0[:, 4 * N:4 * C], T.x[:, 4 * N:4 * C]).then_inc(T.sem.dXB, 16)
-    need("Y", [("dXA", 16)])
+    for k in OPT.get("LD", LD):
+        if k == "u":
+            g.sync.dma_start(T.e0[:, 0:8], T.u[:, 0:8]).then_inc(T.sem.dU, 16)
+        else:
+            g.sync.dma_start(xs(0, k), T.x[:, sl(k, 4 * N)]).then_inc(T.sem["dX%d" % k], 16)
     g.sync.dma_start(T.wq[:, :].bitcast(dt.uint8), T.wc[:, :]).then_inc(T.sem.dW, 16)
     g.sync.dma_start(T.wsc[:, :], T.ws[:, :]).then_inc(T.sem.dW, 16)
+    need("Y", [("sent0", (2 - (0 in OPT.get("apart", APART))) * lanes)])
     g.sync.dma_start(T.vt[:, :], T.v[:, :]).then_inc(T.sem.dV, 16)
 
-    col = lambda k: T.pcf[:, k:k + 1]
-    c_two = run("V", [], fill(T.two[:, :], 2.0))
-    c_ut = run("V", [], fill(T.ut[:, 8:512], 0.0))
-    c_off0 = run("V", [], fill(T.off0[:, :], 0))
-    c_e0 = run("V", [], fill(T.e0[:, :], 0.0))
-    i_p = run("G", [], lambda: g.iota(T.pci[:, 0:1], [[0, 1]], 0, 1))
-    i_9 = run("G", [], iota(T.y9[:, :], [[-4, TAB1 // 28], [9, 28]], 0))
-    a_mk = run("G", [c_two], lambda: g.affine_select(T.mk[:, :], T.two[:, 0:8], [[-16, 8]], O.is_ge, 0.0, 0, 1))
-    pbc = run("G", [("dP", 16)], lambda: g.partition_broadcast(T.pbc[:, :], T.pin[0:1, :], 128))
-    i_16 = run("G", [], iota(T.c16[:, :], [[0, N // 16], [1, 16]], 74))
-    a_e0 = run("G", [c_two, c_e0], lambda: g.affine_select(T.e0[:, 3:515:4], T.two[:, :], [[-1, 128]], O.is_equal, 0.0, 0, 1))
-    d_9 = [run("S", [i_9], act(T.d9[:, 0:TAB1], T.y9[:, :], F.Abs)),
-           run("S", [i_9], act(T.d9[:, TAB1:TAB0], T.y9[:, 0:TAB0 - TAB1], F.Abs, bias=-4.0 * (TAB1 // 28)))]
-    b_9 = [run("S", [d_9[0]], act(T.b9[:, 0:TAB1], T.d9[:, 0:TAB1], F.Abs, bias=-128.0)),
-           run("S", [d_9[1]], act(T.b9[:, TAB1:TAB0], T.d9[:, TAB1:TAB0], F.Abs, bias=-128.0))]
-    k15 = run("V", [i_p], ts(T.pci[:, 1:2], T.pci[:, 0:1], 15, O.bitwise_and))
-    k7 = run("V", [i_p], ts(T.pci[:, 2:3], T.pci[:, 0:1], 1, O.logical_shift_right, 7, O.bitwise_and))
-    c_pb = run("V", [], fill(T.pb[:, 0:16], 0.0))
-    c_ca = run("V", [], fill(T.carry[:, 0:1], 0.0))
-    c_tab = run("V", [], fill(T.tab[:, 0:1], 128.0))
-    k_q = run("V", [k15], ts(col(0), T.pci[:, 1:2], 74.0, O.add))
-    k_8 = run("V", [k7], ts(col(1), T.pci[:, 2:3], -1.0, O.mult, -78.0, O.add))
-    uq = run("V", [("dU", 16), c_ut], quant(T.uq[:, :], T.us[:, :], T.ut[:, :]))
-    c_ho = run("V", [], fill(T.hold[:, 1:2 * N:2], 9.0))
-    c_four = run("V", [], fill(T.four[:, :], 4.0))
-    c_av = run("V", [], fill(T.av[:, 1:2 * C:2], -256.0))
-    u2 = [run("V", [uq, c_off0], cp(T.u2q[:, 0:128].bitcast(dt.uint32), T.uq[:, 0:2].bitcast(dt.uint32).indirect(T.off0[:, 0:8]))),
-          run("S", [uq, c_off0], act(T.u2s[:, 0:128], T.us[:, 0:2].indirect(T.off0[:, 0:8])))]
-    E = {}
+    ONCE = {
+        "ip": ("G", [], iota(pint(0, 2), [[-SINK // 8, 2]], 1)),
+        "ic": ("G", [], iota(T.cols[:, :], [[1, 128]], -1)),
+        "i16": ("G", [], iota(T.c16[:, :], [[0, N // 16], [1, 16]])),
+        "i9": ("G", [], iota(T.y9[:, :], [[-4, TAB1 // 28], [9, 28]])),
+        "pbc": ("G", ["dP"], lambda: g.partition_broadcast(T.pbc[:, :], T.pin[0:1, :], 128)),
+        "e0": ("V", [], fill(T.e0[:, 8:528], 0.0)),
+        "off0": ("V", [], fill(T.off0[:, :], 0)),
+        "k0": ("V", ["ip"], ts(pint(2, 3), pint(0, 1), 15, O.bitwise_and)),
+        "k1": ("V", ["ip"], ts(pint(3, 4), pint(0, 1), 1, O.logical_shift_right, 7, O.bitwise_and)),
+        "kf": ("V", ["k0", "k1"], cp(T.pcf[:, 0:3], pint(1, 4))),
+        "k15": ("S", ["kf"], act(col(3), col(1), F.Identity, bias=2.0 * (SINK - LIFT - 63))),
+        "kc": ("S", ["kf"], act(col(4), col(2), F.Identity, scale=-1.0, bias=-3.0)),
+        "ko": ("S", ["k15"], act(col(5), col(2), F.Identity, scale=18.0, bias=col(3))),
+        "diag": ("V", ["ic", "e0"], ts(T.e0[:, 11:523:4], T.cols[:, :], 0.0, O.is_equal, 2.0 ** -6, O.mult)),
+        "mk": ("V", ["ic"], ts(T.mk[:, :], T.cols[:, 0:128:16], 0.0, O.is_le, 2.0, O.mult)),
+        "c8": ("S", ["kc", "i16"], act(T.c8[:, :], T.c16[:, :], F.Abs, bias=col(4))),
+        "h8": ("V", ["c8"], ts(T.h8[:, :], T.c8[:, :], 4.0, O.is_equal, -1024.0, O.mult)),
+        "h9": ("S", ["h8"], act(T.h8[:, :], T.h8[:, :], F.Identity, bias=9.0)),
+        "h8end": ("V", ["h9", "ic"], ts(T.h8[:, 7:N:8], T.cols[:, 0:N // 8], col(0), O.add, 8.0, O.mult)),
+        "uq": ("V", ["dU", "diag"], quant(T.uq[:, :], T.us[:, :], T.e0[:, 0:512])),
+        "u2q": ("V", ["uq", "off0"], cp(T.u2q[:, :].bitcast(dt.uint32), T.uq[:, 0:2].bitcast(dt.uint32).indirect(T.off0[:, :]))),
+        "u2s": ("S", ["uq", "off0"], act(T.u2s[:, :], T.us[:, 0:2].indirect(T.off0[:, :]))),
+        "d0": ("S", ["i9"], act(T.d9[:, 0:TAB1], T.y9[:, :], F.Abs)),
+        "d1": ("S", ["i9"], act(T.d9[:, TAB1:TAB0], T.y9[:, 0:TAB0 - TAB1], F.Abs, bias=-4.0 * (TAB1 // 28))),
+        "b0": ("S", ["d0"], act(T.b9[:, 0:TAB1], T.d9[:, 0:TAB1], F.Abs, bias=-128.0)),
+        "b1": ("S", ["d1"], act(T.b9[:, TAB1:TAB0], T.d9[:, TAB1:TAB0], F.Abs, bias=-128.0)),
+        "pm": ("V", ["pbc", "mk"], tt(T.pm[:, :], T.pbc[:, :], T.mk[:, :], O.mult)),
+        "ks": ("V", ["pm"], lambda: g.vector.tensor_reduce(col(7), T.pm[:, :], AxisListType.X, O.add)),
+        "kb": ("S", ["ks"], act(col(8), col(7), F.Identity, scale=-0.5, bias=float(LIFT))),
+        "hi0": ("S", ["ks", "b0"], act(T.hi[:, 0:TAB1], T.b9[:, 0:TAB1], F.Identity, bias=col(7))),
+        "hi1": ("S", ["ks", "b1"], act(T.hi[:, TAB1:TAB0], T.b9[:, TAB1:TAB0], F.Identity, bias=col(7))),
+        "tab": ("V", ["hi0"], scan(T.tab[:, 0:TAB1], T.b9[:, 0:TAB1], T.hi[:, 0:TAB1], 128.0, O.max, O.min)),
+        "tab1": ("V", ["hi1", "tab"], scan(T.tab[:, TAB1:TAB0], T.b9[:, TAB1:TAB0], T.hi[:, TAB1:TAB0], T.tab[:, TAB1 - 1:TAB1], O.max, O.min)),
+        "ki": ("V", [(0, 0, "p", 0)], ts(col(9), T.sg[:, 0:1], -9.0 if tallied else -4.5, O.mult, 128.0 if tallied else 123.5, O.add)),
+        "cap": ("V", ["ki", "tab"], ts(T.tab[:, 1:15], T.tab[:, 1:15], col(9), O.min)),
+        "vq": ("V", ["dV"], quant(T.vq[:, :], T.vs[:, :], T.vt[:, :])),
+        "th0": ("V", ["kf", "i16"], ts(T.th[:, sl(0)], T.c16[:, :], col(1), O.is_gt, BIG, O.mult)),
+        "th1": ("V", ["kf", "i16"], ts(T.th[:, sl(1)], T.c16[:, :], col(1), O.is_le, BIG, O.mult)),
+        "pb": ("V", [], fill(T.pb[:, 0:16], 0.0)),
+        "one": ("V", [], fill(T.one[:, :], 1.0)),
+        "h16": ("V", ["kf", "i16"], ts(T.h16[:, :], T.c16[:, :], col(1), O.is_equal, 1024.0, O.mult)),
+    }
+    for b in range(4):
+        ONCE["E%d" % b] = ("V", ["diag"], quant(T.eq[:, sl(b, 128)], T.es[:, sl(b, 128)], T.e0[:, 11 - b:523 - b]))
+    for i in range(3):
+        a = TAB0 + 256 * i
+        e = min(a + 256, TAB)
+        ONCE["more%d" % i] = ("S", ["more%d" % (i - 1) if i else "tab1"], act(T.tab[:, a:e], T.tab[:, a - 256:e - 256]))
 
-    def equant(b):
-        E[b] = run("V", [a_e0], quant(T.eq[:, 128 * b:128 * b + 128], T.es[:, 128 * b:128 * b + 128], T.e0[:, 3 - b:515 - b]))
+    user = {u: (j, ring[i - 1], int(i == 0)) for j, ring in enumerate(OPT.get("RING", RING)) for i, u in enumerate(ring)}
 
-    st = {}
-    carry = [c_ca, 0]
+    def bank(kind, k, b=0, t=1):
+        return user[("U", 1, 2) if (kind, k, t) == ("S", 1, 0) else (kind, k, b)][0]
 
-    def sl(k):
-        return slice(C0[k], C0[k] + NB[k])
+    def freed(t, kind, k, b=0):
+        _, (kd, kk, bb), back = user[kind, k, b]
+        if t == 0 and (kind, k) == ("S", 1):
+            return None
+        if t == 0 and (kind, k, b) == ("U", 1, 2):
+            return st[0, 1, "p", 1]
+        if t == 0 and (kd, kk) == ("S", 1):
+            kd, kk, bb = user["S", 1, 0][1]
+        if t < back:
+            return None
+        return st[t - back, kk, {"S": "p", "L": "x", "U": "T"}[kd], 1 if kd == "S" else bb]
+
+    def cs(k):
+        return slice(N * k, N * k + NB[k])
 
     def qx(t, k):
-        a = C0[k]
-        deps = [("dXB" if k else "dXA", 16)] if t == 0 else [st[t - 1, k, "x", b] for b in range(4)]
-        st[t, k, "q"] = run("V", deps, quant(QT[t][:, sl(k)], ST[t][:, sl(k)], XT[t][:, 4 * a:4 * a + 4 * N]))
+        deps = [("dX%d" % k, 16)] if t == 0 else [st[t - 1, k, "x", b] for b in range(4)]
+        st[t, k, "q"] = run("V", deps, quant(QT[t][:, sl(k)], ST[t][:, sl(k)], xs(t, k)))
 
-    def send(t):
+    def send(t, k):
         need("G", [st[t, 0, "q"]])
         rid, pid = topo.addr(prev, core)
-        m = topo.mask(core, prev)
-        g.remote_dma(QT[t][:, C:W].bitcast(dt.uint8), QT[t][:, 0:H].bitcast(dt.uint8), T.sem["arr%d" % t], T.sem.sent, pid, rid, m)
-        g.remote_dma(ST[t][:, C:W], ST[t][:, 0:H], T.sem["arr%d" % t], T.sem.sent, pid, rid, m)
+        es = topo.engines(core, prev)
+        apart = t in OPT.get("apart", APART)
+        m = [sum(1 << e for e in (es[i::2] if apart == 2 else es[i * lanes // 2:(i + 1) * lanes // 2] if apart else es)) for i in range(2)]
+        sent = T.sem["sent" if t else "sent0"]
+        g.remote_dma(QT[t][:, C:W].bitcast(dt.uint8), QT[t][:, 0:H].bitcast(dt.uint8), T.sem["arr%d" % t], sent, pid, rid, m[0])
+        g.remote_dma(ST[t][:, C:W], ST[t][:, 0:H], T.sem["arr%d" % t], sent, pid, rid, m[1])
+        st[t, 2, "q"] = ("arr%d" % t, (2 - apart) * len(topo.engines(nxt, core)))
 
     def score(t, k):
-        st[t, k, "S"] = mm(B_S[k], N, [st[t, k, "q"]] + u2, T.u2q[:, :], T.u2s[:, :], QT[t][:, sl(k)], ST[t][:, sl(k)])
+        st[t, k, "S"] = mm(bank("S", k, 0, t), N, [st[t, k, "q"], st["u2q"], st["u2s"], freed(t, "S", k)], T.u2q[:, :], T.u2s[:, :], QT[t][:, sl(k)], ST[t][:, sl(k)])
 
-    def unpack(t, k, bs):
-        dep = st[t, k, "q"] if k < 2 else ("arr%d" % t, 2 * len(topo.engines(nxt, core)))
-        for b in bs:
-            st[t, k, "D", b] = mm(B_D[k][b], NB[k], [E[b], dep], T.eq[:, 128 * b:128 * b + 128], T.es[:, 128 * b:128 * b + 128], QT[t][:, sl(k)], ST[t][:, sl(k)])
-
-    def half(t, c, lo, hi, i=0, step=1):
-        return WT[t][:, 2 * (W * c + lo) + i:2 * (W * c + hi):step]
-
-    def lay(t, k, bs):
-        for b in bs:
-            st[t, k, "T", b] = bank[B_D[k][b]] = run("S", [st[t, k, "D", b]], act(half(t, b % 2, C0[k], C0[k] + NB[k], b // 2, 2), ps(B_D[k][b], NB[k]), scale=2.0 ** -7))
-
-    def signs(t, k):
-        a = C * t + C0[k]
-        x = st[t, k, "S"]
-        st[t, k, "pa"] = run("V", [x] + th, tt(T.pa[:, a:a + N], ps(B_S[k], N), T.tha[:, :], O.is_gt))
-        st[t, k, "pb"] = bank[B_S[k]] = run("V", [x] + th, tt(T.pb[:, a + 16:a + 16 + N], ps(B_S[k], N), T.thb[:, :], O.is_gt))
+    def sign(t, k):
+        st[t, k, "p", 0] = st[t, k, "p", 1] = run("S", [st[t, k, "S"]], act(T.sg[:, sl(k)], ps(bank("S", k, 0, t)), F.Sign, bias=-TINY))
 
     def counts(t, k):
-        a = C * t + C0[k]
-        st[t, k, "cnt"] = run("V", [st[t, k, "pb"], c_pb], scan(T.cnt[:, a:a + N], T.pa[:, a:a + N], T.pb[:, a:a + N], 0.0, O.add, O.add))
+        st[t, k, "cnt"] = run("V", [st[t, k, "p", 1], st["one"]], scan(T.cnt[:, sl(k)], T.sg[:, sl(k)], T.one[:, :], 0.0, O.add, O.add))
+
+    def keep(t, k):
+        st[t, k, "kept"] = run("V", [st[t, k, "cnt"], st["h16"]], scan(T.kept[:, sl(k)], T.h16[:, :], T.cnt[:, sl(k)], 0.0, O.add, O.min))
+
+    def signs(t, k, i):
+        a = C * t + N * k + 16
+        st[t, k, "p", i] = run("V", [st[t, k, "S"], st["th%d" % i]] + [st[t, k, "p", 0] and None for _ in range(i)],
+                               tt(T.pb[:, a:a + N] if i else T.sg[:, sl(k)], ps(bank("S", k, 0, t)), T.th[:, sl(i)], O.is_gt))
+
+    def tally(t, k):
+        a, i = C * t + N * k, 2 * t + k - 1
+        st[t, k, "cnt"] = st[t, k, "kept"] = run("V", [st[t, k, "p", 1], st[i // 2, i % 2, "p", 1] if a else st["pb"]],
+                                                 scan(T.kept[:, sl(k)], T.sg[:, sl(k)], T.pb[:, a:a + N], 0.0, O.add, O.add))
+
+    def before(t, k):
+        i = 2 * t + k
+        return (T.carry[:, i:i + 1], st["carry", i]) if i else (0.0, None)
 
     def places(t, k):
-        a, w, cc = C * t + C0[k], 20 * t + 10 * k, carry[1]
-        st[t, k, "nw"] = run("V", [st[t, k, "cnt"], carry[0]], ts(T.nw[:, w:w + N // 16], T.cnt[:, a + 15:a + N:16], T.carry[:, cc:cc + 1], O.add))
+        c, tk = before(t, k)
+        st[t, k, "nw"] = run("V", [st[t, k, "kept"], tk], ts(T.nw[:, 10 * k:10 * k + N // 16], T.kept[:, N * k + 15:N * k + N:16], 1.0 if tallied else 0.5, O.mult, c, O.add))
 
-    def count_on(t, k):
-        a, cc = C * t + C0[k], 2 * t + k
-        if (t, k) != (R - 1, 1):
-            carry[0] = run("S", [st[t, k, "cnt"], carry[0]], act(T.carry[:, cc + 1:cc + 2], T.cnt[:, a + N - 1:a + N], F.Identity, bias=T.carry[:, cc:cc + 1]))
-            carry[1] = cc + 1
+    def carry(t, k):
+        c, tk = before(t, k)
+        i = 2 * t + k + 1
+        st["carry", i] = run("S", [st[t, k, "cnt"], tk], act(T.carry[:, i:i + 1], (T.kept if tallied else T.cnt)[:, N * k + N - 1:N * k + N], F.Identity, bias=c, scale=1.0 if tallied else 0.5))
 
     def look(t, k):
-        w = 20 * t + 10 * k
-        width = (TAB1, TAB0)[k] // 16 * 16 if t == 0 else TAB
-        st[t, k, "a"] = run("S", [st[t, k, "nw"], c_av, st.get((t - 1, k, "hh"))] + tabs,
-                            act(T.av[:, 2 * C0[k]:2 * C0[k] + 2 * N:2], T.tab[:, 0:width].indirect(T.nw[:, w:w + N // 16]), F.Identity, bias=col(2)))
+        width = TAB if t else TAB0 if k else TAB1
+        st[t, k, "a"] = run("S", [st[t, k, "nw"], st["kb"], st["cap"], st["more2" if t else "tab1" if k else "tab"]],
+                            act(T.av[:, sl(k)], T.tab[:, 0:width].indirect(T.nw[:, 10 * k:10 * k + N // 16]), F.Identity, bias=col(8)))
 
     def held(t, k):
-        d = 2 * (C * t + C0[k])
-        st[t, k, "hh"] = run("V", [st[t, k, "a"]] + hd, scan(T.hh[:, d:d + 2 * N], T.hold[:, :], T.av[:, 2 * C0[k]:2 * C0[k] + 2 * N], 0.0, O.add, O.max))
+        st[t, k, "hh"] = run("V", [st[t, k, "a"], st["h8end"]], scan(T.hh[:, sl(k)], T.av[:, sl(k)], T.h8[:, :], -1024.0, O.max, O.add))
 
     def offs(t, k):
-        d, o = 2 * (C * t + C0[k]), 36 * t + 18 * k
-        st[t, k, "off"] = run("V", [st[t, k, "hh"], k_o], ts(T.off[:, o:o + 18], T.hh[:, d + 15:d + 2 * N:16], 2.0, O.mult, col(3), O.add))
+        st[t, k, "off"] = run("V", [st[t, k, "hh"], st["ko"]], ts(T.off[:, sl(k, N // 8)], T.hh[:, N * k + 7:N * k + N:8], 2.0, O.mult, col(5), O.add))
 
-    def twin(t, k, c, q):
-        z = 4 * (C * t + C0[k]) + 2 * N * c
-        st[t, k, "own", c] = run(q, [st[t, k, "T", c], st[t, k, "T", c + 2]], (cp if q == "V" else act)(T.own[:, z:z + 2 * N], half(t, c, C0[k], C0[k] + N)))
+    def unpack(t, k, b):
+        st[t, k, "D", b] = mm(bank("U", k, b), NB[k], [st["E%d" % b], st[t, k, "q"], freed(t, "U", k, b)], T.eq[:, sl(b, 128)], T.es[:, sl(b, 128)], QT[t][:, cs(k)], ST[t][:, cs(k)])
+
+    def half(c, lo, hi, i=0, step=1):
+        return T.win[:, 2 * (W * c + lo) + i:2 * (W * c + hi):step]
+
+    def lay(t, k, b, q="S"):
+        old = [st[t - 1, j, "z", b] for j in range(max(k - 1, 0), min(k, 1) + 1)] if t else []
+        st[t, k, "T", b] = run(q, [st[t, k, "D", b]] + old, (act if q == "S" else cp)(half(b % 2, N * k, N * k + NB[k], b // 2, 2), ps(bank("U", k, b), NB[k])))
+
+    def twin(t, k, c, q="S"):
+        out, src = T.own[:, sl(2 * k + c, 2 * N)], half(c, N * k, N * k + N)
+        call = cp(out, src) if q == "V" else act(out, src) if q == "S" else lambda: g.affine_select(out, src, [[0, 2 * N]], O.is_ge, 0.0, 0, 0)
+        st[t, k, "own", c] = run(q, [st[t, k, "T", c], st[t, k, "T", c + 2]], call)
+
+    def far(t, k, c):
+        return half(c, N * k, N * k + N + H).indirect(T.off[:, sl(k, N // 8)]), [st[t, k, "off"]] + [st[t, j, "T", b] for j in (k, k + 1) for b in (c, c + 2)]
+
+    def zs(k, b=0, step=1):
+        return T.zt[:, 4 * N * k + b:4 * N * k + 4 * N:step]
 
     def blend(t, k, c):
-        o, z = 36 * t + 18 * k, 4 * (C * t + C0[k])
-        st[t, k, "z", c] = run("V", [st[t, k, "off"], st[t, k, "own", c], st[t, k + 1, "T", c], st[t, k + 1, "T", c + 2]],
-                               tt(T.zt[:, z + c:z + 4 * N:2], half(t, c, C0[k], (C, W)[k]).indirect(T.off[:, o:o + 18]), T.own[:, z + 2 * N * c:z + 2 * N * c + 2 * N], O.add))
+        f, deps = far(t, k, c)
+        st[t, k, "z", c] = st[t, k, "z", c + 2] = run("V", deps + [st[t, k, "own", c]], tt(zs(k, c, 2), f, T.own[:, sl(2 * k + c, 2 * N)], O.add))
+
+    def gather(t, k, c):
+        f, deps = far(t, k, c)
+        st[t, k, "F", c] = run("S", deps, act(T.own[:, sl(2 * k + c, 2 * N)], f))
+
+    def add(t, k, b):
+        o = 2 * N * (2 * k + b % 2)
+        st[t, k, "z", b] = run("V", [st[t, k, "F", b % 2]], tt(zs(k, b, 4), ps(bank("U", k, b)), T.own[:, o + b // 2:o + 2 * N:2], O.add))
 
     def qz(t, k):
-        a = C * t + C0[k]
-        st[t, k, "qz"] = run("V", [st[t, k, "z", 0], st[t, k, "z", 1]], quant(T.zq[:, a:a + N], T.zs[:, a:a + N], T.zt[:, 4 * a:4 * a + 4 * N]))
+        st[t, k, "qz"] = run("V", [st[t, k, "z", b] for b in range(4)], quant(T.zq[:, sl(k)], T.zs[:, sl(k)], zs(k)))
 
-    def layer(t, k):
-        a = C * t + C0[k]
-        for b in range(4):
-            st[t, k, "r", b] = mm(B_W[k][b], N, [("dW", 32), st[t, k, "qz"]], T.wq[:, 128 * b:128 * b + 128], T.wsc[:, 128 * b:128 * b + 128], T.zq[:, a:a + N], T.zs[:, a:a + N])
+    def layer(t, k, b):
+        st[t, k, "r", b] = mm(bank("L", k, b), N, [("dW", 32), st[t, k, "qz"], freed(t, "L", k, b)], T.wq[:, sl(b, 128)], T.wsc[:, sl(b, 128)], T.zq[:, sl(k)], T.zs[:, sl(k)])
 
-    def xupd(t, k, bs=range(4)):
-        a, e = 4 * C0[k], 4 * C0[k] + 4 * N
-        for b in bs:
-            st[t, k, "x", b] = bank[B_W[k][b]] = run("V", [st[t, k, "r", b], st[t, k, "q"]], tt(XT[t + 1][:, a + b:e:4], ps(B_W[k][b], N), XT[t][:, a + b:e:4], O.add))
+    def xupd(t, k, b):
+        st[t, k, "x", b] = run("V", [st[t, k, "r", b], st[t, k, "q"]], tt(xs(t + 1, k, b, 4), ps(bank("L", k, b)), xs(t, k, b, 4), O.add))
 
-    def results(k):
-        y = mm(B_S[k], N, [vq, st[R, k, "q"]], T.vq[:, :], T.vs[:, :], QT[R][:, sl(k)], ST[R][:, sl(k)])
-        st["y", k] = run("S", [y], act(T.ysb[:, sl(k)], ps(B_S[k], N)))
+    def ao(t, k):
+        a = run("S", [st[t, 0, "a"], st[t, 1, "a"]], act(T.aof[:, :], T.av[:, :], F.Identity, bias=-float(LIFT)))
+        need("Y", [a])
+        g.sync.dma_start(T.ao[:, :], T.aof[0:128:16, :]).then_inc(T.sem.outA, 16)
 
-    qx(0, 0)
-    send(0)
-    score(0, 0)
-    pm = run("V", [pbc, a_mk], tt(T.pm[:, :], T.pbc[:, :], T.mk[:, :], O.mult))
-    th = [run("V", [i_16, k_q], ts(T.tha[:, :], T.c16[:, :], col(0), O.is_gt, BIG, O.mult)),
-          run("V", [i_16, k_q], ts(T.thb[:, :], T.c16[:, :], col(0), O.is_le, BIG, O.mult))]
-    k_s = run("V", [pm], lambda: g.vector.tensor_reduce(col(4), T.pm[:, :], AxisListType.X, O.add))
-    hi = [run("S", [k_s, b_9[0]], act(T.hi[:, 0:TAB1], T.b9[:, 0:TAB1], F.Identity, bias=col(4))),
-          run("S", [k_s, b_9[1]], act(T.hi[:, TAB1:TAB0], T.b9[:, TAB1:TAB0], F.Identity, bias=col(4)))]
-    i_8 = run("S", [i_16, k_8], act(T.c8[:, :], T.c16[:, :], F.Abs, bias=col(1)))
-    equant(0)
-    k_n = run("V", [k_s], ts(col(2), col(4), -0.5, O.mult))
-    equant(2)
-    unpack(0, 0, (0, 2))
-    signs(0, 0)
-    qx(0, 1)
-    k_i = run("V", [st[0, 0, "pa"]], ts(col(5), T.pa[:, 0:1], -128.0, O.mult, 128.0, O.add))
-    score(0, 1)
-    counts(0, 0)
-    equant(1)
-    tabs = [c_tab, k_n, run("V", [k_i, hi[0]], scan(T.tab[:, 1:TAB1], T.b9[:, 1:TAB1], T.hi[:, 1:TAB1], col(5), O.max, O.min))]
-    places(0, 0)
-    equant(3)
-    lay(0, 0, (0, 2))
-    look(0, 0)
-    count_on(0, 0)
-    unpack(0, 1, (0, 2))
-    unpack(0, 0, (1, 3))
-    signs(0, 1)
-    hd = [run("V", [c_ho, c_four], scan(T.hold[:, 15:2 * N:16], T.four[:, 0:N // 8], T.four[:, 0:N // 8], -108.0, O.add, O.add)),
-          run("V", [i_8], ts(T.hold[:, 0:2 * N:2], T.c8[:, :], 4.0, O.is_equal, -1024.0, O.mult))]
-    k_o = run("V", [k7, k_q], ts(col(3), T.pci[:, 2:3], 18.0, O.mult, col(0), O.add))
-    counts(0, 1)
-    tabs.append(run("V", [tabs[-1], hi[1]], scan(T.tab[:, TAB1:TAB0], T.b9[:, TAB1:TAB0], T.hi[:, TAB1:TAB0], T.tab[:, TAB1 - 1:TAB1], O.max, O.min)))
-    held(0, 0)
-    places(0, 1)
-    lay(0, 1, (0, 2))
-    lay(0, 0, (1, 3))
-    unpack(0, 1, (1, 3))
-    twin(0, 0, 0, "V")
-    offs(0, 0)
-    lay(0, 1, (1,))
-    look(0, 1)
-    lay(0, 1, (3,))
-    twin(0, 0, 1, "V")
+    def codes(t, k):
+        need("Y", [st[R, j, "q"] for j in range(k + 1)])
+        g.sync.dma_start(T.oc[:, sl(k, 4 * N)], QT[R][:, sl(k)].bitcast(dt.uint8)).then_inc(T.sem.outA, 16)
+        if k:
+            for i in range(4):
+                g.sync.dma_start(T.osc[4 * i:4 * i + 4, :], ST[R][32 * i:32 * i + 4, 0:C]).then_inc(T.sem.outA, 16)
 
-    for t in range(R):
-        last = t == R - 1
-        blend(t, 0, 0)
-        held(t, 1)
-        blend(t, 0, 1)
-        offs(t, 1)
-        twin(t, 1, 0, "S")
-        twin(t, 1, 1, "S")
-        unpack(t, 2, (0, 2, 1, 3))
-        lay(t, 2, (0, 2, 1, 3))
-        count_on(t, 1)
-        qz(t, 0)
-        layer(t, 0)
-        if t == 0:
-            for a, e in ((TAB0, TAB0 + 256), (TAB0 + 256, TAB0 + 512), (TAB0 + 512, TAB)):
-                tabs.append(run("S", tabs[-1:], act(T.tab[:, a:e], T.tab[:, a - 256:e - 256])))
-        if last:
-            ax = run("S", [st[t, 0, "a"], st[t, 1, "a"]], act(T.aof[:, :], T.av[:, 0:2 * C:2]))
-            need("Y", [ax])
-            g.sync.dma_start(T.ao[:, :], T.aof[0:128:16, :]).then_inc(T.sem.outA, 16)
-        blend(t, 1, 0)
-        blend(t, 1, 1)
-        xupd(t, 0, (0,))
-        qz(t, 1)
-        xupd(t, 0, (1, 2, 3))
-        layer(t, 1)
-        if last:
-            vq = run("V", [("dV", 16)], quant(T.vq[:, :], T.vs[:, :], T.vt[:, :]))
-        qx(t + 1, 0)
-        if last:
-            xupd(t, 1)
-            qx(t + 1, 1)
-            break
-        u = t + 1
-        send(u)
-        score(u, 0)
-        unpack(u, 0, (0, 2, 1))
-        xupd(t, 1)
-        signs(u, 0)
-        unpack(u, 0, (3,))
-        lay(u, 0, (0, 2))
-        qx(u, 1)
-        score(u, 1)
-        unpack(u, 1, (0, 2, 1, 3))
-        counts(u, 0)
-        places(u, 0)
-        lay(u, 0, (1,))
-        look(u, 0)
-        count_on(u, 0)
-        lay(u, 0, (3,))
-        twin(u, 0, 0, "V")
-        signs(u, 1)
-        counts(u, 1)
-        held(u, 0)
-        places(u, 1)
-        offs(u, 0)
-        twin(u, 0, 1, "V")
-        lay(u, 1, (0, 2, 1))
-        look(u, 1)
-        lay(u, 1, (3,))
-    results(0)
-    need("Y", [st[R, 0, "q"]])
-    g.sync.dma_start(T.oc[:, 0:4 * N], QT[R][:, 0:N].bitcast(dt.uint8)).then_inc(T.sem.outA, 16)
-    need("Y", [st["y", 0]])
-    g.sync.dma_start(T.y[:, 0:N], T.ysb[:, 0:N]).then_inc(T.sem.outA, 16)
-    results(1)
-    need("Y", [st[R, 1, "q"]])
-    g.sync.dma_start(T.oc[:, 4 * N:4 * C], QT[R][:, N:C].bitcast(dt.uint8)).then_inc(T.sem.outA, 16)
-    for k in range(4):
-        g.sync.dma_start(T.osc[4 * k:4 * k + 4, :], ST[R][32 * k:32 * k + 4, 0:C]).then_inc(T.sem.outA, 16)
-    need("S", [st["y", 1]])
-    g.scalar.dma_start(T.y[:, N:C], T.ysb[:, N:C]).then_inc(T.sem.outB, 16)
+    def result(t, k):
+        y = mm(bank("L", k, 0), N, [st["vq"], st[R, k, "q"]], T.vq[:, :], T.vs[:, :], QT[R][:, sl(k)], ST[R][:, sl(k)])
+        y = run("S", [y], act(T.ysb[:, sl(k)], ps(bank("L", k, 0))))
+        st["y", k] = y
+
+    def store(t, k):
+        need("YS"[k], [st["y", k]])
+        eng["YS"[k]].dma_start(T.y[:, sl(k)], T.ysb[:, sl(k)]).then_inc(T.sem.outB, 16)
+
+    STEP = {"qx": qx, "send": send, "score": score, "sign": sign, "counts": counts, "keep": keep, "signs": signs, "tally": tally, "places": places, "carry": carry,
+            "look": look, "held": held, "offs": offs, "unpack": unpack, "lay": lay, "vlay": lambda t, k, b: lay(t, k, b, "V"), "blend": blend, "gather": gather,
+            "add": add, "twin": twin, "vtwin": lambda t, k, c: twin(t, k, c, "V"), "gtwin": lambda t, k, c: twin(t, k, c, "G"),
+            "qz": qz, "layer": layer, "xupd": xupd, "ao": ao, "last": qx, "codes": codes, "result": result, "store": store}
+    for t, step in OPT.get("ALL") or ORDER:
+        cur[0] = (t, step)
+        if step in ONCE:
+            q, deps, call = ONCE[step]
+            st[step] = run(q, [st[d] for d in deps], call)
+        else:
+            name, arg = step.split()
+            STEP[name](t - arg[0].islower(), "ABC".index(arg[0].upper()), *[int(c) for c in arg[1:]])
     for q in ("V", "S", "T", "G"):
         need("Y", [(q, count[q])])
-    g.sync.wait_ge(T.sem.outA, 16 * 8)
-    g.scalar.wait_ge(T.sem.outB, 16)
-    g.wait_ge(T.sem.sent, 2 * R * len(topo.engines(core, prev)))
+    g.sync.wait_ge(T.sem.outA, 16 * 7)
+    g.scalar.wait_ge(T.sem.outB, 32)
+    g.wait_ge(T.sem.sent, 2 * (R - 1) * lanes)

from concourse.mybir import dt, AluOpType as O, AxisListType, ActivationFunctionType as F

C, H, R, W = 288, 128, 3, 416
N = 144
NB = (N, N, H)
TAB, TAB0, TAB1 = 880, 308, 168
TINY = 2.0 ** -126
BIG = 2.0 ** 90
LIFT, SINK = 8, 264
OPT = {}

F8 = "float8_e4m3fn_x4"
SCRATCH = {
    "e0": ("sbuf", [128, 8 + 520], "bfloat16"), "vt": ("sbuf", [128, 512], "bfloat16"),
    "uq": ("sbuf", [128, 128], F8), "us": ("sbuf", [128, 128], "uint8"),
    "u2q": ("sbuf", [128, 128], F8), "u2s": ("sbuf", [128, 128], "uint8"),
    "vq": ("sbuf", [128, 128], F8), "vs": ("sbuf", [128, 128], "uint8"),
    "wq": ("sbuf", [128, 512], F8), "wsc": ("sbuf", [128, 512], "uint8"),
    "eq": ("sbuf", [128, 512], F8), "es": ("sbuf", [128, 512], "uint8"),
    "off0": ("sbuf", [128, 8], "uint16"),
    "pci": ("sbuf", [128, 4], "int32"), "pcf": ("sbuf", [128, 16], "float32"),
    "cols": ("sbuf", [128, 128], "bfloat16"), "c16": ("sbuf", [128, N], "bfloat16"), "c8": ("sbuf", [128, N], "bfloat16"),
    "y9": ("sbuf", [128, TAB1], "bfloat16"), "d9": ("sbuf", [128, TAB0], "bfloat16"), "b9": ("sbuf", [128, TAB0], "bfloat16"),
    "hi": ("sbuf", [128, TAB0], "bfloat16"), "tab": ("sbuf", [128, TAB], "bfloat16"),
    "mk": ("sbuf", [128, 8], "bfloat16"), "pm": ("sbuf", [128, 8], "float32"),
    "pin": ("sbuf", [1, 8], "int32"), "pbc": ("sbuf", [128, 8], "int32"),
    "carry": ("sbuf", [128, 8], "float32"),
    "sg": ("sbuf", [128, C], "bfloat16"), "one": ("sbuf", [128, N], "bfloat16"), "th": ("sbuf", [128, 2 * N], "bfloat16"),
    "pb": ("sbuf", [128, 16 + R * C], "bfloat16"),
    "h16": ("sbuf", [128, N], "bfloat16"), "h8": ("sbuf", [128, N], "bfloat16"),
    "cnt": ("sbuf", [128, C], "bfloat16"), "kept": ("sbuf", [128, C], "bfloat16"), "nw": ("sbuf", [128, 20], "uint16"),
    "av": ("sbuf", [128, C], "bfloat16"), "hh": ("sbuf", [128, C], "bfloat16"), "off": ("sbuf", [128, 36], "uint16"),
    "win": ("sbuf", [128, 4 * W], "bfloat16"), "own": ("sbuf", [128, 4 * C], "bfloat16"), "zt": ("sbuf", [128, 4 * C], "bfloat16"),
    "zq": ("sbuf", [128, C], F8), "zs": ("sbuf", [128, C], "uint8"),
    "X": ("sbuf", [128, 4 * (R + 1) * C], "bfloat16"),
    "ysb": ("sbuf", [128, C], "float32"), "aof": ("sbuf", [128, C], "float32"),
    "ps": ("psum", [128, 4096], "float32"),
}
for _t in range(R + 1):
    SCRATCH["q%d" % _t] = ("sbuf", [128, W], F8)
    SCRATCH["s%d" % _t] = ("sbuf", [128, W], "uint8")
SEMAPHORES = ["V", "S", "T", "G", "dX0", "dX1", "dU", "dP", "dW", "dV", "sent0", "sent", "outA", "outB", "arr0", "arr1", "arr2"]
RING = [[("U", 0, 0), ("L", 0, 0)], [("U", 0, 1), ("S", 1, 0), ("U", 2, 1), ("L", 0, 1)], [("U", 0, 2), ("L", 0, 2)], [("S", 0, 0), ("U", 0, 3), ("U", 2, 3), ("L", 0, 3)],
        [("U", 1, 0), ("L", 1, 0)], [("U", 1, 1), ("U", 2, 0), ("L", 1, 1)], [("U", 1, 2), ("L", 1, 2)], [("U", 1, 3), ("U", 2, 2), ("L", 1, 3)]]
RING = [[("U", 0, 0), ("S", 1, 0), ("L", 0, 0)], [("U", 0, 1), ("U", 2, 2), ("L", 0, 1)], [("U", 0, 2), ("U", 2, 0), ("L", 0, 2)], [("S", 0, 0), ("U", 0, 3), ("L", 0, 3)],
        [("U", 1, 0), ("L", 1, 0)], [("U", 1, 1), ("U", 2, 1), ("L", 1, 1)], [("U", 1, 2), ("L", 1, 2)], [("U", 1, 3), ("U", 2, 3), ("L", 1, 3)]]
START = """ic, e0, off0, pb, ip, i9, diag, mk, k0, k1, uq, pbc, i16, E1, kf, E3, d0, qx A, send A, u2s, u2q, d1, b0, pm, kc, th0, th1, score A, unpack A1,
    qx B, b1, ks, k15, c8, E0, score B, unpack A0, E2, hi0, signs A0, signs A1, unpack B1, unpack B3, unpack B0, unpack A2, kb, lay A1, h8, signs B0, tab,
    tally A, unpack A3, ki, h9, lay A0, signs B1, unpack B2, carry A, hi1, places A, cap, lay A3, gtwin A1, tally B, h8end, look A, vlay A2, tab1, places B,
    lay B1, vlay B3, ko, look B, vtwin A0, held A, vlay B0, lay B2, offs A, twin B1, twin B0, held B, blend A1, blend A0, offs B,
    unpack C1, unpack C3, unpack C0, unpack C2, lay C1, lay C3, lay C0, lay C2, carry B, more0, qz A, layer A0, layer A3, layer A1, layer A2,
    blend B1, blend B0, more1, more2, xupd A0, xupd A3, qz B, layer B0, layer B1, layer B2, layer B3, xupd A1, xupd A2"""
ROUND = """qx A, send A, score A, unpack A0, unpack A2, unpack A1, xupd b0, xupd b1, xupd b2, xupd b3, signs A0, signs A1, unpack A3, lay A0, lay A2, lay A1,
    qx B, score B, unpack B0, unpack B2, unpack B1, unpack B3, tally A, twin A0, lay A3, gtwin A1, places A, look A, carry A, signs B0, signs B1,
    lay B0, lay B2, lay B1, lay B3, tally B, held A, places B, offs A, look B, gtwin B1, unpack C0, unpack C2, unpack C1, unpack C3,
    blend A0, held B, blend A1, offs B, lay C0, lay C2, lay C1, lay C3, gather B0, carry B, qz A, layer A0, layer A3, layer A1, layer A2, blend B1,
    xupd A0, add B0, add B2, xupd A3, xupd A1, qz B, layer B0, layer B1, layer B2, layer B3, xupd A2"""
END = "last A, codes A, result A, store A, xupd b0, xupd b1, xupd b2, xupd b3, last B, codes B, result B, store B"
START = """ic, off0, e0, pb, ip, i9, diag, mk, k0, k1, E0, pbc, uq, d1, i16, E2, d0, kf, u2s, kc, qx A, send A, b1, pm, u2q, b0, unpack A0, c8, E1, k15, ks, th1,
    score A, th0, qx B, unpack A1, hi0, unpack A2, E3, lay A0, signs A0, score B, signs A1, kb, unpack B1, hi1, unpack B0, h8, tab, lay A1, ki, unpack A3,
    tally A, ko, signs B0, lay A2, signs B1, h9, places A, cap, carry A, lay A3, unpack B2, tally B, tab1, unpack B3, lay B0, h8end, look A, gtwin A1,
    places B, vtwin A0, vlay B2, look B, held A, vlay B3, more0, offs A, held B, lay B1, carry B, blend A0, twin B0, twin B1, blend A1, offs B,
    unpack C3, unpack C1, unpack C0, unpack C2, vlay C1, qz A, lay C3, lay C0, layer A0, lay C2, blend B1, more1, layer A3, layer A2, layer A1, blend B0,
    xupd A0, xupd A3, qz B, layer B0, layer B1, layer B2, layer B3, xupd A2, xupd A1, more2"""
ROUND = """qx A, send A, score A, unpack A0, unpack A2, unpack A1, xupd b0, xupd b1, xupd b2, xupd b3, signs A0, lay A0, signs A1, qx B, lay A2, lay A1, unpack A3,
    tally A, score B, gtwin A0, unpack B0, lay A3, places A, unpack B1, unpack B2, signs B0, unpack B3, signs B1, look A, vlay B1, carry A, gtwin A1, lay B2,
    tally B, held A, lay B0, lay B3, places B, offs A, look B, unpack C0, gtwin B1, blend A0, unpack C2, unpack C1, unpack C3, lay C0, lay C2, held B,
    blend A1, lay C3, offs B, vlay C1, qz A, gather B0, blend B1, layer A0, layer A1, carry B, layer A3, layer A2,
    xupd A0, add B2, add B0, xupd A1, xupd A3, qz B, layer B0, layer B1, layer B2, layer B3, xupd A2, vq"""
LAST = """qx A, send A, score A, unpack A0, unpack A2, unpack A1, xupd b0, xupd b1, xupd b2, xupd b3, signs A0, lay A0, signs A1, qx B, lay A2, lay A1, unpack A3,
    tally A, score B, gtwin A0, unpack B0, lay A3, places A, unpack B1, unpack B2, signs B0, unpack B3, signs B1, look A, vlay B1, carry A, gtwin A1, lay B2,
    tally B, held A, lay B0, lay B3, places B, offs A, look B, blend A0, gtwin B1, unpack C1, twin B0, unpack C3, unpack C2, unpack C0, held B,
    lay C1, blend A1, lay C3, lay C0, lay C2, offs B, ao A, qz A, blend B1, layer A3, layer A0, layer A1, blend B0, layer A2,
    xupd A3, xupd A0, qz B, layer B0, layer B1, layer B2, layer B3, xupd A1, xupd A2"""
ORDER = [(t, step.strip()) for t, s in enumerate((START, ROUND, LAST, END)) for step in s.split(",")]
TALLY, SPLIT, LD, APART = True, "B", ("u", 0, 1), (0,)
PACK = "0u1z340t0w0x0i0s111w331r0y0h20240r2o0f2p2303101406012k0g282j2r250p2b0z0b2c07290k2y2f2a2t122h2w2d0m21162e18000q2i0c0d0l132mG021p2u2q222g2x1aV192s0n1q1cV15V1b2nG0o1x171y090e2l311s2z08321f301g1e1dV260a0j1h1k1j351i0405382737361l1o1n4e1m393c4k4i3b4x3a4w4u4l4m3o4f1t4p3nV4y3p4j4c523qV1u3i4z4rV48514n504sG3s4o3t3l4q3r3uV4d4a573f495455534t563m3g3x3w3y3z4b4g3k3h41423j433e403d5a4h5958455b4644476h5e5d6n6l5f705c6y6z6o5s6p5r6i5q6s7175736f6m5t726b746q6wG6u6r5o6t5m5xV5u6d5w6g5j795y766c78776xG5k62615z605p5i6j6e5n665l6563647c5h5g7a6k7b7d67686a7k697e7h7i7m7f7g7l7j7n"


def steps(tally, split):
    c = "ip ic i16 i9 pbc e0 off0 k0 k1 kf diag mk E1 uq E3 u2q u2s k15 d0 d1 b0 b1 pm E0 ks kb E2 hi0 hi1 tab tab1 kc c8 h8 h9 h8end ko".split()
    o = [(0, x) for x in c + (["th0", "th1", "pb"] if tally else ["one", "h16"])]
    for t in range(R):
        s = []
        for b in "AB":
            s += ["qx " + b] + ["send A"] * (b == "A") + ["score " + b]
            s += ["signs %s0" % b, "signs %s1" % b, "tally " + b] if tally else ["sign " + b, "counts " + b, "keep " + b]
            s += ["ki", "cap"] * ((t, b) == (0, "A")) + ["places " + b] + ["carry " + b] * ((t, b) != (R - 1, "B")) + ["look " + b, "held " + b, "offs " + b]
            s += ["unpack %s%d" % (b, j) for j in range(4)] + ["lay %s%d" % (b, j) for j in range(4)] + ["twin %s%d" % (b, j) for j in range(b in split, 2)]
        s += (["more0", "more1", "more2"], ["vq"], ["ao A"])[t]
        s += [x + " C%d" % j for j in range(4) for x in ("unpack", "lay")]
        for b in "AB":
            s += (["gather %s0" % b, "add %s0" % b, "add %s2" % b] if b in split else ["blend %s0" % b]) + ["blend %s1" % b, "qz " + b]
            s += ["layer %s%d" % (b, j) for j in range(4)] + ["xupd %s%d" % (b, j) for j in range(4)]
        o += [(t, x) for x in s]
    return o + [(R, x) for x in ("last A", "codes A", "result A", "last B", "codes B", "result B")]


def order(code, tally, split):
    al, can, out, i = "0123456789abcdefghijklmnopqrstuwxyz", sorted(steps(tally, split)), [], 0
    while i < len(code):
        t, s = can[al.index(code[i]) * 35 + al.index(code[i + 1])]
        i += 2
        if code[i:i + 1] in ("V", "G"):
            s = code[i].lower() + s
            i += 1
        out.append((t, s))
    return out


def rank_program(g, core, T, topo):
    rank = T.rank_of(core)
    if rank is None:
        return
    n_ranks = len(T.cores)
    prev = T.cores[(rank - 1) % n_ranks]
    nxt = T.cores[(rank + 1) % n_ranks]
    eng = {"V": g.vector, "S": g.scalar, "T": g.tensor, "G": g, "Y": g.sync}
    count = {"V": 0, "S": 0, "T": 0, "G": 0}
    known = {}
    cur = [None]
    tallied = OPT.get("tally", TALLY)

    def need(q, toks):
        if "trace" in OPT:
            OPT["trace"].append((cur[0], q, toks, count.get(q, 0) + 1))
        best = {}
        for tk in toks:
            if tk is None:
                continue
            best[tk[0]] = max(best.get(tk[0], 0), tk[1])
        for s in best:
            if best[s] > known.get((q, s), 0):
                eng[q].wait_ge(T.sem[s], best[s])
                known[(q, s)] = best[s]

    def run(q, deps, call):
        need(q, deps)
        call().then_inc(T.sem[q], 1)
        count[q] += 1
        return (q, count[q])

    def ts(out, in0, s1, op0, s2=None, op1=None):
        if op1 is None:
            return lambda: g.vector.tensor_scalar(out, in0, s1, None, op0)
        return lambda: g.vector.tensor_scalar(out, in0, s1, s2, op0, op1)

    def tt(out, a, b, op):
        return lambda: g.vector.tensor_tensor(out, a, b, op)

    def cp(out, in_):
        return lambda: g.vector.tensor_copy(out, in_)

    def scan(out, d0, d1, init, op0, op1):
        return lambda: g.vector.tensor_tensor_scan(out, d0, d1, init, op0, op1)

    def act(out, in_, f=F.Copy, **kw):
        return lambda: g.scalar.activation(out, in_, f, **kw)

    def quant(q, s, t):
        return lambda: g.vector.quantize_mx(q, s, t)

    def fill(ap, c):
        return lambda: g.vector.memset(ap, c)

    def iota(out, pattern, step=0, base=0):
        return lambda: g.iota(out, pattern, base, step, allow_small_or_imprecise_dtypes=True)

    def ps(bank, n=N):
        return T.ps[:, 512 * bank:512 * bank + n]

    def mm(bank, n, deps, lq, ls, rq, rs):
        return run("T", deps, lambda: g.tensor.matmul_mx(ps(bank, n), lq, ls, rq, rs, True, True))

    def sl(k, n=N):
        return slice(n * k, n * k + n)

    def xs(t, k, b=0, step=1):
        return T.X[:, 4 * (C * t + N * k) + b:4 * (C * t + N * k + N):step]

    QT = [T["q%d" % t] for t in range(R + 1)]
    ST = [T["s%d" % t] for t in range(R + 1)]
    st = {"dU": ("dU", 16), "dP": ("dP", 16), "dV": ("dV", 16)}
    col = lambda k: T.pcf[:, k:k + 1]
    pint = lambda a, b: T.pci[:, a:b]
    lanes = len(topo.engines(core, prev))

    if "u" not in OPT.get("LD", LD):
        g.scalar.dma_start(T.e0[:, 0:8], T.u[:, 0:8]).then_inc(T.sem.dU, 16)
    g.scalar.dma_start(T.pin[0:1, :], T.p[:, :]).then_inc(T.sem.dP, 16)
    for k in OPT.get("LD", LD):
        if k == "u":
            g.sync.dma_start(T.e0[:, 0:8], T.u[:, 0:8]).then_inc(T.sem.dU, 16)
        else:
            g.sync.dma_start(xs(0, k), T.x[:, sl(k, 4 * N)]).then_inc(T.sem["dX%d" % k], 16)
    g.sync.dma_start(T.wq[:, :].bitcast(dt.uint8), T.wc[:, :]).then_inc(T.sem.dW, 16)
    g.sync.dma_start(T.wsc[:, :], T.ws[:, :]).then_inc(T.sem.dW, 16)
    need("Y", [("sent0", (2 - (0 in OPT.get("apart", APART))) * lanes)])
    g.sync.dma_start(T.vt[:, :], T.v[:, :]).then_inc(T.sem.dV, 16)

    ONCE = {
        "ip": ("G", [], iota(pint(0, 2), [[-SINK // 8, 2]], 1)),
        "ic": ("G", [], iota(T.cols[:, :], [[1, 128]], -1)),
        "i16": ("G", [], iota(T.c16[:, :], [[0, N // 16], [1, 16]])),
        "i9": ("G", [], iota(T.y9[:, :], [[-4, TAB1 // 28], [9, 28]])),
        "pbc": ("G", ["dP"], lambda: g.partition_broadcast(T.pbc[:, :], T.pin[0:1, :], 128)),
        "e0": ("V", [], fill(T.e0[:, 8:528], 0.0)),
        "off0": ("V", [], fill(T.off0[:, :], 0)),
        "k0": ("V", ["ip"], ts(pint(2, 3), pint(0, 1), 15, O.bitwise_and)),
        "k1": ("V", ["ip"], ts(pint(3, 4), pint(0, 1), 1, O.logical_shift_right, 7, O.bitwise_and)),
        "kf": ("V", ["k0", "k1"], cp(T.pcf[:, 0:3], pint(1, 4))),
        "k15": ("S", ["kf"], act(col(3), col(1), F.Identity, bias=2.0 * (SINK - LIFT - 63))),
        "kc": ("S", ["kf"], act(col(4), col(2), F.Identity, scale=-1.0, bias=-3.0)),
        "ko": ("S", ["k15"], act(col(5), col(2), F.Identity, scale=18.0, bias=col(3))),
        "diag": ("V", ["ic", "e0"], ts(T.e0[:, 11:523:4], T.cols[:, :], 0.0, O.is_equal, 2.0 ** -6, O.mult)),
        "mk": ("V", ["ic"], ts(T.mk[:, :], T.cols[:, 0:128:16], 0.0, O.is_le, 2.0, O.mult)),
        "c8": ("S", ["kc", "i16"], act(T.c8[:, :], T.c16[:, :], F.Abs, bias=col(4))),
        "h8": ("V", ["c8"], ts(T.h8[:, :], T.c8[:, :], 4.0, O.is_equal, -1024.0, O.mult)),
        "h9": ("S", ["h8"], act(T.h8[:, :], T.h8[:, :], F.Identity, bias=9.0)),
        "h8end": ("V", ["h9", "ic"], ts(T.h8[:, 7:N:8], T.cols[:, 0:N // 8], col(0), O.add, 8.0, O.mult)),
        "uq": ("V", ["dU", "diag"], quant(T.uq[:, :], T.us[:, :], T.e0[:, 0:512])),
        "u2q": ("V", ["uq", "off0"], cp(T.u2q[:, :].bitcast(dt.uint32), T.uq[:, 0:2].bitcast(dt.uint32).indirect(T.off0[:, :]))),
        "u2s": ("S", ["uq", "off0"], act(T.u2s[:, :], T.us[:, 0:2].indirect(T.off0[:, :]))),
        "d0": ("S", ["i9"], act(T.d9[:, 0:TAB1], T.y9[:, :], F.Abs)),
        "d1": ("S", ["i9"], act(T.d9[:, TAB1:TAB0], T.y9[:, 0:TAB0 - TAB1], F.Abs, bias=-4.0 * (TAB1 // 28))),
        "b0": ("S", ["d0"], act(T.b9[:, 0:TAB1], T.d9[:, 0:TAB1], F.Abs, bias=-128.0)),
        "b1": ("S", ["d1"], act(T.b9[:, TAB1:TAB0], T.d9[:, TAB1:TAB0], F.Abs, bias=-128.0)),
        "pm": ("V", ["pbc", "mk"], tt(T.pm[:, :], T.pbc[:, :], T.mk[:, :], O.mult)),
        "ks": ("V", ["pm"], lambda: g.vector.tensor_reduce(col(7), T.pm[:, :], AxisListType.X, O.add)),
        "kb": ("S", ["ks"], act(col(8), col(7), F.Identity, scale=-0.5, bias=float(LIFT))),
        "hi0": ("S", ["ks", "b0"], act(T.hi[:, 0:TAB1], T.b9[:, 0:TAB1], F.Identity, bias=col(7))),
        "hi1": ("S", ["ks", "b1"], act(T.hi[:, TAB1:TAB0], T.b9[:, TAB1:TAB0], F.Identity, bias=col(7))),
        "tab": ("V", ["hi0"], scan(T.tab[:, 0:TAB1], T.b9[:, 0:TAB1], T.hi[:, 0:TAB1], 128.0, O.max, O.min)),
        "tab1": ("V", ["hi1", "tab"], scan(T.tab[:, TAB1:TAB0], T.b9[:, TAB1:TAB0], T.hi[:, TAB1:TAB0], T.tab[:, TAB1 - 1:TAB1], O.max, O.min)),
        "ki": ("V", [(0, 0, "p", 0)], ts(col(9), T.sg[:, 0:1], -9.0 if tallied else -4.5, O.mult, 128.0 if tallied else 123.5, O.add)),
        "cap": ("V", ["ki", "tab"], ts(T.tab[:, 1:15], T.tab[:, 1:15], col(9), O.min)),
        "vq": ("V", ["dV"], quant(T.vq[:, :], T.vs[:, :], T.vt[:, :])),
        "th0": ("V", ["kf", "i16"], ts(T.th[:, sl(0)], T.c16[:, :], col(1), O.is_gt, BIG, O.mult)),
        "th1": ("V", ["kf", "i16"], ts(T.th[:, sl(1)], T.c16[:, :], col(1), O.is_le, BIG, O.mult)),
        "pb": ("V", [], fill(T.pb[:, 0:16], 0.0)),
        "one": ("V", [], fill(T.one[:, :], 1.0)),
        "h16": ("V", ["kf", "i16"], ts(T.h16[:, :], T.c16[:, :], col(1), O.is_equal, 1024.0, O.mult)),
    }
    for b in range(4):
        ONCE["E%d" % b] = ("V", ["diag"], quant(T.eq[:, sl(b, 128)], T.es[:, sl(b, 128)], T.e0[:, 11 - b:523 - b]))
    for i in range(3):
        a = TAB0 + 256 * i
        e = min(a + 256, TAB)
        ONCE["more%d" % i] = ("S", ["more%d" % (i - 1) if i else "tab1"], act(T.tab[:, a:e], T.tab[:, a - 256:e - 256]))

    user = {u: (j, ring[i - 1], int(i == 0)) for j, ring in enumerate(OPT.get("RING", RING)) for i, u in enumerate(ring)}

    def bank(kind, k, b=0, t=1):
        return user[("U", 1, 2) if (kind, k, t) == ("S", 1, 0) else (kind, k, b)][0]

    def freed(t, kind, k, b=0):
        _, (kd, kk, bb), back = user[kind, k, b]
        if t == 0 and (kind, k) == ("S", 1):
            return None
        if t == 0 and (kind, k, b) == ("U", 1, 2):
            return st[0, 1, "p", 1]
        if t == 0 and (kd, kk) == ("S", 1):
            kd, kk, bb = user["S", 1, 0][1]
        if t < back:
            return None
        return st[t - back, kk, {"S": "p", "L": "x", "U": "T"}[kd], 1 if kd == "S" else bb]

    def cs(k):
        return slice(N * k, N * k + NB[k])

    def qx(t, k):
        deps = [("dX%d" % k, 16)] if t == 0 else [st[t - 1, k, "x", b] for b in range(4)]
        st[t, k, "q"] = run("V", deps, quant(QT[t][:, sl(k)], ST[t][:, sl(k)], xs(t, k)))

    def send(t, k):
        need("G", [st[t, 0, "q"]])
        rid, pid = topo.addr(prev, core)
        es = topo.engines(core, prev)
        apart = t in OPT.get("apart", APART)
        m = [sum(1 << e for e in (es[i::2] if apart == 2 else es[i * lanes // 2:(i + 1) * lanes // 2] if apart else es)) for i in range(2)]
        sent = T.sem["sent" if t else "sent0"]
        g.remote_dma(QT[t][:, C:W].bitcast(dt.uint8), QT[t][:, 0:H].bitcast(dt.uint8), T.sem["arr%d" % t], sent, pid, rid, m[0])
        g.remote_dma(ST[t][:, C:W], ST[t][:, 0:H], T.sem["arr%d" % t], sent, pid, rid, m[1])
        st[t, 2, "q"] = ("arr%d" % t, (2 - apart) * len(topo.engines(nxt, core)))

    def score(t, k):
        st[t, k, "S"] = mm(bank("S", k, 0, t), N, [st[t, k, "q"], st["u2q"], st["u2s"], freed(t, "S", k)], T.u2q[:, :], T.u2s[:, :], QT[t][:, sl(k)], ST[t][:, sl(k)])

    def sign(t, k):
        st[t, k, "p", 0] = st[t, k, "p", 1] = run("S", [st[t, k, "S"]], act(T.sg[:, sl(k)], ps(bank("S", k, 0, t)), F.Sign, bias=-TINY))

    def counts(t, k):
        st[t, k, "cnt"] = run("V", [st[t, k, "p", 1], st["one"]], scan(T.cnt[:, sl(k)], T.sg[:, sl(k)], T.one[:, :], 0.0, O.add, O.add))

    def keep(t, k):
        st[t, k, "kept"] = run("V", [st[t, k, "cnt"], st["h16"]], scan(T.kept[:, sl(k)], T.h16[:, :], T.cnt[:, sl(k)], 0.0, O.add, O.min))

    def signs(t, k, i):
        a = C * t + N * k + 16
        st[t, k, "p", i] = run("V", [st[t, k, "S"], st["th%d" % i]] + [st[t, k, "p", 0] and None for _ in range(i)],
                               tt(T.pb[:, a:a + N] if i else T.sg[:, sl(k)], ps(bank("S", k, 0, t)), T.th[:, sl(i)], O.is_gt))

    def tally(t, k):
        a, i = C * t + N * k, 2 * t + k - 1
        st[t, k, "cnt"] = st[t, k, "kept"] = run("V", [st[t, k, "p", 1], st[i // 2, i % 2, "p", 1] if a else st["pb"]],
                                                 scan(T.kept[:, sl(k)], T.sg[:, sl(k)], T.pb[:, a:a + N], 0.0, O.add, O.add))

    def before(t, k):
        i = 2 * t + k
        return (T.carry[:, i:i + 1], st["carry", i]) if i else (0.0, None)

    def places(t, k):
        c, tk = before(t, k)
        st[t, k, "nw"] = run("V", [st[t, k, "kept"], tk], ts(T.nw[:, 10 * k:10 * k + N // 16], T.kept[:, N * k + 15:N * k + N:16], 1.0 if tallied else 0.5, O.mult, c, O.add))

    def carry(t, k):
        c, tk = before(t, k)
        i = 2 * t + k + 1
        st["carry", i] = run("S", [st[t, k, "cnt"], tk], act(T.carry[:, i:i + 1], (T.kept if tallied else T.cnt)[:, N * k + N - 1:N * k + N], F.Identity, bias=c, scale=1.0 if tallied else 0.5))

    def look(t, k):
        width = TAB if t else TAB0 if k else TAB1
        st[t, k, "a"] = run("S", [st[t, k, "nw"], st["kb"], st["cap"], st["more2" if t else "tab1" if k else "tab"]],
                            act(T.av[:, sl(k)], T.tab[:, 0:width].indirect(T.nw[:, 10 * k:10 * k + N // 16]), F.Identity, bias=col(8)))

    def held(t, k):
        st[t, k, "hh"] = run("V", [st[t, k, "a"], st["h8end"]], scan(T.hh[:, sl(k)], T.av[:, sl(k)], T.h8[:, :], -1024.0, O.max, O.add))

    def offs(t, k):
        st[t, k, "off"] = run("V", [st[t, k, "hh"], st["ko"]], ts(T.off[:, sl(k, N // 8)], T.hh[:, N * k + 7:N * k + N:8], 2.0, O.mult, col(5), O.add))

    def unpack(t, k, b):
        st[t, k, "D", b] = mm(bank("U", k, b), NB[k], [st["E%d" % b], st[t, k, "q"], freed(t, "U", k, b)], T.eq[:, sl(b, 128)], T.es[:, sl(b, 128)], QT[t][:, cs(k)], ST[t][:, cs(k)])

    def half(c, lo, hi, i=0, step=1):
        return T.win[:, 2 * (W * c + lo) + i:2 * (W * c + hi):step]

    def lay(t, k, b, q="S"):
        old = [st[t - 1, j, "z", b] for j in range(max(k - 1, 0), min(k, 1) + 1)] if t else []
        st[t, k, "T", b] = run(q, [st[t, k, "D", b]] + old, (act if q == "S" else cp)(half(b % 2, N * k, N * k + NB[k], b // 2, 2), ps(bank("U", k, b), NB[k])))

    def twin(t, k, c, q="S"):
        out, src = T.own[:, sl(2 * k + c, 2 * N)], half(c, N * k, N * k + N)
        call = cp(out, src) if q == "V" else act(out, src) if q == "S" else lambda: g.affine_select(out, src, [[0, 2 * N]], O.is_ge, 0.0, 0, 0)
        st[t, k, "own", c] = run(q, [st[t, k, "T", c], st[t, k, "T", c + 2]], call)

    def far(t, k, c):
        return half(c, N * k, N * k + N + H).indirect(T.off[:, sl(k, N // 8)]), [st[t, k, "off"]] + [st[t, j, "T", b] for j in (k, k + 1) for b in (c, c + 2)]

    def zs(k, b=0, step=1):
        return T.zt[:, 4 * N * k + b:4 * N * k + 4 * N:step]

    def blend(t, k, c):
        f, deps = far(t, k, c)
        st[t, k, "z", c] = st[t, k, "z", c + 2] = run("V", deps + [st[t, k, "own", c]], tt(zs(k, c, 2), f, T.own[:, sl(2 * k + c, 2 * N)], O.add))

    def gather(t, k, c):
        f, deps = far(t, k, c)
        st[t, k, "F", c] = run("S", deps, act(T.own[:, sl(2 * k + c, 2 * N)], f))

    def add(t, k, b):
        o = 2 * N * (2 * k + b % 2)
        st[t, k, "z", b] = run("V", [st[t, k, "F", b % 2]], tt(zs(k, b, 4), ps(bank("U", k, b)), T.own[:, o + b // 2:o + 2 * N:2], O.add))

    def qz(t, k):
        st[t, k, "qz"] = run("V", [st[t, k, "z", b] for b in range(4)], quant(T.zq[:, sl(k)], T.zs[:, sl(k)], zs(k)))

    def layer(t, k, b):
        st[t, k, "r", b] = mm(bank("L", k, b), N, [("dW", 32), st[t, k, "qz"], freed(t, "L", k, b)], T.wq[:, sl(b, 128)], T.wsc[:, sl(b, 128)], T.zq[:, sl(k)], T.zs[:, sl(k)])

    def xupd(t, k, b):
        st[t, k, "x", b] = run("V", [st[t, k, "r", b], st[t, k, "q"]], tt(xs(t + 1, k, b, 4), ps(bank("L", k, b)), xs(t, k, b, 4), O.add))

    def ao(t, k):
        a = run("S", [st[t, 0, "a"], st[t, 1, "a"]], act(T.aof[:, :], T.av[:, :], F.Identity, bias=-float(LIFT)))
        need("Y", [a])
        g.sync.dma_start(T.ao[:, :], T.aof[0:128:16, :]).then_inc(T.sem.outA, 16)

    def codes(t, k):
        need("Y", [st[R, j, "q"] for j in range(k + 1)])
        g.sync.dma_start(T.oc[:, sl(k, 4 * N)], QT[R][:, sl(k)].bitcast(dt.uint8)).then_inc(T.sem.outA, 16)
        if k:
            for i in range(4):
                g.sync.dma_start(T.osc[4 * i:4 * i + 4, :], ST[R][32 * i:32 * i + 4, 0:C]).then_inc(T.sem.outA, 16)

    def result(t, k):
        y = mm(bank("L", k, 0), N, [st["vq"], st[R, k, "q"]], T.vq[:, :], T.vs[:, :], QT[R][:, sl(k)], ST[R][:, sl(k)])
        y = run("S", [y], act(T.ysb[:, sl(k)], ps(bank("L", k, 0))))
        st["y", k] = y

    def store(t, k):
        need("YS"[k], [st["y", k]])
        eng["YS"[k]].dma_start(T.y[:, sl(k)], T.ysb[:, sl(k)]).then_inc(T.sem.outB, 16)

    STEP = {"qx": qx, "send": send, "score": score, "sign": sign, "counts": counts, "keep": keep, "signs": signs, "tally": tally, "places": places, "carry": carry,
            "look": look, "held": held, "offs": offs, "unpack": unpack, "lay": lay, "vlay": lambda t, k, b: lay(t, k, b, "V"), "blend": blend, "gather": gather,
            "add": add, "twin": twin, "vtwin": lambda t, k, c: twin(t, k, c, "V"), "gtwin": lambda t, k, c: twin(t, k, c, "G"),
            "qz": qz, "layer": layer, "xupd": xupd, "ao": ao, "last": qx, "codes": codes, "result": result, "store": store}
    for t, step in OPT.get("ALL") or ORDER:
        cur[0] = (t, step)
        if step in ONCE:
            q, deps, call = ONCE[step]
            st[step] = run(q, [st[d] for d in deps], call)
        else:
            name, arg = step.split()
            STEP[name](t - arg[0].islower(), "ABC".index(arg[0].upper()), *[int(c) for c in arg[1:]])
    for q in ("V", "S", "T", "G"):
        need("Y", [(q, count[q])])
    g.sync.wait_ge(T.sem.outA, 16 * 7)
    g.scalar.wait_ge(T.sem.outB, 32)
    g.wait_ge(T.sem.sent, 2 * (R - 1) * lanes)
